import numpy as np
import ml_dtypes


def mxq(x, axis, fmt="e4m3"):
    dtype, down = {"e4m3": (ml_dtypes.float8_e4m3fn, 7), "e5m2": (ml_dtypes.float8_e5m2, 14)}[fmt]
    v = np.moveaxis(np.asarray(x, np.float32).astype(ml_dtypes.bfloat16).astype(np.float64), axis, -1)
    blocks = v.reshape(v.shape[:-1] + (-1, 32))
    amax = np.abs(blocks).max(-1, keepdims=True)
    byte = np.maximum(np.where(amax > 0, np.frexp(amax)[1] - 1 + 127, 0) - down, 1)
    scale = np.exp2(byte - 127.0)
    codes = (blocks / scale).astype(np.float32).astype(dtype).astype(np.float64)
    return np.moveaxis((codes * scale).reshape(v.shape), -1, axis)


WIDE = False


def mx_kscale(k):
    if not WIDE:
        return np.ones(k)
    levels = np.array([10, -10, 5, -5, 0])
    if k % 512:
        return np.exp2(np.random.permutation(np.resize(levels, k // 32))).repeat(32)
    a = np.empty((k // 512, 16))
    for p in range(k // 512):
        a[p, :8] = np.random.permutation(np.resize(levels, 8))
        for g in range(8):
            far = levels[np.abs(levels - a[p, g]) >= 10]
            a[p, g + 8] = far[np.random.randint(len(far))]
    return np.exp2(a.ravel()).repeat(32)


def f64(x):
    return np.asarray(x).astype(np.float64)


def striped(idx):
    return np.tile(idx.reshape(-1, 16).T, (8, 1)).astype(np.uint16)


def unstriped(offs):
    return offs[:16].T.reshape(-1).astype(np.int64)


E2M1 = np.array([0.0, 0.5, 1.0, 1.5, 2.0, 3.0, 4.0, 6.0, -0.0, -0.5, -1.0, -1.5, -2.0, -3.0, -4.0, -6.0])


def pack_weight(w, fmt):
    k, n = w.shape
    w = f64(np.asarray(w, np.float32).astype(ml_dtypes.bfloat16)).reshape(k // 32, 32, n)
    amax = np.abs(w).max(1)
    if fmt == "e4m3":
        byte = np.frexp(amax)[1] - 1 + 127 - 7
    else:
        mant, ex = np.frexp(amax / 6.0)
        byte = np.where(mant > 0.5, ex, ex - 1) + 127
    byte = np.clip(np.where(amax > 0, byte, 1), 1, 254)
    scaled = (w * np.exp2(127.0 - byte)[:, None, :]).reshape(k, n).astype(np.float32)
    by_word = np.ascontiguousarray(scaled.reshape(k // 512, 128, 4, n).transpose(0, 1, 3, 2))
    if fmt == "e4m3":
        words = by_word.astype(ml_dtypes.float8_e4m3fn).view(np.uint8)
    else:
        c = by_word.astype(ml_dtypes.float4_e2m1fn).view(np.uint8) & 0xF
        words = (c[..., 0::2] | (c[..., 1::2] << 4)).reshape(k // 512, 128, 2 * n)
    return np.ascontiguousarray(words), np.ascontiguousarray(byte.astype(np.uint8).reshape(k // 512, 16, n))


def unpack_weight(words, scales, fmt):
    g, _, n = scales.shape
    words = np.ascontiguousarray(words).reshape(g, 128, n, -1)
    if fmt == "e4m3":
        vals = words.view(ml_dtypes.float8_e4m3fn).astype(np.float64)
    else:
        nib = np.empty((g, 128, n, 4), np.uint8)
        nib[..., 0::2] = words & 0xF
        nib[..., 1::2] = words >> 4
        vals = E2M1[nib]
    vals = vals * np.repeat(np.exp2(scales.astype(np.float64) - 127.0), 8, axis=1)[..., None]
    return vals.transpose(0, 1, 3, 2).reshape(g * 512, n)


def gelu(v):
    return 0.5 * v * (1.0 + np.tanh(np.sqrt(2.0 / np.pi) * (v + 0.044715 * v**3)))


K, H, N, T, S, T2, P = 512, 1024, 384, 4096, 1024, 2048, 1024

def setup_inputs():
    n = np.random.standard_normal
    s = mx_kscale(K)[:, None]
    u = mx_kscale(H)[:, None]
    tab_words, tab_scales = pack_weight(n((K, T)) * s, "e4m3")
    w2_words, w2_scales = pack_weight(n((K, H)) / np.sqrt(K) / s * u.T, "e2m1")
    return {
        "tab_words": tab_words, "tab_scales": tab_scales,
        "offs": striped(np.random.permutation(T)[:S]),
        "w1": (n((K, H)) / np.sqrt(K) / s * u.T).astype(np.float32),
        "w2_words": w2_words, "w2_scales": w2_scales,
        "offs2": striped(np.random.permutation(T2)[:S]),
        "wgs": np.exp(0.3 * n((128, S))).astype(np.float32),
        "ref": (0.8 * n((H, T2)) * u).astype(np.float32),
        "w3": (n((H, N)) / np.sqrt(H) / u).astype(np.float32),
        "offs3": striped(np.random.permutation(T2)[:P]),
        "sens": np.exp(0.3 * n((N, P))).astype(np.float32),
        "offs4": striped(np.random.permutation(T2)[:P]),
        "wgo": np.exp(0.3 * n((128, P))).astype(np.float32),
    }

def reference(tab_words, tab_scales, offs, w1, w2_words, w2_scales, offs2, wgs, ref, w3, offs3, sens, offs4, wgo):
    v = unpack_weight(tab_words, tab_scales, "e4m3")[:, unstriped(offs)]
    a = mxq(f64(w1), 0, "e4m3").T @ v
    b = unpack_weight(w2_words, w2_scales, "e2m1").T @ v
    h = np.sqrt(np.square(a) + np.square(b))
    page = np.zeros((H, T2))
    page[:, unstriped(offs2)] = np.tile(f64(wgs), (H // 128, 1)) * h
    z = page - f64(ref)
    y = mxq(f64(w3), 0, "e4m3").T @ mxq(z, 0, "e4m3")
    x = y[:, unstriped(offs3)] * f64(sens)
    out = np.zeros((N, T2))
    out[:, unstriped(offs4)] = np.tile(f64(wgo), (N // 128, 1)) * x
    return out

@@ -1,0 +1,280 @@
+from contextlib import ExitStack
+
+import concourse.mybir as mybir
+from concourse.masks import make_identity
+
+K, H, N, T, S, T2, M = 512, 1024, 384, 4096, 1024, 2048, 1024
+P = 128
+BANK = 512
+FLOPS = 2 * K * H * S * 2 + 2 * H * N * T2
+
+F32 = mybir.dt.float32
+BF16 = mybir.dt.bfloat16
+I32 = mybir.dt.int32
+U32 = mybir.dt.uint32
+U16 = mybir.dt.uint16
+U8 = mybir.dt.uint8
+FP8X4 = mybir.dt.float8_e4m3fn_x4
+FP4X4 = mybir.dt.float4_e2m1fn_x4
+ACT = mybir.ActivationFunctionType
+MULT = mybir.AluOpType.mult
+
+W1_CHUNKS = ((0, 128), (128, 256), (256, 512), (512, 1024))
+ROW_TILES = H // P
+GROUPS = T2 // BANK
+
+
+def tile_list_plate_proofing_kernel(
+    tc, tab_words, tab_scales, offs, w1, w2_words, w2_scales, offs2, wgs, ref, w3, offs3, sens, offs4, wgo, out
+):
+    nc = tc.nc
+    with ExitStack() as ctx:
+        held = ctx.enter_context(tc.tile_pool(name="held", bufs=1))
+        psum = ctx.enter_context(tc.psum_pool(name="psum", bufs=1))
+
+        def sb(shape, dtype, name, tag=None, bufs=1):
+            return held.tile(shape, dtype, name=name, tag=tag or name, bufs=bufs, align_bytes=64)
+
+        def bank(tag, name, bufs=2):
+            return psum.tile([P, BANK], F32, name=name, tag=tag, bufs=bufs)
+
+        def load_list(src, name):
+            tile = held.tile([P, S // 16], U16, name=name)
+            nc.sync.dma_start(tile[:], src)
+            return tile
+
+        def load_scale_rows(plane, rows):
+            for q in range(4):
+                nc.sync.dma_start(plane[32 * q : 32 * q + 4, :].bitcast(I32), rows[4 * q : 4 * q + 4, :].bitcast(I32))
+
+        def interleave(copy, grouped, raw):
+            copy(
+                out=grouped.rearrange("p (c i) t -> p c t i", i=4),
+                in_=raw.rearrange("p t (c i) -> p c t i", i=4),
+            )
+
+        tab_s = sb([P, T], U8, "tab_s")
+        w2_s = sb([P, H], U8, "w2_s")
+        nc.vector.memset(tab_s[:].bitcast(I32), 0)
+        nc.vector.memset(w2_s[:].bitcast(I32), 0)
+        list1 = load_list(offs, "list1")
+        load_scale_rows(tab_s, tab_scales[0])
+        tab_w = sb([P, T], U32, "tab_w", tag="wide")
+        nc.sync.dma_start(tab_w[:].bitcast(I32), tab_words[0].rearrange("p t i -> p (t i)").bitcast(I32))
+
+        w1_raw = {}
+
+        def load_w1(c):
+            c0, c1 = W1_CHUNKS[c]
+            w1_raw[c] = sb([P, 4, c1 - c0], F32, f"w1_raw{c}")
+            nc.sync.dma_start(w1_raw[c][:], w1[:, c0:c1].rearrange("(p j) c -> p j c", j=4))
+
+        load_w1(0)
+        w2_w = sb([P, 2 * H], U8, "w2_w")
+        nc.sync.dma_start(w2_w[:].bitcast(I32), w2_words[0].bitcast(I32))
+        load_scale_rows(w2_s, w2_scales[0])
+        wgs_raw = sb([P, S], F32, "wgs_raw", tag="place_w")
+        load_w1(1)
+        nc.sync.dma_start(wgs_raw[:], wgs)
+        list2 = load_list(offs2, "list2")
+        load_w1(2)
+        load_w1(3)
+
+        ident = sb([P, P], F32, "ident")
+        make_identity(nc, ident[:])
+
+        pages = [sb([P, T2], F32, f"page{i}") for i in range(3)]
+        for page in pages:
+            nc.gpsimd.memset(page[:], 0.0)
+
+        v_w, v_s = [], []
+
+        def gather_table(hh):
+            cols = slice(32 * hh, 32 * hh + 32)
+            s_t = sb([P, BANK], U8, f"v_s{hh}")
+            w_t = sb([P, BANK], U32, f"v_w{hh}")
+            nc.vector.tensor_copy(s_t[:], tab_s[:].indirect(list1[:, cols]))
+            nc.vector.tensor_copy(w_t[:], tab_w[:].indirect(list1[:, cols]))
+            v_s.append(s_t)
+            v_w.append(w_t)
+
+        w1_q = {}
+
+        def quantise_w1(c):
+            c0, c1 = W1_CHUNKS[c]
+            width = c1 - c0
+            grouped = sb([P, width, 4], BF16, f"w1_bf{c}", tag="w1_bf", bufs=2)
+            interleave(nc.scalar.copy, grouped[:], w1_raw[c][:])
+            codes = sb([P, width], U32, f"w1_c{c}")
+            plane = sb([P, width], U8, f"w1_s{c}")
+            nc.vector.quantize_mx(codes[:].bitcast(FP8X4), plane[:], grouped[:].rearrange("p c t -> p (c t)"))
+            for i in range(c0 // P, c1 // P):
+                w1_q[i] = (codes[:, i * P - c0 : (i + 1) * P - c0], plane[:, i * P - c0 : (i + 1) * P - c0])
+
+        gather_table(0)
+        quantise_w1(0)
+        gather_table(1)
+        quantise_w1(1)
+        wgs_neg = sb([P, S], F32, "wgs_neg")
+        nc.scalar.activation(wgs_neg[:], wgs_raw[:], ACT.Copy, scale=-1.0)
+
+        refs = {}
+
+        def load_ref(i):
+            refs[i] = sb([P, T2], F32, f"ref{i}", tag="rows", bufs=3)
+            nc.sync.dma_start(refs[i][:], ref[i * P : (i + 1) * P, :])
+
+        mags = {}
+
+        def magnitudes(i):
+            mags[i] = sb([P, S], F32, f"mag{i}", tag="mag", bufs=3)
+            for hh in range(2):
+                sq = []
+                for which in range(2):
+                    acc = bank("resp", f"resp{i}_{hh}_{which}", bufs=4)
+                    for jj in range(4):
+                        cols = slice(jj * P, (jj + 1) * P)
+                        if which == 0:
+                            rhs, rhs_scale = w1_q[i][0].bitcast(FP8X4), w1_q[i][1]
+                        else:
+                            rhs = w2_w[:, 2 * P * i : 2 * P * (i + 1)].bitcast(FP4X4)
+                            rhs_scale = w2_s[:, P * i : P * (i + 1)]
+                        nc.tensor.matmul_mx(
+                            out=acc[:, cols], lhsT=v_w[hh][:, cols].bitcast(FP8X4), lhsT_scale=v_s[hh][:, cols],
+                            rhs=rhs, rhs_scale=rhs_scale, start=True, stop=True,
+                        )
+                    squared = sb([P, BANK], F32, f"sq{i}_{hh}_{which}", tag="sq", bufs=4)
+                    nc.scalar.activation(squared[:], acc[:], ACT.Square)
+                    sq.append(squared)
+                total = bank("turn", f"sum{i}_{hh}")
+                for which in range(2):
+                    for jj in range(4):
+                        cols = slice(jj * P, (jj + 1) * P)
+                        nc.tensor.matmul(
+                            total[:, cols], sq[which][:, cols], ident[:], is_transpose=True,
+                            start=(which == 0 and jj == 0), stop=(which == 1 and jj == 3),
+                        )
+                nc.scalar.activation(mags[i][:, hh * BANK : (hh + 1) * BANK], total[:], ACT.Sqrt)
+
+        def place(i):
+            page = pages[i % len(pages)]
+            parts = 2 if i == 0 else 1
+            for a in range(parts):
+                w = S // parts
+                cols = slice(a * w, (a + 1) * w)
+                nc.vector.tensor_tensor(
+                    page[:].indirect(list2[:, a * w // 16 : (a + 1) * w // 16]), mags[i][:, cols], wgs_neg[:, cols], MULT
+                )
+
+        z_t = {}
+
+        def deviation(i):
+            b, quarter = divmod(i, 4)
+            page = pages[i % len(pages)]
+            for g in range(GROUPS):
+                if quarter == 0:
+                    z_t[b, g] = sb([P, 4, 2, P, 2], BF16, f"z_t{b}_{g}")
+                acc = bank("turn", f"dev{i}_{g}")
+                for which, src in enumerate((refs[i], page)):
+                    for tb in range(4):
+                        nc.tensor.matmul(
+                            acc[:, tb * P : (tb + 1) * P], src[:, g * BANK + tb * P : g * BANK + (tb + 1) * P], ident[:],
+                            is_transpose=True, start=(which == 0 and tb == 0), stop=(which == 1 and tb == 3),
+                        )
+                nc.scalar.copy(
+                    out=z_t[b, g][:, :, :, 32 * quarter : 32 * quarter + 32, :],
+                    in_=acc[:].rearrange("s (tb p u e) -> s tb u p e", tb=4, u=2, e=2),
+                )
+
+        z_q = {}
+
+        def turn_back(b, g, second_copy):
+            words = z_t[b, g][:].rearrange("s tb u p e -> s (tb u p e)").bitcast(F32)
+            grouped = sb([P, BANK * 4], BF16, f"z_bf{b}_{g}", tag="z_bf", bufs=2)
+            grouped_words = grouped[:].bitcast(F32)
+            for half in range(2):
+                acc = bank("back", f"back{b}_{g}_{half}")
+                for k in range(4):
+                    src = words[:, (4 * half + k) * P : (4 * half + k + 1) * P]
+                    nc.tensor.transpose(acc[:, k * P : (k + 1) * P], src, ident[:])
+                copy = second_copy if half else nc.scalar.copy
+                copy(
+                    out=grouped_words[:, half * BANK : (half + 1) * BANK].rearrange("p (tb t u) -> p tb t u", tb=2, u=2),
+                    in_=acc[:].rearrange("p (tb u t) -> p tb t u", tb=2, u=2),
+                )
+            codes = sb([P, BANK], U32, f"z_c{b}_{g}")
+            plane = sb([P, BANK], U8, f"z_s{b}_{g}")
+            nc.vector.quantize_mx(codes[:].bitcast(FP8X4), plane[:], grouped[:])
+            z_q[b, g] = (codes, plane)
+
+        w3_bf = sb([P, 2 * N, 4], BF16, "w3_bf")
+        w3_c = sb([P, 2 * N], U32, "w3_c")
+        w3_s = sb([P, 2 * N], U8, "w3_s")
+
+        def prepare_w3():
+            for b in range(2):
+                raw = sb([P, 4, N], F32, f"w3_raw{b}", tag="w1_raw3" if b == 0 else None)
+                nc.sync.dma_start(raw[:], w3[b * 512 : (b + 1) * 512, :].rearrange("(p j) n -> p j n", j=4))
+                interleave(nc.scalar.copy, w3_bf[:, b * N : (b + 1) * N, :], raw[:])
+            flat = w3_bf[:].rearrange("p c t -> p (c t)")
+            for c0, c1 in ((0, 512), (512, 768)):
+                nc.vector.quantize_mx(w3_c[:, c0:c1].bitcast(FP8X4), w3_s[:, c0:c1], flat[:, 4 * c0 : 4 * c1])
+
+        magnitudes(0)
+        load_ref(0)
+        place(0)
+        magnitudes(1)
+        quantise_w1(2)
+        load_ref(1)
+        magnitudes(2)
+        quantise_w1(3)
+        for i in range(1, ROW_TILES):
+            place(i)
+            deviation(i - 1)
+            if i + 1 < ROW_TILES:
+                load_ref(i + 1)
+            if i + 2 < ROW_TILES:
+                magnitudes(i + 2)
+            else:
+                turn_back(0, 2 * (i - 6), nc.scalar.copy)
+                turn_back(0, 2 * (i - 6) + 1, nc.scalar.copy)
+            if i == 6:
+                prepare_w3()
+
+        list3 = load_list(offs3, "list3")
+        list4 = load_list(offs4, "list4")
+        sens_t = sb([P, N // P, M], F32, "sens_t", tag="wide")
+        nc.sync.dma_start(sens_t[:], sens.rearrange("(n p) m -> p n m", p=P))
+        wgo_t = sb([P, M], F32, "wgo_t", tag="place_w")
+        nc.sync.dma_start(wgo_t[:], wgo)
+        outs = [sb([P, T2], F32, f"out_page{i}") for i in range(2)]
+        for page in outs:
+            nc.gpsimd.memset(page[:], 0.0)
+
+        deviation(ROW_TILES - 1)
+
+        scores = [sb([P, T2], F32, f"score{n}", tag="rows", bufs=3) for n in range(N // P)]
+
+        def score(n, g):
+            acc = bank("resp", f"score_acc{n}_{g}", bufs=4)
+            for b in range(2):
+                cols = slice(b * N + n * P, b * N + (n + 1) * P)
+                nc.tensor.matmul_mx(
+                    out=acc[:], lhsT=w3_c[:, cols].bitcast(FP8X4), lhsT_scale=w3_s[:, cols],
+                    rhs=z_q[b, g][0][:].bitcast(FP8X4), rhs_scale=z_q[b, g][1][:], start=(b == 0), stop=(b == 1),
+                )
+            nc.scalar.activation(scores[n][:, g * BANK : (g + 1) * BANK], acc[:], ACT.Copy, scale=-1.0)
+
+        for g in range(GROUPS):
+            turn_back(1, g, nc.vector.tensor_copy)
+            score(0, g)
+        for n in range(1, N // P):
+            for g in range(GROUPS):
+                score(n, g)
+
+        for n in range(N // P):
+            picked = sb([P, M], F32, f"picked{n}", tag="mag", bufs=3)
+            nc.vector.tensor_tensor(picked[:], scores[n][:].indirect(list3[:]), sens_t[:, n, :], MULT)
+            page = outs[n % 2]
+            nc.vector.tensor_tensor(page[:].indirect(list4[:]), picked[:], wgo_t[:], MULT)
+            nc.sync.dma_start(out[n * P : (n + 1) * P, :], page[:])

@@ -19,7 +19,7 @@ FP4X4 = mybir.dt.float4_e2m1fn_x4
 ACT = mybir.ActivationFunctionType
 MULT = mybir.AluOpType.mult
 
-W1_CHUNKS = ((0, 128), (128, 256), (256, 512), (512, 1024))
+W1_CHUNKS = ((0, 128), (128, 256), (256, 512), (512, 768), (768, 1024))
 ROW_TILES = H // P
 GROUPS = T2 // BANK
 
@@ -30,22 +30,36 @@ def tile_list_plate_proofing_kernel(
     nc = tc.nc
     with ExitStack() as ctx:
         held = ctx.enter_context(tc.tile_pool(name="held", bufs=1))
+        shared = ctx.enter_context(tc.tile_pool(name="shared", bufs=1))
         psum = ctx.enter_context(tc.psum_pool(name="psum", bufs=1))
 
         def sb(shape, dtype, name, tag=None, bufs=1):
             return held.tile(shape, dtype, name=name, tag=tag or name, bufs=bufs, align_bytes=64)
 
-        def bank(tag, name, bufs=2):
-            return psum.tile([P, BANK], F32, name=name, tag=tag, bufs=bufs)
+        def placed(shape, dtype, name, offset, tag=None):
+            return shared.tile(shape, dtype, name=name, tag=tag or name, offset=offset, align_bytes=64)
+
+        def row_tile(k, name):
+            if k % 3 == 0:
+                return sb([P, T2], F32, name, tag="rows0")
+            return placed([P, T2], F32, name, (20992, 12800)[k % 3 - 1], tag=f"rows{k % 3}")
+
+        mx_banks = [psum.tile([P, BANK], F32, name=f"mx_bank{k}") for k in range(4)]
+        turn_banks = [psum.tile([P, BANK], F32, name=f"turn_bank{k}") for k in range(4)]
+        turn_uses = []
+
+        def turn_bank():
+            turn_uses.append(None)
+            return turn_banks[(len(turn_uses) - 1) % len(turn_banks)]
 
         def load_list(src, name):
             tile = held.tile([P, S // 16], U16, name=name)
             nc.sync.dma_start(tile[:], src)
             return tile
 
-        def load_scale_rows(plane, rows):
+        def load_scale_rows(queue, plane, rows):
             for q in range(4):
-                nc.sync.dma_start(plane[32 * q : 32 * q + 4, :].bitcast(I32), rows[4 * q : 4 * q + 4, :].bitcast(I32))
+                queue.dma_start(plane[32 * q : 32 * q + 4, :].bitcast(I32), rows[4 * q : 4 * q + 4, :].bitcast(I32))
 
         def interleave(copy, grouped, raw):
             copy(
@@ -53,47 +67,57 @@ def tile_list_plate_proofing_kernel(
                 in_=raw.rearrange("p t (c i) -> p c t i", i=4),
             )
 
-        tab_s = sb([P, T], U8, "tab_s")
-        w2_s = sb([P, H], U8, "w2_s")
-        nc.vector.memset(tab_s[:].bitcast(I32), 0)
-        nc.vector.memset(w2_s[:].bitcast(I32), 0)
-        list1 = load_list(offs, "list1")
-        load_scale_rows(tab_s, tab_scales[0])
-        tab_w = sb([P, T], U32, "tab_w", tag="wide")
-        nc.sync.dma_start(tab_w[:].bitcast(I32), tab_words[0].rearrange("p t i -> p (t i)").bitcast(I32))
-
         w1_raw = {}
 
         def load_w1(c):
             c0, c1 = W1_CHUNKS[c]
-            w1_raw[c] = sb([P, 4, c1 - c0], F32, f"w1_raw{c}")
+            w1_raw[c] = sb([P, 4, c1 - c0], F32, f"w1_raw{c}", tag="v_w1" if c == 2 else None)
             nc.sync.dma_start(w1_raw[c][:], w1[:, c0:c1].rearrange("(p j) c -> p j c", j=4))
 
+        tab_s = placed([P, T], U8, "tab_s", 20992)
+        w2_s = sb([P, H], U8, "w2_s")
+        nc.vector.memset(tab_s[:].bitcast(I32), 0)
+        nc.gpsimd.memset(w2_s[:].bitcast(I32), 0)
+        load_scale_rows(nc.gpsimd, w2_s, w2_scales[0])
+        warm = sb([P, 2], F32, "warm")
+        nc.vector.memset(warm[:, 0:1], 1.0)
+        nc.scalar.activation(warm[:, 1:2], warm[:, 0:1], ACT.Sqrt)
+        list1 = load_list(offs, "list1")
+        list2 = load_list(offs2, "list2")
+        list3 = load_list(offs3, "list3")
+        list4 = load_list(offs4, "list4")
         load_w1(0)
+        tab_w = placed([P, T], U32, "tab_w", 4096)
+        nc.sync.dma_start(tab_w[:].bitcast(I32), tab_words[0].rearrange("p t i -> p (t i)").bitcast(I32))
         w2_w = sb([P, 2 * H], U8, "w2_w")
         nc.sync.dma_start(w2_w[:].bitcast(I32), w2_words[0].bitcast(I32))
-        load_scale_rows(w2_s, w2_scales[0])
-        wgs_raw = sb([P, S], F32, "wgs_raw", tag="place_w")
         load_w1(1)
-        nc.sync.dma_start(wgs_raw[:], wgs)
-        list2 = load_list(offs2, "list2")
+        load_scale_rows(nc.scalar, tab_s, tab_scales[0])
         load_w1(2)
+        wgs_raw = placed([P, S], F32, "wgs_raw", 25088)
+        nc.sync.dma_start(wgs_raw[:], wgs)
         load_w1(3)
+        load_w1(4)
 
         ident = sb([P, P], F32, "ident")
         make_identity(nc, ident[:])
+        pages, outs = [], []
 
-        pages = [sb([P, T2], F32, f"page{i}") for i in range(3)]
-        for page in pages:
+        def zeroed(name, tag=None):
+            page = sb([P, T2], F32, name, tag=tag)
             nc.gpsimd.memset(page[:], 0.0)
+            return page
+
+        pages.append(zeroed("page0"))
+        pages.append(zeroed("page1"))
 
         v_w, v_s = [], []
 
         def gather_table(hh):
             cols = slice(32 * hh, 32 * hh + 32)
             s_t = sb([P, BANK], U8, f"v_s{hh}")
-            w_t = sb([P, BANK], U32, f"v_w{hh}")
             nc.vector.tensor_copy(s_t[:], tab_s[:].indirect(list1[:, cols]))
+            w_t = sb([P, BANK], U32, f"v_w{hh}")
             nc.vector.tensor_copy(w_t[:], tab_w[:].indirect(list1[:, cols]))
             v_s.append(s_t)
             v_w.append(w_t)
@@ -103,97 +127,116 @@ def tile_list_plate_proofing_kernel(
         def quantise_w1(c):
             c0, c1 = W1_CHUNKS[c]
             width = c1 - c0
-            grouped = sb([P, width, 4], BF16, f"w1_bf{c}", tag="w1_bf", bufs=2)
+            if c == 1:
+                grouped = placed([P, width, 4], BF16, "w1_bf1", 0)
+            else:
+                grouped = sb([P, width, 4], BF16, f"w1_bf{c}", tag=f"early_square{c - 2}" if c >= 3 else None)
             interleave(nc.scalar.copy, grouped[:], w1_raw[c][:])
-            codes = sb([P, width], U32, f"w1_c{c}")
+            if c == 0:
+                codes = placed([P, width], U32, "w1_c0", 20480)
+            else:
+                codes = sb([P, width], U32, f"w1_c{c}")
             plane = sb([P, width], U8, f"w1_s{c}")
             nc.vector.quantize_mx(codes[:].bitcast(FP8X4), plane[:], grouped[:].rearrange("p c t -> p (c t)"))
             for i in range(c0 // P, c1 // P):
                 w1_q[i] = (codes[:, i * P - c0 : (i + 1) * P - c0], plane[:, i * P - c0 : (i + 1) * P - c0])
 
-        gather_table(0)
         quantise_w1(0)
-        gather_table(1)
+        gather_table(0)
         quantise_w1(1)
-        wgs_neg = sb([P, S], F32, "wgs_neg")
-        nc.scalar.activation(wgs_neg[:], wgs_raw[:], ACT.Copy, scale=-1.0)
+        quantise_w1(2)
+        gather_table(1)
+        wgs_neg = placed([P, S], F32, "wgs_neg", 0)
+        nc.vector.tensor_scalar_mul(wgs_neg[:], wgs_raw[:], -1.0)
 
         refs = {}
 
         def load_ref(i):
-            refs[i] = sb([P, T2], F32, f"ref{i}", tag="rows", bufs=3)
+            refs[i] = row_tile(i, f"ref{i}")
             nc.sync.dma_start(refs[i][:], ref[i * P : (i + 1) * P, :])
 
-        mags = {}
+        mags = [sb([P, S], F32, f"mag{k}") for k in range(3)]
+        first_mags = [sb([P, BANK], F32, f"first_mag{hh}") for hh in range(2)]
+        squares = [sb([P, BANK], F32, f"square{k}") for k in range(4)]
+
+        early = {i: sb([P, BANK], F32, f"early_square{i}") for i in (1, 2)}
+
+        def square_tile(i, k):
+            return early[i] if k == 3 and i in early else squares[k]
+
+        def respond(i, k):
+            hh, which = divmod(k, 2)
+            acc = mx_banks[k]
+            for jj in range(4):
+                cols = slice(jj * P, (jj + 1) * P)
+                if which == 0:
+                    rhs, rhs_scale = w1_q[i][0].bitcast(FP8X4), w1_q[i][1]
+                else:
+                    rhs = w2_w[:, 2 * P * i : 2 * P * (i + 1)].bitcast(FP4X4)
+                    rhs_scale = w2_s[:, P * i : P * (i + 1)]
+                nc.tensor.matmul_mx(
+                    out=acc[:, cols], lhsT=v_w[hh][:, cols].bitcast(FP8X4), lhsT_scale=v_s[hh][:, cols],
+                    rhs=rhs, rhs_scale=rhs_scale, start=True, stop=True,
+                )
+            nc.scalar.activation(square_tile(i, k)[:], acc[:], ACT.Square)
+
+        def magnitude(i, hh):
+            total = turn_bank()
+            for which in range(2):
+                for jj in range(4):
+                    cols = slice(jj * P, (jj + 1) * P)
+                    nc.tensor.matmul(
+                        total[:, cols], square_tile(i, 2 * hh + which)[:, cols], ident[:], is_transpose=True,
+                        start=(which == 0 and jj == 0), stop=(which == 1 and jj == 3),
+                    )
+            target = mags[i % 3][:, hh * BANK : (hh + 1) * BANK] if i else first_mags[hh][:]
+            nc.scalar.activation(target, total[:], ACT.Sqrt)
 
         def magnitudes(i):
-            mags[i] = sb([P, S], F32, f"mag{i}", tag="mag", bufs=3)
             for hh in range(2):
-                sq = []
-                for which in range(2):
-                    acc = bank("resp", f"resp{i}_{hh}_{which}", bufs=4)
-                    for jj in range(4):
-                        cols = slice(jj * P, (jj + 1) * P)
-                        if which == 0:
-                            rhs, rhs_scale = w1_q[i][0].bitcast(FP8X4), w1_q[i][1]
-                        else:
-                            rhs = w2_w[:, 2 * P * i : 2 * P * (i + 1)].bitcast(FP4X4)
-                            rhs_scale = w2_s[:, P * i : P * (i + 1)]
-                        nc.tensor.matmul_mx(
-                            out=acc[:, cols], lhsT=v_w[hh][:, cols].bitcast(FP8X4), lhsT_scale=v_s[hh][:, cols],
-                            rhs=rhs, rhs_scale=rhs_scale, start=True, stop=True,
-                        )
-                    squared = sb([P, BANK], F32, f"sq{i}_{hh}_{which}", tag="sq", bufs=4)
-                    nc.scalar.activation(squared[:], acc[:], ACT.Square)
-                    sq.append(squared)
-                total = bank("turn", f"sum{i}_{hh}")
-                for which in range(2):
-                    for jj in range(4):
-                        cols = slice(jj * P, (jj + 1) * P)
-                        nc.tensor.matmul(
-                            total[:, cols], sq[which][:, cols], ident[:], is_transpose=True,
-                            start=(which == 0 and jj == 0), stop=(which == 1 and jj == 3),
-                        )
-                nc.scalar.activation(mags[i][:, hh * BANK : (hh + 1) * BANK], total[:], ACT.Sqrt)
+                respond(i, 2 * hh)
+                respond(i, 2 * hh + 1)
+                magnitude(i, hh)
 
         def place(i):
-            page = pages[i % len(pages)]
-            parts = 2 if i == 0 else 1
-            for a in range(parts):
-                w = S // parts
-                cols = slice(a * w, (a + 1) * w)
-                nc.vector.tensor_tensor(
-                    page[:].indirect(list2[:, a * w // 16 : (a + 1) * w // 16]), mags[i][:, cols], wgs_neg[:, cols], MULT
-                )
+            page = pages[i % 3]
+            if i:
+                nc.vector.tensor_tensor(page[:].indirect(list2[:]), mags[i % 3][:], wgs_neg[:], MULT)
+            else:
+                for hh in range(2):
+                    nc.vector.tensor_tensor(
+                        page[:].indirect(list2[:, 32 * hh : 32 * hh + 32]), first_mags[hh][:],
+                        wgs_neg[:, hh * BANK : (hh + 1) * BANK], MULT,
+                    )
 
         z_t = {}
 
-        def deviation(i):
+        def deviation(i, g):
             b, quarter = divmod(i, 4)
-            page = pages[i % len(pages)]
-            for g in range(GROUPS):
-                if quarter == 0:
-                    z_t[b, g] = sb([P, 4, 2, P, 2], BF16, f"z_t{b}_{g}")
-                acc = bank("turn", f"dev{i}_{g}")
-                for which, src in enumerate((refs[i], page)):
-                    for tb in range(4):
-                        nc.tensor.matmul(
-                            acc[:, tb * P : (tb + 1) * P], src[:, g * BANK + tb * P : g * BANK + (tb + 1) * P], ident[:],
-                            is_transpose=True, start=(which == 0 and tb == 0), stop=(which == 1 and tb == 3),
-                        )
-                nc.scalar.copy(
-                    out=z_t[b, g][:, :, :, 32 * quarter : 32 * quarter + 32, :],
-                    in_=acc[:].rearrange("s (tb p u e) -> s tb u p e", tb=4, u=2, e=2),
-                )
+            page = pages[i % 3]
+            if quarter == 0:
+                z_t[b, g] = sb([P, 4, 2, P, 2], BF16, f"z_t{b}_{g}")
+            acc = mx_banks[g] if i >= ROW_TILES - 2 else turn_bank()
+            for which, src in enumerate((refs[i], page)):
+                for tb in range(4):
+                    nc.tensor.matmul(
+                        acc[:, tb * P : (tb + 1) * P], src[:, g * BANK + tb * P : g * BANK + (tb + 1) * P], ident[:],
+                        is_transpose=True, start=(which == 0 and tb == 0), stop=(which == 1 and tb == 3),
+                    )
+            nc.scalar.copy(
+                out=z_t[b, g][:, :, :, 32 * quarter : 32 * quarter + 32, :],
+                in_=acc[:].rearrange("s (tb p u e) -> s tb u p e", tb=4, u=2, e=2),
+            )
 
         z_q = {}
+        z_bf = [sb([P, BANK * 4], BF16, f"z_bf{k}") for k in range(4)]
 
         def turn_back(b, g, second_copy):
             words = z_t[b, g][:].rearrange("s tb u p e -> s (tb u p e)").bitcast(F32)
-            grouped = sb([P, BANK * 4], BF16, f"z_bf{b}_{g}", tag="z_bf", bufs=2)
+            grouped = z_bf[g]
             grouped_words = grouped[:].bitcast(F32)
             for half in range(2):
-                acc = bank("back", f"back{b}_{g}_{half}")
+                acc = turn_bank()
                 for k in range(4):
                     src = words[:, (4 * half + k) * P : (4 * half + k + 1) * P]
                     nc.tensor.transpose(acc[:, k * P : (k + 1) * P], src, ident[:])
@@ -202,78 +245,97 @@ def tile_list_plate_proofing_kernel(
                     out=grouped_words[:, half * BANK : (half + 1) * BANK].rearrange("p (tb t u) -> p tb t u", tb=2, u=2),
                     in_=acc[:].rearrange("p (tb u t) -> p tb t u", tb=2, u=2),
                 )
+
+        def quantise_z(b, g):
+            grouped = z_bf[g]
             codes = sb([P, BANK], U32, f"z_c{b}_{g}")
-            plane = sb([P, BANK], U8, f"z_s{b}_{g}")
+            plane = sb([P, BANK], U8, f"z_s{b}_{g}") if b else placed([P, BANK], U8, f"z_s{b}_{g}", g * BANK)
             nc.vector.quantize_mx(codes[:].bitcast(FP8X4), plane[:], grouped[:])
             z_q[b, g] = (codes, plane)
 
         w3_bf = sb([P, 2 * N, 4], BF16, "w3_bf")
         w3_c = sb([P, 2 * N], U32, "w3_c")
-        w3_s = sb([P, 2 * N], U8, "w3_s")
+        w3_s = placed([P, 2 * N], U8, "w3_s", 4 * BANK)
 
-        def prepare_w3():
-            for b in range(2):
-                raw = sb([P, 4, N], F32, f"w3_raw{b}", tag="w1_raw3" if b == 0 else None)
-                nc.sync.dma_start(raw[:], w3[b * 512 : (b + 1) * 512, :].rearrange("(p j) n -> p j n", j=4))
-                interleave(nc.scalar.copy, w3_bf[:, b * N : (b + 1) * N, :], raw[:])
+        def round_w3(b):
+            raw = sb([P, 4, N], F32, f"w3_raw{b}", tag=f"v_w{b}")
+            nc.sync.dma_start(raw[:], w3[b * 512 : (b + 1) * 512, :].rearrange("(p j) n -> p j n", j=4))
+            interleave(nc.scalar.copy, w3_bf[:, b * N : (b + 1) * N, :], raw[:])
+
+        def quantise_w3():
             flat = w3_bf[:].rearrange("p c t -> p (c t)")
             for c0, c1 in ((0, 512), (512, 768)):
                 nc.vector.quantize_mx(w3_c[:, c0:c1].bitcast(FP8X4), w3_s[:, c0:c1], flat[:, 4 * c0 : 4 * c1])
 
-        magnitudes(0)
         load_ref(0)
+        magnitudes(0)
+        pages.append(zeroed("page2", tag="w1_s0"))
         place(0)
         magnitudes(1)
-        quantise_w1(2)
+        outs.append(zeroed("out_page0", tag="w1_c1"))
+        outs.append(zeroed("out_page1", tag="w1_s1"))
+        quantise_w1(3)
         load_ref(1)
         magnitudes(2)
-        quantise_w1(3)
+        quantise_w1(4)
         for i in range(1, ROW_TILES):
             place(i)
-            deviation(i - 1)
             if i + 1 < ROW_TILES:
                 load_ref(i + 1)
-            if i + 2 < ROW_TILES:
-                magnitudes(i + 2)
-            else:
-                turn_back(0, 2 * (i - 6), nc.scalar.copy)
-                turn_back(0, 2 * (i - 6) + 1, nc.scalar.copy)
-            if i == 6:
-                prepare_w3()
-
-        list3 = load_list(offs3, "list3")
-        list4 = load_list(offs4, "list4")
-        sens_t = sb([P, N // P, M], F32, "sens_t", tag="wide")
-        nc.sync.dma_start(sens_t[:], sens.rearrange("(n p) m -> p n m", p=P))
-        wgo_t = sb([P, M], F32, "wgo_t", tag="place_w")
-        nc.sync.dma_start(wgo_t[:], wgo)
-        outs = [sb([P, T2], F32, f"out_page{i}") for i in range(2)]
-        for page in outs:
-            nc.gpsimd.memset(page[:], 0.0)
-
-        deviation(ROW_TILES - 1)
-
-        scores = [sb([P, T2], F32, f"score{n}", tag="rows", bufs=3) for n in range(N // P)]
-
-        def score(n, g):
-            acc = bank("resp", f"score_acc{n}_{g}", bufs=4)
-            for b in range(2):
-                cols = slice(b * N + n * P, b * N + (n + 1) * P)
-                nc.tensor.matmul_mx(
-                    out=acc[:], lhsT=w3_c[:, cols].bitcast(FP8X4), lhsT_scale=w3_s[:, cols],
-                    rhs=z_q[b, g][0][:].bitcast(FP8X4), rhs_scale=z_q[b, g][1][:], start=(b == 0), stop=(b == 1),
-                )
-            nc.scalar.activation(scores[n][:, g * BANK : (g + 1) * BANK], acc[:], ACT.Copy, scale=-1.0)
-
-        for g in range(GROUPS):
-            turn_back(1, g, nc.vector.tensor_copy)
-            score(0, g)
-        for n in range(1, N // P):
             for g in range(GROUPS):
-                score(n, g)
+                if i + 2 < ROW_TILES:
+                    respond(i + 2, g)
+                deviation(i - 1, g)
+            if i == 4:
+                turn_back(0, 0, nc.scalar.copy)
+            if i == 5:
+                for g in range(1, GROUPS):
+                    turn_back(0, g, nc.scalar.copy)
+            if i + 2 < ROW_TILES:
+                magnitude(i + 2, 0)
+                magnitude(i + 2, 1)
+            else:
+                round_w3(i - 6)
+        for g in range(GROUPS):
+            quantise_z(0, g)
+        quantise_w3()
+
+        sens_t = sb([P, N // P, M], F32, "sens_t", tag="w2_w")
+        nc.sync.dma_start(sens_t[:], sens.rearrange("(n p) m -> p n m", p=P))
+        wgo_t = sb([P, M], F32, "wgo_t", tag="w1_c4")
+        nc.sync.dma_start(wgo_t[:], wgo)
+
+        scores = [row_tile(ROW_TILES + n, f"score{n}") for n in range(N // P)]
+
+        def score_pass(n, g, b):
+            cols = slice(b * N + n * P, b * N + (n + 1) * P)
+            nc.tensor.matmul_mx(
+                out=mx_banks[g][:], lhsT=w3_c[:, cols].bitcast(FP8X4), lhsT_scale=w3_s[:, cols],
+                rhs=z_q[b, g][0][:].bitcast(FP8X4), rhs_scale=z_q[b, g][1][:], start=(b == 0), stop=(b == 1),
+            )
+
+        def score_out(n, g):
+            score_pass(n, g, 0)
+            score_pass(n, g, 1)
+            cols = slice(g * BANK, (g + 1) * BANK)
+            if (n, g) == (0, GROUPS - 1):
+                nc.vector.tensor_scalar_mul(scores[n][:, cols], mx_banks[g][:], -1.0)
+            else:
+                nc.scalar.activation(scores[n][:, cols], mx_banks[g][:], ACT.Copy, scale=-1.0)
+
+        last = ROW_TILES - 1
+        deviation(last, 0)
+        for g in range(GROUPS):
+            if g + 1 < GROUPS:
+                deviation(last, g + 1)
+            turn_back(1, g, nc.vector.tensor_copy if g in (1, 2) else nc.scalar.copy)
+            quantise_z(1, g)
+        for n in range(N // P):
+            for g in range(GROUPS):
+                score_out(n, g)
 
         for n in range(N // P):
-            picked = sb([P, M], F32, f"picked{n}", tag="mag", bufs=3)
+            picked = mags[n]
             nc.vector.tensor_tensor(picked[:], scores[n][:].indirect(list3[:]), sens_t[:, n, :], MULT)
             page = outs[n % 2]
             nc.vector.tensor_tensor(page[:].indirect(list4[:]), picked[:], wgo_t[:], MULT)

@@ -4,8 +4,6 @@ import concourse.mybir as mybir
 from concourse.masks import make_identity
 
 K, H, N, T, S, T2, M = 512, 1024, 384, 4096, 1024, 2048, 1024
-P = 128
-BANK = 512
 FLOPS = 2 * K * H * S * 2 + 2 * H * N * T2
 
 F32 = mybir.dt.float32
@@ -19,9 +17,25 @@ FP4X4 = mybir.dt.float4_e2m1fn_x4
 ACT = mybir.ActivationFunctionType
 MULT = mybir.AluOpType.mult
 
-W1_CHUNKS = ((0, 128), (128, 256), (256, 512), (512, 768), (768, 1024))
+P = 128
+BANK = 512
+PACK = 4
+PASS = P * PACK
+BLOCKS = BANK // P
+HALF_LIST = BANK // 16
 ROW_TILES = H // P
+TILES_PER_PASS = PASS // P
 GROUPS = T2 // BANK
+SCORE_TILES = N // P
+W1_CHUNK = 2 * P
+RING = 3
+AHEAD = 2
+
+TABLE_WORDS_AT = 0
+FIRST_CODES_AT = 4 * T
+TABLE_SCALES_AT = FIRST_CODES_AT + 4 * W1_CHUNK
+WGS_AT = TABLE_SCALES_AT + 4 * T2
+ROWS_AT = (TABLE_SCALES_AT, WGS_AT, TABLE_SCALES_AT - 4 * T2)
 
 
 def tile_list_plate_proofing_kernel(
@@ -33,16 +47,14 @@ def tile_list_plate_proofing_kernel(
         shared = ctx.enter_context(tc.tile_pool(name="shared", bufs=1))
         psum = ctx.enter_context(tc.psum_pool(name="psum", bufs=1))
 
-        def sb(shape, dtype, name, tag=None, bufs=1):
-            return held.tile(shape, dtype, name=name, tag=tag or name, bufs=bufs, align_bytes=64)
+        def sb(shape, dtype, name, tag=None):
+            return held.tile(shape, dtype, name=name, tag=tag or name, bufs=1, align_bytes=64)
 
         def placed(shape, dtype, name, offset, tag=None):
             return shared.tile(shape, dtype, name=name, tag=tag or name, offset=offset, align_bytes=64)
 
         def row_tile(k, name):
-            if k % 3 == 0:
-                return sb([P, T2], F32, name, tag="rows0")
-            return placed([P, T2], F32, name, (20992, 12800)[k % 3 - 1], tag=f"rows{k % 3}")
+            return placed([P, T2], F32, name, ROWS_AT[k % RING], tag=f"rows{k % RING}")
 
         mx_banks = [psum.tile([P, BANK], F32, name=f"mx_bank{k}") for k in range(4)]
         turn_banks = [psum.tile([P, BANK], F32, name=f"turn_bank{k}") for k in range(4)]
@@ -61,23 +73,28 @@ def tile_list_plate_proofing_kernel(
             for q in range(4):
                 queue.dma_start(plane[32 * q : 32 * q + 4, :].bitcast(I32), rows[4 * q : 4 * q + 4, :].bitcast(I32))
 
-        def interleave(copy, grouped, raw):
-            copy(
-                out=grouped.rearrange("p (c i) t -> p c t i", i=4),
-                in_=raw.rearrange("p t (c i) -> p c t i", i=4),
+        def round_and_interleave(grouped, raw):
+            nc.scalar.copy(
+                out=grouped.rearrange("p (c i) j -> p c j i", i=4),
+                in_=raw.rearrange("p j (c i) -> p c j i", i=4),
             )
+
+        def zeroed(name, tag=None):
+            page = sb([P, T2], F32, name, tag=tag)
+            nc.gpsimd.memset(page[:], 0.0)
+            return page
 
         w1_raw = {}
 
         def load_w1(c):
-            c0, c1 = W1_CHUNKS[c]
-            w1_raw[c] = sb([P, 4, c1 - c0], F32, f"w1_raw{c}", tag="v_w1" if c == 2 else None)
-            nc.sync.dma_start(w1_raw[c][:], w1[:, c0:c1].rearrange("(p j) c -> p j c", j=4))
+            w1_raw[c] = sb([P, PACK, W1_CHUNK], F32, f"w1_raw{c}", tag="w1_raw")
+            cols = slice(c * W1_CHUNK, (c + 1) * W1_CHUNK)
+            nc.sync.dma_start(w1_raw[c][:], w1[:, cols].rearrange("(p j) c -> p j c", j=PACK))
 
-        tab_s = placed([P, T], U8, "tab_s", 20992)
+        tab_s = placed([P, T], U8, "tab_s", TABLE_SCALES_AT)
         w2_s = sb([P, H], U8, "w2_s")
-        nc.vector.memset(tab_s[:].bitcast(I32), 0)
-        nc.gpsimd.memset(w2_s[:].bitcast(I32), 0)
+        nc.gpsimd.memset(tab_s[:].bitcast(I32), 0)
+        nc.vector.memset(w2_s[:].bitcast(I32), 0)
         load_scale_rows(nc.gpsimd, w2_s, w2_scales[0])
         warm = sb([P, 2], F32, "warm")
         nc.vector.memset(warm[:, 0:1], 1.0)
@@ -87,67 +104,54 @@ def tile_list_plate_proofing_kernel(
         list3 = load_list(offs3, "list3")
         list4 = load_list(offs4, "list4")
         load_w1(0)
-        tab_w = placed([P, T], U32, "tab_w", 4096)
+        load_scale_rows(nc.sync, tab_s, tab_scales[0])
+        tab_w = placed([P, T], U32, "tab_w", TABLE_WORDS_AT)
         nc.sync.dma_start(tab_w[:].bitcast(I32), tab_words[0].rearrange("p t i -> p (t i)").bitcast(I32))
         w2_w = sb([P, 2 * H], U8, "w2_w")
         nc.sync.dma_start(w2_w[:].bitcast(I32), w2_words[0].bitcast(I32))
-        load_w1(1)
-        load_scale_rows(nc.scalar, tab_s, tab_scales[0])
-        load_w1(2)
-        wgs_raw = placed([P, S], F32, "wgs_raw", 25088)
-        nc.sync.dma_start(wgs_raw[:], wgs)
-        load_w1(3)
-        load_w1(4)
 
         ident = sb([P, P], F32, "ident")
         make_identity(nc, ident[:])
-        pages, outs = [], []
-
-        def zeroed(name, tag=None):
-            page = sb([P, T2], F32, name, tag=tag)
-            nc.gpsimd.memset(page[:], 0.0)
-            return page
-
-        pages.append(zeroed("page0"))
-        pages.append(zeroed("page1"))
+        pages = [zeroed("page0"), zeroed("page1")]
+        out_pages = []
 
         v_w, v_s = [], []
 
         def gather_table(hh):
-            cols = slice(32 * hh, 32 * hh + 32)
-            s_t = sb([P, BANK], U8, f"v_s{hh}")
-            nc.vector.tensor_copy(s_t[:], tab_s[:].indirect(list1[:, cols]))
-            w_t = sb([P, BANK], U32, f"v_w{hh}")
-            nc.vector.tensor_copy(w_t[:], tab_w[:].indirect(list1[:, cols]))
-            v_s.append(s_t)
-            v_w.append(w_t)
+            entries = list1[:, hh * HALF_LIST : (hh + 1) * HALF_LIST]
+            v_s.append(sb([P, BANK], U8, f"v_s{hh}"))
+            nc.vector.tensor_copy(v_s[hh][:], tab_s[:].indirect(entries))
+            v_w.append(sb([P, BANK], U32, f"v_w{hh}"))
+            nc.vector.tensor_copy(v_w[hh][:], tab_w[:].indirect(entries))
 
         w1_q = {}
 
         def quantise_w1(c):
-            c0, c1 = W1_CHUNKS[c]
-            width = c1 - c0
-            if c == 1:
-                grouped = placed([P, width, 4], BF16, "w1_bf1", 0)
-            else:
-                grouped = sb([P, width, 4], BF16, f"w1_bf{c}", tag=f"early_square{c - 2}" if c >= 3 else None)
-            interleave(nc.scalar.copy, grouped[:], w1_raw[c][:])
             if c == 0:
-                codes = placed([P, width], U32, "w1_c0", 20480)
+                grouped = placed([P, W1_CHUNK, PACK], BF16, "w1_bf0", WGS_AT)
             else:
-                codes = sb([P, width], U32, f"w1_c{c}")
-            plane = sb([P, width], U8, f"w1_s{c}")
-            nc.vector.quantize_mx(codes[:].bitcast(FP8X4), plane[:], grouped[:].rearrange("p c t -> p (c t)"))
-            for i in range(c0 // P, c1 // P):
-                w1_q[i] = (codes[:, i * P - c0 : (i + 1) * P - c0], plane[:, i * P - c0 : (i + 1) * P - c0])
+                grouped = sb([P, W1_CHUNK, PACK], BF16, f"w1_bf{c}", tag=f"early_square{c - 1}" if c >= 2 else None)
+            round_and_interleave(grouped[:], w1_raw[c][:])
+            if c == 0:
+                codes = placed([P, W1_CHUNK], U32, "w1_c0", FIRST_CODES_AT)
+            else:
+                codes = sb([P, W1_CHUNK], U32, f"w1_c{c}")
+            plane = sb([P, W1_CHUNK], U8, f"w1_s{c}")
+            nc.vector.quantize_mx(codes[:].bitcast(FP8X4), plane[:], grouped[:].rearrange("p c j -> p (c j)"))
+            for k in range(W1_CHUNK // P):
+                cols = slice(k * P, (k + 1) * P)
+                w1_q[c * W1_CHUNK // P + k] = (codes[:, cols], plane[:, cols])
 
         quantise_w1(0)
+        load_w1(1)
+        wgs_raw = placed([P, S], F32, "wgs_raw", WGS_AT)
+        nc.sync.dma_start(wgs_raw[:], wgs)
         gather_table(0)
-        quantise_w1(1)
-        quantise_w1(2)
         gather_table(1)
-        wgs_neg = placed([P, S], F32, "wgs_neg", 0)
+        wgs_neg = placed([P, S], F32, "wgs_neg", TABLE_WORDS_AT)
         nc.vector.tensor_scalar_mul(wgs_neg[:], wgs_raw[:], -1.0)
+        quantise_w1(1)
+        load_w1(2)
 
         refs = {}
 
@@ -155,41 +159,42 @@ def tile_list_plate_proofing_kernel(
             refs[i] = row_tile(i, f"ref{i}")
             nc.sync.dma_start(refs[i][:], ref[i * P : (i + 1) * P, :])
 
-        mags = [sb([P, S], F32, f"mag{k}") for k in range(3)]
-        first_mags = [sb([P, BANK], F32, f"first_mag{hh}") for hh in range(2)]
+        mags = [sb([P, S], F32, f"mag{k}") for k in range(RING)]
+        first_mags = [sb([P, BANK], F32, "first_mag0"), sb([P, BANK], F32, "first_mag1", tag="w1_bf1")]
         squares = [sb([P, BANK], F32, f"square{k}") for k in range(4)]
-
-        early = {i: sb([P, BANK], F32, f"early_square{i}") for i in (1, 2)}
+        early_squares = {i: sb([P, BANK], F32, f"early_square{i}") for i in (1, 2)}
 
         def square_tile(i, k):
-            return early[i] if k == 3 and i in early else squares[k]
+            return early_squares[i] if k == len(squares) - 1 and i in early_squares else squares[k]
 
         def respond(i, k):
             hh, which = divmod(k, 2)
             acc = mx_banks[k]
-            for jj in range(4):
+            if which == 0:
+                rhs, rhs_scale = w1_q[i][0].bitcast(FP8X4), w1_q[i][1]
+            else:
+                rhs = w2_w[:, 2 * P * i : 2 * P * (i + 1)].bitcast(FP4X4)
+                rhs_scale = w2_s[:, P * i : P * (i + 1)]
+            for jj in range(BLOCKS):
                 cols = slice(jj * P, (jj + 1) * P)
-                if which == 0:
-                    rhs, rhs_scale = w1_q[i][0].bitcast(FP8X4), w1_q[i][1]
-                else:
-                    rhs = w2_w[:, 2 * P * i : 2 * P * (i + 1)].bitcast(FP4X4)
-                    rhs_scale = w2_s[:, P * i : P * (i + 1)]
                 nc.tensor.matmul_mx(
                     out=acc[:, cols], lhsT=v_w[hh][:, cols].bitcast(FP8X4), lhsT_scale=v_s[hh][:, cols],
                     rhs=rhs, rhs_scale=rhs_scale, start=True, stop=True,
                 )
             nc.scalar.activation(square_tile(i, k)[:], acc[:], ACT.Square)
 
+        def add_transposed(acc, first, second):
+            for which, block in enumerate((first, second)):
+                for jj in range(BLOCKS):
+                    nc.tensor.matmul(
+                        acc[:, jj * P : (jj + 1) * P], block[:, jj * P : (jj + 1) * P], ident[:], is_transpose=True,
+                        start=(which == 0 and jj == 0), stop=(which == 1 and jj == BLOCKS - 1),
+                    )
+
         def magnitude(i, hh):
             total = turn_bank()
-            for which in range(2):
-                for jj in range(4):
-                    cols = slice(jj * P, (jj + 1) * P)
-                    nc.tensor.matmul(
-                        total[:, cols], square_tile(i, 2 * hh + which)[:, cols], ident[:], is_transpose=True,
-                        start=(which == 0 and jj == 0), stop=(which == 1 and jj == 3),
-                    )
-            target = mags[i % 3][:, hh * BANK : (hh + 1) * BANK] if i else first_mags[hh][:]
+            add_transposed(total, square_tile(i, 2 * hh), square_tile(i, 2 * hh + 1))
+            target = mags[i % RING][:, hh * BANK : (hh + 1) * BANK] if i else first_mags[hh][:]
             nc.scalar.activation(target, total[:], ACT.Sqrt)
 
         def magnitudes(i):
@@ -199,144 +204,140 @@ def tile_list_plate_proofing_kernel(
                 magnitude(i, hh)
 
         def place(i):
-            page = pages[i % 3]
+            page = pages[i % RING]
             if i:
-                nc.vector.tensor_tensor(page[:].indirect(list2[:]), mags[i % 3][:], wgs_neg[:], MULT)
+                nc.vector.tensor_tensor(page[:].indirect(list2[:]), mags[i % RING][:], wgs_neg[:], MULT)
             else:
                 for hh in range(2):
                     nc.vector.tensor_tensor(
-                        page[:].indirect(list2[:, 32 * hh : 32 * hh + 32]), first_mags[hh][:],
+                        page[:].indirect(list2[:, hh * HALF_LIST : (hh + 1) * HALF_LIST]), first_mags[hh][:],
                         wgs_neg[:, hh * BANK : (hh + 1) * BANK], MULT,
                     )
 
         z_t = {}
 
         def deviation(i, g):
-            b, quarter = divmod(i, 4)
-            page = pages[i % 3]
+            b, quarter = divmod(i, TILES_PER_PASS)
             if quarter == 0:
-                z_t[b, g] = sb([P, 4, 2, P, 2], BF16, f"z_t{b}_{g}")
-            acc = mx_banks[g] if i >= ROW_TILES - 2 else turn_bank()
-            for which, src in enumerate((refs[i], page)):
-                for tb in range(4):
-                    nc.tensor.matmul(
-                        acc[:, tb * P : (tb + 1) * P], src[:, g * BANK + tb * P : g * BANK + (tb + 1) * P], ident[:],
-                        is_transpose=True, start=(which == 0 and tb == 0), stop=(which == 1 and tb == 3),
-                    )
+                z_t[b, g] = sb([P, BLOCKS, 2, P, 2], BF16, f"z_t{b}_{g}")
+            acc = mx_banks[g] if i >= ROW_TILES - AHEAD else turn_bank()
+            cols = slice(g * BANK, (g + 1) * BANK)
+            add_transposed(acc, refs[i][:, cols], pages[i % RING][:, cols])
             nc.scalar.copy(
                 out=z_t[b, g][:, :, :, 32 * quarter : 32 * quarter + 32, :],
-                in_=acc[:].rearrange("s (tb p u e) -> s tb u p e", tb=4, u=2, e=2),
+                in_=acc[:].rearrange("s (tb p u e) -> s tb u p e", tb=BLOCKS, u=2, e=2),
             )
 
         z_q = {}
-        z_bf = [sb([P, BANK * 4], BF16, f"z_bf{k}") for k in range(4)]
+        z_bf = [sb([P, BANK * PACK], BF16, f"z_bf{g}") for g in range(GROUPS)]
 
         def turn_back(b, g, second_copy):
             words = z_t[b, g][:].rearrange("s tb u p e -> s (tb u p e)").bitcast(F32)
-            grouped = z_bf[g]
-            grouped_words = grouped[:].bitcast(F32)
+            grouped_words = z_bf[g][:].bitcast(F32)
             for half in range(2):
                 acc = turn_bank()
-                for k in range(4):
-                    src = words[:, (4 * half + k) * P : (4 * half + k + 1) * P]
+                for k in range(BLOCKS):
+                    src = words[:, (BLOCKS * half + k) * P : (BLOCKS * half + k + 1) * P]
                     nc.tensor.transpose(acc[:, k * P : (k + 1) * P], src, ident[:])
                 copy = second_copy if half else nc.scalar.copy
                 copy(
-                    out=grouped_words[:, half * BANK : (half + 1) * BANK].rearrange("p (tb t u) -> p tb t u", tb=2, u=2),
-                    in_=acc[:].rearrange("p (tb u t) -> p tb t u", tb=2, u=2),
+                    out=grouped_words[:, half * BANK : (half + 1) * BANK].rearrange("p (tb s u) -> p tb s u", tb=2, u=2),
+                    in_=acc[:].rearrange("p (tb u s) -> p tb s u", tb=2, u=2),
                 )
 
         def quantise_z(b, g):
-            grouped = z_bf[g]
             codes = sb([P, BANK], U32, f"z_c{b}_{g}")
-            plane = sb([P, BANK], U8, f"z_s{b}_{g}") if b else placed([P, BANK], U8, f"z_s{b}_{g}", g * BANK)
-            nc.vector.quantize_mx(codes[:].bitcast(FP8X4), plane[:], grouped[:])
+            if b:
+                plane = sb([P, BANK], U8, f"z_s{b}_{g}")
+            else:
+                plane = placed([P, BANK], U8, f"z_s{b}_{g}", TABLE_WORDS_AT + g * BANK)
+            nc.vector.quantize_mx(codes[:].bitcast(FP8X4), plane[:], z_bf[g][:])
             z_q[b, g] = (codes, plane)
 
-        w3_bf = sb([P, 2 * N, 4], BF16, "w3_bf")
+        w3_bf = sb([P, 2 * N, PACK], BF16, "w3_bf")
         w3_c = sb([P, 2 * N], U32, "w3_c")
-        w3_s = placed([P, 2 * N], U8, "w3_s", 4 * BANK)
+        w3_s = placed([P, 2 * N], U8, "w3_s", TABLE_WORDS_AT + GROUPS * BANK)
 
         def round_w3(b):
-            raw = sb([P, 4, N], F32, f"w3_raw{b}", tag=f"v_w{b}")
-            nc.sync.dma_start(raw[:], w3[b * 512 : (b + 1) * 512, :].rearrange("(p j) n -> p j n", j=4))
-            interleave(nc.scalar.copy, w3_bf[:, b * N : (b + 1) * N, :], raw[:])
+            raw = sb([P, PACK, N], F32, f"w3_raw{b}", tag=f"v_w{b}")
+            nc.sync.dma_start(raw[:], w3[b * PASS : (b + 1) * PASS, :].rearrange("(p j) n -> p j n", j=PACK))
+            round_and_interleave(w3_bf[:, b * N : (b + 1) * N, :], raw[:])
 
         def quantise_w3():
-            flat = w3_bf[:].rearrange("p c t -> p (c t)")
-            for c0, c1 in ((0, 512), (512, 768)):
-                nc.vector.quantize_mx(w3_c[:, c0:c1].bitcast(FP8X4), w3_s[:, c0:c1], flat[:, 4 * c0 : 4 * c1])
+            flat = w3_bf[:].rearrange("p c j -> p (c j)")
+            for c0, c1 in ((0, BANK), (BANK, 2 * N)):
+                nc.vector.quantize_mx(w3_c[:, c0:c1].bitcast(FP8X4), w3_s[:, c0:c1], flat[:, PACK * c0 : PACK * c1])
 
         load_ref(0)
         magnitudes(0)
-        pages.append(zeroed("page2", tag="w1_s0"))
         place(0)
         magnitudes(1)
-        outs.append(zeroed("out_page0", tag="w1_c1"))
-        outs.append(zeroed("out_page1", tag="w1_s1"))
-        quantise_w1(3)
+        pages.append(zeroed("page2", tag="w1_s0"))
+        quantise_w1(2)
+        load_w1(3)
         load_ref(1)
         magnitudes(2)
-        quantise_w1(4)
+        quantise_w1(3)
         for i in range(1, ROW_TILES):
             place(i)
             if i + 1 < ROW_TILES:
                 load_ref(i + 1)
+            if i + AHEAD < ROW_TILES:
+                for k in range(len(squares)):
+                    respond(i + AHEAD, k)
+            if i == 1:
+                out_pages.append(zeroed("out_page0", tag="w1_c1"))
+                out_pages.append(zeroed("out_page1", tag="w1_s1"))
             for g in range(GROUPS):
-                if i + 2 < ROW_TILES:
-                    respond(i + 2, g)
                 deviation(i - 1, g)
-            if i == 4:
+            if i == TILES_PER_PASS:
                 turn_back(0, 0, nc.scalar.copy)
-            if i == 5:
+            if i == TILES_PER_PASS + 1:
                 for g in range(1, GROUPS):
                     turn_back(0, g, nc.scalar.copy)
-            if i + 2 < ROW_TILES:
-                magnitude(i + 2, 0)
-                magnitude(i + 2, 1)
+            if i + AHEAD < ROW_TILES:
+                magnitude(i + AHEAD, 0)
+                magnitude(i + AHEAD, 1)
             else:
-                round_w3(i - 6)
+                round_w3(i + AHEAD - ROW_TILES)
         for g in range(GROUPS):
             quantise_z(0, g)
         quantise_w3()
 
-        sens_t = sb([P, N // P, M], F32, "sens_t", tag="w2_w")
+        sens_t = sb([P, SCORE_TILES, M], F32, "sens_t", tag="w2_w")
         nc.sync.dma_start(sens_t[:], sens.rearrange("(n p) m -> p n m", p=P))
-        wgo_t = sb([P, M], F32, "wgo_t", tag="w1_c4")
+        wgo_t = sb([P, M], F32, "wgo_t", tag="w1_c3")
         nc.sync.dma_start(wgo_t[:], wgo)
 
-        scores = [row_tile(ROW_TILES + n, f"score{n}") for n in range(N // P)]
+        scores = [row_tile(ROW_TILES + n, f"score{n}") for n in range(SCORE_TILES)]
 
-        def score_pass(n, g, b):
-            cols = slice(b * N + n * P, b * N + (n + 1) * P)
-            nc.tensor.matmul_mx(
-                out=mx_banks[g][:], lhsT=w3_c[:, cols].bitcast(FP8X4), lhsT_scale=w3_s[:, cols],
-                rhs=z_q[b, g][0][:].bitcast(FP8X4), rhs_scale=z_q[b, g][1][:], start=(b == 0), stop=(b == 1),
-            )
-
-        def score_out(n, g):
-            score_pass(n, g, 0)
-            score_pass(n, g, 1)
-            cols = slice(g * BANK, (g + 1) * BANK)
+        def score(n, g):
+            for b in range(2):
+                cols = slice(b * N + n * P, b * N + (n + 1) * P)
+                nc.tensor.matmul_mx(
+                    out=mx_banks[g][:], lhsT=w3_c[:, cols].bitcast(FP8X4), lhsT_scale=w3_s[:, cols],
+                    rhs=z_q[b, g][0][:].bitcast(FP8X4), rhs_scale=z_q[b, g][1][:], start=(b == 0), stop=(b == 1),
+                )
+            target = scores[n][:, g * BANK : (g + 1) * BANK]
             if (n, g) == (0, GROUPS - 1):
-                nc.vector.tensor_scalar_mul(scores[n][:, cols], mx_banks[g][:], -1.0)
+                nc.vector.tensor_scalar_mul(target, mx_banks[g][:], -1.0)
             else:
-                nc.scalar.activation(scores[n][:, cols], mx_banks[g][:], ACT.Copy, scale=-1.0)
+                nc.scalar.activation(target, mx_banks[g][:], ACT.Copy, scale=-1.0)
 
         last = ROW_TILES - 1
         deviation(last, 0)
         for g in range(GROUPS):
             if g + 1 < GROUPS:
                 deviation(last, g + 1)
-            turn_back(1, g, nc.vector.tensor_copy if g in (1, 2) else nc.scalar.copy)
+            turn_back(1, g, nc.vector.tensor_copy if 0 < g < GROUPS - 1 else nc.scalar.copy)
             quantise_z(1, g)
-        for n in range(N // P):
+        for n in range(SCORE_TILES):
             for g in range(GROUPS):
-                score_out(n, g)
+                score(n, g)
 
-        for n in range(N // P):
+        for n in range(SCORE_TILES):
             picked = mags[n]
             nc.vector.tensor_tensor(picked[:], scores[n][:].indirect(list3[:]), sens_t[:, n, :], MULT)
-            page = outs[n % 2]
+            page = out_pages[n % len(out_pages)]
             nc.vector.tensor_tensor(page[:].indirect(list4[:]), picked[:], wgo_t[:], MULT)
             nc.sync.dma_start(out[n * P : (n + 1) * P, :], page[:])

@@ -27,15 +27,19 @@ ROW_TILES = H // P
 TILES_PER_PASS = PASS // P
 GROUPS = T2 // BANK
 SCORE_TILES = N // P
-W1_CHUNK = 2 * P
+QUARTER = 2 * P
+W1_RUNS = ((0, 1), (1, 3), (3, ROW_TILES))
 RING = 3
 AHEAD = 2
 
+KIB = 1024
 TABLE_WORDS_AT = 0
-FIRST_CODES_AT = 4 * T
-TABLE_SCALES_AT = FIRST_CODES_AT + 4 * W1_CHUNK
-WGS_AT = TABLE_SCALES_AT + 4 * T2
-ROWS_AT = (TABLE_SCALES_AT, WGS_AT, TABLE_SCALES_AT - 4 * T2)
+WGS_NEG_AT = 8 * KIB
+W1_BF_AT = (31 * KIB + KIB // 2, 12 * KIB)
+TABLE_SCALES_AT = 16 * KIB
+W1_RAW_AT = (24 * KIB, 28 * KIB, 32 * KIB)
+WGS_AT = W1_RAW_AT[0]
+ROWS_AT = (TABLE_SCALES_AT, TABLE_WORDS_AT, W1_RAW_AT[2])
 
 
 def tile_list_plate_proofing_kernel(
@@ -73,85 +77,84 @@ def tile_list_plate_proofing_kernel(
             for q in range(4):
                 queue.dma_start(plane[32 * q : 32 * q + 4, :].bitcast(I32), rows[4 * q : 4 * q + 4, :].bitcast(I32))
 
-        def round_and_interleave(grouped, raw):
-            nc.scalar.copy(
+        def round_and_interleave(copy, grouped, raw):
+            copy(
                 out=grouped.rearrange("p (c i) j -> p c j i", i=4),
                 in_=raw.rearrange("p j (c i) -> p c j i", i=4),
             )
 
-        def zeroed(name, tag=None):
+        def zeroed(engine, name, tag=None):
             page = sb([P, T2], F32, name, tag=tag)
-            nc.gpsimd.memset(page[:], 0.0)
+            engine.memset(page[:], 0.0)
             return page
 
         w1_raw = {}
 
         def load_w1(c):
-            w1_raw[c] = sb([P, PACK, W1_CHUNK], F32, f"w1_raw{c}", tag="w1_raw")
-            cols = slice(c * W1_CHUNK, (c + 1) * W1_CHUNK)
-            nc.sync.dma_start(w1_raw[c][:], w1[:, cols].rearrange("(p j) c -> p j c", j=PACK))
+            first, end = W1_RUNS[c]
+            w1_raw[c] = placed([P, PACK, (end - first) * P], F32, f"w1_raw{c}", W1_RAW_AT[c])
+            nc.sync.dma_start(w1_raw[c][:], w1[:, first * P : end * P].rearrange("(p j) c -> p j c", j=PACK))
 
         tab_s = placed([P, T], U8, "tab_s", TABLE_SCALES_AT)
         w2_s = sb([P, H], U8, "w2_s")
         nc.gpsimd.memset(tab_s[:].bitcast(I32), 0)
         nc.vector.memset(w2_s[:].bitcast(I32), 0)
-        load_scale_rows(nc.gpsimd, w2_s, w2_scales[0])
         warm = sb([P, 2], F32, "warm")
         nc.vector.memset(warm[:, 0:1], 1.0)
         nc.scalar.activation(warm[:, 1:2], warm[:, 0:1], ACT.Sqrt)
         list1 = load_list(offs, "list1")
         list2 = load_list(offs2, "list2")
-        list3 = load_list(offs3, "list3")
-        list4 = load_list(offs4, "list4")
         load_w1(0)
         load_scale_rows(nc.sync, tab_s, tab_scales[0])
         tab_w = placed([P, T], U32, "tab_w", TABLE_WORDS_AT)
         nc.sync.dma_start(tab_w[:].bitcast(I32), tab_words[0].rearrange("p t i -> p (t i)").bitcast(I32))
         w2_w = sb([P, 2 * H], U8, "w2_w")
         nc.sync.dma_start(w2_w[:].bitcast(I32), w2_words[0].bitcast(I32))
+        load_scale_rows(nc.sync, w2_s, w2_scales[0])
+        list3 = load_list(offs3, "list3")
+        list4 = load_list(offs4, "list4")
 
         ident = sb([P, P], F32, "ident")
         make_identity(nc, ident[:])
-        pages = [zeroed("page0"), zeroed("page1")]
+        pages = [zeroed(nc.vector, "page0"), zeroed(nc.gpsimd, "page1")]
         out_pages = []
 
-        v_w, v_s = [], []
-
-        def gather_table(hh):
-            entries = list1[:, hh * HALF_LIST : (hh + 1) * HALF_LIST]
-            v_s.append(sb([P, BANK], U8, f"v_s{hh}"))
-            nc.vector.tensor_copy(v_s[hh][:], tab_s[:].indirect(entries))
-            v_w.append(sb([P, BANK], U32, f"v_w{hh}"))
-            nc.vector.tensor_copy(v_w[hh][:], tab_w[:].indirect(entries))
+        halves = [list1[:, hh * HALF_LIST : (hh + 1) * HALF_LIST] for hh in range(2)]
+        v_s = [sb([P, BANK], U8, f"v_s{hh}") for hh in range(2)]
+        v_w = [sb([P, BANK], U32, f"v_w{hh}") for hh in range(2)]
 
         w1_q = {}
 
-        def quantise_w1(c):
-            if c == 0:
-                grouped = placed([P, W1_CHUNK, PACK], BF16, "w1_bf0", WGS_AT)
+        def quantise_w1(c, copy):
+            first, end = W1_RUNS[c]
+            width = (end - first) * P
+            if c < len(W1_BF_AT):
+                grouped = placed([P, width, PACK], BF16, f"w1_bf{c}", W1_BF_AT[c])
             else:
-                grouped = sb([P, W1_CHUNK, PACK], BF16, f"w1_bf{c}", tag=f"early_square{c - 1}" if c >= 2 else None)
-            round_and_interleave(grouped[:], w1_raw[c][:])
-            if c == 0:
-                codes = placed([P, W1_CHUNK], U32, "w1_c0", FIRST_CODES_AT)
-            else:
-                codes = sb([P, W1_CHUNK], U32, f"w1_c{c}")
-            plane = sb([P, W1_CHUNK], U8, f"w1_s{c}")
-            nc.vector.quantize_mx(codes[:].bitcast(FP8X4), plane[:], grouped[:].rearrange("p c j -> p (c j)"))
-            for k in range(W1_CHUNK // P):
+                grouped = sb([P, width, PACK], BF16, f"w1_bf{c}")
+            round_and_interleave(copy, grouped[:], w1_raw[c][:])
+            codes = sb([P, width], U32, f"w1_c{c}")
+            plane = sb([P, width], U8, f"w1_s{c}")
+            flat = grouped[:].rearrange("p c j -> p (c j)")
+            for c0 in range(0, width, BANK):
+                c1 = min(c0 + BANK, width)
+                nc.vector.quantize_mx(codes[:, c0:c1].bitcast(FP8X4), plane[:, c0:c1], flat[:, PACK * c0 : PACK * c1])
+            for k in range(end - first):
                 cols = slice(k * P, (k + 1) * P)
-                w1_q[c * W1_CHUNK // P + k] = (codes[:, cols], plane[:, cols])
+                w1_q[first + k] = (codes[:, cols], plane[:, cols])
 
-        quantise_w1(0)
-        load_w1(1)
+        quantise_w1(0, nc.scalar.copy)
         wgs_raw = placed([P, S], F32, "wgs_raw", WGS_AT)
         nc.sync.dma_start(wgs_raw[:], wgs)
-        gather_table(0)
-        gather_table(1)
-        wgs_neg = placed([P, S], F32, "wgs_neg", TABLE_WORDS_AT)
-        nc.vector.tensor_scalar_mul(wgs_neg[:], wgs_raw[:], -1.0)
-        quantise_w1(1)
+        load_w1(1)
         load_w1(2)
+        for hh in range(2):
+            nc.vector.tensor_copy(v_s[hh][:], tab_s[:].indirect(halves[hh]))
+        for hh in range(2):
+            nc.vector.tensor_copy(v_w[hh][:], tab_w[:].indirect(halves[hh]))
+        wgs_neg = placed([P, S], F32, "wgs_neg", WGS_NEG_AT)
+        nc.vector.tensor_scalar_mul(wgs_neg[:], wgs_raw[:], -1.0)
+        quantise_w1(1, nc.vector.tensor_copy)
 
         refs = {}
 
@@ -160,59 +163,56 @@ def tile_list_plate_proofing_kernel(
             nc.sync.dma_start(refs[i][:], ref[i * P : (i + 1) * P, :])
 
         mags = [sb([P, S], F32, f"mag{k}") for k in range(RING)]
-        first_mags = [sb([P, BANK], F32, "first_mag0"), sb([P, BANK], F32, "first_mag1", tag="w1_bf1")]
-        squares = [sb([P, BANK], F32, f"square{k}") for k in range(4)]
-        early_squares = {i: sb([P, BANK], F32, f"early_square{i}") for i in (1, 2)}
+        first_mags = [sb([P, QUARTER], F32, f"first_mag{q}") for q in range(4)]
+        squares = [sb([P, BANK], F32, f"square{q}") for q in range(4)]
 
-        def square_tile(i, k):
-            return early_squares[i] if k == len(squares) - 1 and i in early_squares else squares[k]
-
-        def respond(i, k):
-            hh, which = divmod(k, 2)
-            acc = mx_banks[k]
-            if which == 0:
-                rhs, rhs_scale = w1_q[i][0].bitcast(FP8X4), w1_q[i][1]
-            else:
-                rhs = w2_w[:, 2 * P * i : 2 * P * (i + 1)].bitcast(FP4X4)
-                rhs_scale = w2_s[:, P * i : P * (i + 1)]
-            for jj in range(BLOCKS):
-                cols = slice(jj * P, (jj + 1) * P)
-                nc.tensor.matmul_mx(
-                    out=acc[:, cols], lhsT=v_w[hh][:, cols].bitcast(FP8X4), lhsT_scale=v_s[hh][:, cols],
-                    rhs=rhs, rhs_scale=rhs_scale, start=True, stop=True,
-                )
-            nc.scalar.activation(square_tile(i, k)[:], acc[:], ACT.Square)
-
-        def add_transposed(acc, first, second):
-            for which, block in enumerate((first, second)):
-                for jj in range(BLOCKS):
-                    nc.tensor.matmul(
-                        acc[:, jj * P : (jj + 1) * P], block[:, jj * P : (jj + 1) * P], ident[:], is_transpose=True,
-                        start=(which == 0 and jj == 0), stop=(which == 1 and jj == BLOCKS - 1),
+        def respond(i, q):
+            acc = mx_banks[q]
+            hh = q // 2
+            operands = (
+                (w2_w[:, 2 * P * i : 2 * P * (i + 1)].bitcast(FP4X4), w2_s[:, P * i : P * (i + 1)]),
+                (w1_q[i][0].bitcast(FP8X4), w1_q[i][1]),
+            )
+            for which, (rhs, rhs_scale) in enumerate(operands):
+                for jj in range(2):
+                    entries = slice((2 * (q % 2) + jj) * P, (2 * (q % 2) + jj + 1) * P)
+                    nc.tensor.matmul_mx(
+                        out=acc[:, (2 * which + jj) * P : (2 * which + jj + 1) * P],
+                        lhsT=v_w[hh][:, entries].bitcast(FP8X4), lhsT_scale=v_s[hh][:, entries],
+                        rhs=rhs, rhs_scale=rhs_scale, start=True, stop=True,
                     )
+            nc.scalar.activation(squares[q][:], acc[:], ACT.Square)
 
-        def magnitude(i, hh):
+        def add_transposed(acc, blocks):
+            for k, (jj, block) in enumerate(blocks):
+                nc.tensor.matmul(
+                    acc[:, jj * P : (jj + 1) * P], block, ident[:], is_transpose=True,
+                    start=(k == 0), stop=(k == len(blocks) - 1),
+                )
+
+        def blocks_of(tile, count=BLOCKS, first=0, to=0):
+            return [(to + jj, tile[:, (first + jj) * P : (first + jj + 1) * P]) for jj in range(count)]
+
+        def magnitude(target, quarters):
             total = turn_bank()
-            add_transposed(total, square_tile(i, 2 * hh), square_tile(i, 2 * hh + 1))
-            target = mags[i % RING][:, hh * BANK : (hh + 1) * BANK] if i else first_mags[hh][:]
-            nc.scalar.activation(target, total[:], ACT.Sqrt)
+            blocks = []
+            for k, q in enumerate(quarters):
+                blocks.extend(blocks_of(squares[q], 2, 0, 2 * k) + blocks_of(squares[q], 2, 2, 2 * k))
+            add_transposed(total, blocks)
+            nc.scalar.activation(target, total[:, : len(quarters) * QUARTER], ACT.Sqrt)
 
-        def magnitudes(i):
-            for hh in range(2):
-                respond(i, 2 * hh)
-                respond(i, 2 * hh + 1)
-                magnitude(i, hh)
+        def half_magnitude(i, hh):
+            magnitude(mags[i % RING][:, hh * BANK : (hh + 1) * BANK], (2 * hh, 2 * hh + 1))
 
         def place(i):
-            page = pages[i % RING]
-            if i:
-                nc.vector.tensor_tensor(page[:].indirect(list2[:]), mags[i % RING][:], wgs_neg[:], MULT)
-            else:
-                for hh in range(2):
-                    nc.vector.tensor_tensor(
-                        page[:].indirect(list2[:, hh * HALF_LIST : (hh + 1) * HALF_LIST]), first_mags[hh][:],
-                        wgs_neg[:, hh * BANK : (hh + 1) * BANK], MULT,
-                    )
+            nc.vector.tensor_tensor(pages[i % RING][:].indirect(list2[:]), mags[i % RING][:], wgs_neg[:], MULT)
+
+        def place_first(q):
+            columns = QUARTER // 16
+            nc.vector.tensor_tensor(
+                pages[0][:].indirect(list2[:, q * columns : (q + 1) * columns]), first_mags[q][:],
+                wgs_neg[:, q * QUARTER : (q + 1) * QUARTER], MULT,
+            )
 
         z_t = {}
 
@@ -222,7 +222,7 @@ def tile_list_plate_proofing_kernel(
                 z_t[b, g] = sb([P, BLOCKS, 2, P, 2], BF16, f"z_t{b}_{g}")
             acc = mx_banks[g] if i >= ROW_TILES - AHEAD else turn_bank()
             cols = slice(g * BANK, (g + 1) * BANK)
-            add_transposed(acc, refs[i][:, cols], pages[i % RING][:, cols])
+            add_transposed(acc, blocks_of(refs[i][:, cols]) + blocks_of(pages[i % RING][:, cols]))
             nc.scalar.copy(
                 out=z_t[b, g][:, :, :, 32 * quarter : 32 * quarter + 32, :],
                 in_=acc[:].rearrange("s (tb p u e) -> s tb u p e", tb=BLOCKS, u=2, e=2),
@@ -250,18 +250,18 @@ def tile_list_plate_proofing_kernel(
             if b:
                 plane = sb([P, BANK], U8, f"z_s{b}_{g}")
             else:
-                plane = placed([P, BANK], U8, f"z_s{b}_{g}", TABLE_WORDS_AT + g * BANK)
+                plane = placed([P, BANK], U8, f"z_s{b}_{g}", WGS_NEG_AT + g * BANK)
             nc.vector.quantize_mx(codes[:].bitcast(FP8X4), plane[:], z_bf[g][:])
             z_q[b, g] = (codes, plane)
 
         w3_bf = sb([P, 2 * N, PACK], BF16, "w3_bf")
         w3_c = sb([P, 2 * N], U32, "w3_c")
-        w3_s = placed([P, 2 * N], U8, "w3_s", TABLE_WORDS_AT + GROUPS * BANK)
+        w3_s = placed([P, 2 * N], U8, "w3_s", WGS_NEG_AT + GROUPS * BANK)
 
         def round_w3(b):
             raw = sb([P, PACK, N], F32, f"w3_raw{b}", tag=f"v_w{b}")
             nc.sync.dma_start(raw[:], w3[b * PASS : (b + 1) * PASS, :].rearrange("(p j) n -> p j n", j=PACK))
-            round_and_interleave(w3_bf[:, b * N : (b + 1) * N, :], raw[:])
+            round_and_interleave(nc.scalar.copy, w3_bf[:, b * N : (b + 1) * N, :], raw[:])
 
         def quantise_w3():
             flat = w3_bf[:].rearrange("p c j -> p (c j)")
@@ -269,44 +269,47 @@ def tile_list_plate_proofing_kernel(
                 nc.vector.quantize_mx(w3_c[:, c0:c1].bitcast(FP8X4), w3_s[:, c0:c1], flat[:, PACK * c0 : PACK * c1])
 
         load_ref(0)
-        magnitudes(0)
-        place(0)
-        magnitudes(1)
-        pages.append(zeroed("page2", tag="w1_s0"))
-        quantise_w1(2)
-        load_w1(3)
+        for q in range(4):
+            respond(0, q)
+            magnitude(first_mags[q][:], (q,))
+            place_first(q)
+        quantise_w1(2, nc.vector.tensor_copy)
+        pages.append(zeroed(nc.gpsimd, "page2", tag="w1_bf2"))
+        out_pages.append(zeroed(nc.gpsimd, "out_page0", tag="first_mag2"))
+        out_pages.append(zeroed(nc.gpsimd, "out_page1", tag="first_mag3"))
         load_ref(1)
-        magnitudes(2)
-        quantise_w1(3)
+        for i in range(1, 1 + AHEAD):
+            for hh in range(2):
+                respond(i, 2 * hh)
+                respond(i, 2 * hh + 1)
+            for hh in range(2):
+                half_magnitude(i, hh)
         for i in range(1, ROW_TILES):
             place(i)
             if i + 1 < ROW_TILES:
                 load_ref(i + 1)
-            if i + AHEAD < ROW_TILES:
-                for k in range(len(squares)):
-                    respond(i + AHEAD, k)
-            if i == 1:
-                out_pages.append(zeroed("out_page0", tag="w1_c1"))
-                out_pages.append(zeroed("out_page1", tag="w1_s1"))
-            for g in range(GROUPS):
-                deviation(i - 1, g)
-            if i == TILES_PER_PASS:
-                turn_back(0, 0, nc.scalar.copy)
-            if i == TILES_PER_PASS + 1:
-                for g in range(1, GROUPS):
-                    turn_back(0, g, nc.scalar.copy)
-            if i + AHEAD < ROW_TILES:
-                magnitude(i + AHEAD, 0)
-                magnitude(i + AHEAD, 1)
+            ahead = i + AHEAD
+            for hh in range(2):
+                if ahead < ROW_TILES:
+                    respond(ahead, 2 * hh)
+                    respond(ahead, 2 * hh + 1)
+                    if hh:
+                        half_magnitude(ahead, 0)
+                deviation(i - 1, 2 * hh)
+                deviation(i - 1, 2 * hh + 1)
+                if ahead >= ROW_TILES:
+                    turn_back(0, 2 * (ahead - ROW_TILES) + hh, nc.scalar.copy)
+            if ahead < ROW_TILES:
+                half_magnitude(ahead, 1)
             else:
-                round_w3(i + AHEAD - ROW_TILES)
+                round_w3(ahead - ROW_TILES)
         for g in range(GROUPS):
             quantise_z(0, g)
         quantise_w3()
 
         sens_t = sb([P, SCORE_TILES, M], F32, "sens_t", tag="w2_w")
         nc.sync.dma_start(sens_t[:], sens.rearrange("(n p) m -> p n m", p=P))
-        wgo_t = sb([P, M], F32, "wgo_t", tag="w1_c3")
+        wgo_t = sb([P, M], F32, "wgo_t", tag="w1_c2")
         nc.sync.dma_start(wgo_t[:], wgo)
 
         scores = [row_tile(ROW_TILES + n, f"score{n}") for n in range(SCORE_TILES)]

@@ -28,18 +28,18 @@ TILES_PER_PASS = PASS // P
 GROUPS = T2 // BANK
 SCORE_TILES = N // P
 QUARTER = 2 * P
-W1_RUNS = ((0, 1), (1, 3), (3, ROW_TILES))
+W1_RUNS = ((0, 1), (1, 2), (2, 4), (4, ROW_TILES))
 RING = 3
 AHEAD = 2
 
 KIB = 1024
 TABLE_WORDS_AT = 0
-WGS_NEG_AT = 8 * KIB
-W1_BF_AT = (31 * KIB + KIB // 2, 12 * KIB)
-TABLE_SCALES_AT = 16 * KIB
-W1_RAW_AT = (24 * KIB, 28 * KIB, 32 * KIB)
-WGS_AT = W1_RAW_AT[0]
-ROWS_AT = (TABLE_SCALES_AT, TABLE_WORDS_AT, W1_RAW_AT[2])
+TABLE_SCALES_AT = 24 * KIB
+WGS_AT = 27 * KIB
+W1_RAW_AT = (44 * KIB, 25 * KIB, 21 * KIB, 8 * KIB)
+W1_BF_AT = (46 * KIB, 47 * KIB, 32 * KIB)
+WGS_NEG_AT = 40 * KIB
+ROWS_AT = (TABLE_WORDS_AT, 32 * KIB, W1_RAW_AT[3])
 
 
 def tile_list_plate_proofing_kernel(
@@ -104,6 +104,8 @@ def tile_list_plate_proofing_kernel(
         nc.scalar.activation(warm[:, 1:2], warm[:, 0:1], ACT.Sqrt)
         list1 = load_list(offs, "list1")
         list2 = load_list(offs2, "list2")
+        list3 = load_list(offs3, "list3")
+        list4 = load_list(offs4, "list4")
         load_w1(0)
         load_scale_rows(nc.sync, tab_s, tab_scales[0])
         tab_w = placed([P, T], U32, "tab_w", TABLE_WORDS_AT)
@@ -111,13 +113,10 @@ def tile_list_plate_proofing_kernel(
         w2_w = sb([P, 2 * H], U8, "w2_w")
         nc.sync.dma_start(w2_w[:].bitcast(I32), w2_words[0].bitcast(I32))
         load_scale_rows(nc.sync, w2_s, w2_scales[0])
-        list3 = load_list(offs3, "list3")
-        list4 = load_list(offs4, "list4")
 
         ident = sb([P, P], F32, "ident")
         make_identity(nc, ident[:])
-        pages = [zeroed(nc.vector, "page0"), zeroed(nc.gpsimd, "page1")]
-        out_pages = []
+        pages = [zeroed(nc.vector, "page0"), zeroed(nc.vector, "page1")]
 
         halves = [list1[:, hh * HALF_LIST : (hh + 1) * HALF_LIST] for hh in range(2)]
         v_s = [sb([P, BANK], U8, f"v_s{hh}") for hh in range(2)]
@@ -131,7 +130,7 @@ def tile_list_plate_proofing_kernel(
             if c < len(W1_BF_AT):
                 grouped = placed([P, width, PACK], BF16, f"w1_bf{c}", W1_BF_AT[c])
             else:
-                grouped = sb([P, width, PACK], BF16, f"w1_bf{c}")
+                grouped = sb([P, width, PACK], BF16, f"w1_bf{c}", tag="early_square")
             round_and_interleave(copy, grouped[:], w1_raw[c][:])
             codes = sb([P, width], U32, f"w1_c{c}")
             plane = sb([P, width], U8, f"w1_s{c}")
@@ -144,17 +143,19 @@ def tile_list_plate_proofing_kernel(
                 w1_q[first + k] = (codes[:, cols], plane[:, cols])
 
         quantise_w1(0, nc.scalar.copy)
+        for hh in range(2):
+            nc.vector.tensor_copy(v_s[hh][:], tab_s[:].indirect(halves[hh]))
         wgs_raw = placed([P, S], F32, "wgs_raw", WGS_AT)
         nc.sync.dma_start(wgs_raw[:], wgs)
         load_w1(1)
         load_w1(2)
         for hh in range(2):
-            nc.vector.tensor_copy(v_s[hh][:], tab_s[:].indirect(halves[hh]))
-        for hh in range(2):
             nc.vector.tensor_copy(v_w[hh][:], tab_w[:].indirect(halves[hh]))
+        load_w1(3)
         wgs_neg = placed([P, S], F32, "wgs_neg", WGS_NEG_AT)
         nc.vector.tensor_scalar_mul(wgs_neg[:], wgs_raw[:], -1.0)
         quantise_w1(1, nc.vector.tensor_copy)
+        quantise_w1(2, nc.vector.tensor_copy)
 
         refs = {}
 
@@ -165,6 +166,14 @@ def tile_list_plate_proofing_kernel(
         mags = [sb([P, S], F32, f"mag{k}") for k in range(RING)]
         first_mags = [sb([P, QUARTER], F32, f"first_mag{q}") for q in range(4)]
         squares = [sb([P, BANK], F32, f"square{q}") for q in range(4)]
+
+        early_squares = {
+            (1, 0): sb([P, BANK], F32, "early_square1", tag="page2"),
+            (2, 0): sb([P, BANK], F32, "early_square2", tag="early_square"),
+        }
+
+        def square_tile(i, q):
+            return early_squares.get((i, q), squares[q])
 
         def respond(i, q):
             acc = mx_banks[q]
@@ -181,7 +190,7 @@ def tile_list_plate_proofing_kernel(
                         lhsT=v_w[hh][:, entries].bitcast(FP8X4), lhsT_scale=v_s[hh][:, entries],
                         rhs=rhs, rhs_scale=rhs_scale, start=True, stop=True,
                     )
-            nc.scalar.activation(squares[q][:], acc[:], ACT.Square)
+            nc.scalar.activation(square_tile(i, q)[:], acc[:], ACT.Square)
 
         def add_transposed(acc, blocks):
             for k, (jj, block) in enumerate(blocks):
@@ -193,16 +202,17 @@ def tile_list_plate_proofing_kernel(
         def blocks_of(tile, count=BLOCKS, first=0, to=0):
             return [(to + jj, tile[:, (first + jj) * P : (first + jj + 1) * P]) for jj in range(count)]
 
-        def magnitude(target, quarters):
+        def magnitude(i, target, quarters):
             total = turn_bank()
             blocks = []
             for k, q in enumerate(quarters):
-                blocks.extend(blocks_of(squares[q], 2, 0, 2 * k) + blocks_of(squares[q], 2, 2, 2 * k))
+                square = square_tile(i, q)
+                blocks.extend(blocks_of(square, 2, 0, 2 * k) + blocks_of(square, 2, 2, 2 * k))
             add_transposed(total, blocks)
             nc.scalar.activation(target, total[:, : len(quarters) * QUARTER], ACT.Sqrt)
 
         def half_magnitude(i, hh):
-            magnitude(mags[i % RING][:, hh * BANK : (hh + 1) * BANK], (2 * hh, 2 * hh + 1))
+            magnitude(i, mags[i % RING][:, hh * BANK : (hh + 1) * BANK], (2 * hh, 2 * hh + 1))
 
         def place(i):
             nc.vector.tensor_tensor(pages[i % RING][:].indirect(list2[:]), mags[i % RING][:], wgs_neg[:], MULT)
@@ -271,12 +281,8 @@ def tile_list_plate_proofing_kernel(
         load_ref(0)
         for q in range(4):
             respond(0, q)
-            magnitude(first_mags[q][:], (q,))
+            magnitude(0, first_mags[q][:], (q,))
             place_first(q)
-        quantise_w1(2, nc.vector.tensor_copy)
-        pages.append(zeroed(nc.gpsimd, "page2", tag="w1_bf2"))
-        out_pages.append(zeroed(nc.gpsimd, "out_page0", tag="first_mag2"))
-        out_pages.append(zeroed(nc.gpsimd, "out_page1", tag="first_mag3"))
         load_ref(1)
         for i in range(1, 1 + AHEAD):
             for hh in range(2):
@@ -284,6 +290,8 @@ def tile_list_plate_proofing_kernel(
                 respond(i, 2 * hh + 1)
             for hh in range(2):
                 half_magnitude(i, hh)
+        quantise_w1(3, nc.scalar.copy)
+        pages.append(zeroed(nc.gpsimd, "page2"))
         for i in range(1, ROW_TILES):
             place(i)
             if i + 1 < ROW_TILES:
@@ -297,19 +305,20 @@ def tile_list_plate_proofing_kernel(
                         half_magnitude(ahead, 0)
                 deviation(i - 1, 2 * hh)
                 deviation(i - 1, 2 * hh + 1)
-                if ahead >= ROW_TILES:
-                    turn_back(0, 2 * (ahead - ROW_TILES) + hh, nc.scalar.copy)
+                if ahead in (ROW_TILES - 1, ROW_TILES):
+                    turn_back(0, 2 * (ahead - ROW_TILES + 1) + hh, nc.scalar.copy)
             if ahead < ROW_TILES:
                 half_magnitude(ahead, 1)
             else:
                 round_w3(ahead - ROW_TILES)
+        out_pages = [zeroed(nc.gpsimd, f"out_page{hh}", tag=f"v_s{hh}") for hh in range(2)]
         for g in range(GROUPS):
             quantise_z(0, g)
         quantise_w3()
 
         sens_t = sb([P, SCORE_TILES, M], F32, "sens_t", tag="w2_w")
         nc.sync.dma_start(sens_t[:], sens.rearrange("(n p) m -> p n m", p=P))
-        wgo_t = sb([P, M], F32, "wgo_t", tag="w1_c2")
+        wgo_t = sb([P, M], F32, "wgo_t", tag="w1_c3")
         nc.sync.dma_start(wgo_t[:], wgo)
 
         scores = [row_tile(ROW_TILES + n, f"score{n}") for n in range(SCORE_TILES)]

@@ -16,6 +16,7 @@ FP8X4 = mybir.dt.float8_e4m3fn_x4
 FP4X4 = mybir.dt.float4_e2m1fn_x4
 ACT = mybir.ActivationFunctionType
 MULT = mybir.AluOpType.mult
+ADD = mybir.AluOpType.add
 
 P = 128
 BANK = 512
@@ -104,18 +105,18 @@ def tile_list_plate_proofing_kernel(
         nc.scalar.activation(warm[:, 1:2], warm[:, 0:1], ACT.Sqrt)
         list1 = load_list(offs, "list1")
         list2 = load_list(offs2, "list2")
-        list3 = load_list(offs3, "list3")
-        list4 = load_list(offs4, "list4")
         load_w1(0)
         load_scale_rows(nc.sync, tab_s, tab_scales[0])
         tab_w = placed([P, T], U32, "tab_w", TABLE_WORDS_AT)
         nc.sync.dma_start(tab_w[:].bitcast(I32), tab_words[0].rearrange("p t i -> p (t i)").bitcast(I32))
         w2_w = sb([P, 2 * H], U8, "w2_w")
         nc.sync.dma_start(w2_w[:].bitcast(I32), w2_words[0].bitcast(I32))
-        load_scale_rows(nc.sync, w2_s, w2_scales[0])
+        list3 = load_list(offs3, "list3")
+        list4 = load_list(offs4, "list4")
 
         ident = sb([P, P], F32, "ident")
         make_identity(nc, ident[:])
+        load_scale_rows(nc.gpsimd, w2_s, w2_scales[0])
         pages = [zeroed(nc.vector, "page0"), zeroed(nc.vector, "page1")]
 
         halves = [list1[:, hh * HALF_LIST : (hh + 1) * HALF_LIST] for hh in range(2)]
@@ -214,6 +215,18 @@ def tile_list_plate_proofing_kernel(
         def half_magnitude(i, hh):
             magnitude(i, mags[i % RING][:, hh * BANK : (hh + 1) * BANK], (2 * hh, 2 * hh + 1))
 
+        def first_magnitude():
+            acc, square, mag = mx_banks[0], squares[0], first_mags[0]
+            weights = ((w1_q[0][0].bitcast(FP8X4), w1_q[0][1]), (w2_w[:, : 2 * P].bitcast(FP4X4), w2_s[:, :P]))
+            for which, (lhsT, lhsT_scale) in enumerate(weights):
+                nc.tensor.matmul_mx(
+                    out=acc[:, which * QUARTER : (which + 1) * QUARTER], lhsT=lhsT, lhsT_scale=lhsT_scale,
+                    rhs=v_w[0][:, :QUARTER].bitcast(FP8X4), rhs_scale=v_s[0][:, :QUARTER], start=True, stop=True,
+                )
+            nc.scalar.activation(square[:], acc[:], ACT.Square)
+            nc.vector.tensor_tensor(mag[:], square[:, :QUARTER], square[:, QUARTER:], ADD)
+            nc.scalar.activation(mag[:], mag[:], ACT.Sqrt)
+
         def place(i):
             nc.vector.tensor_tensor(pages[i % RING][:].indirect(list2[:]), mags[i % RING][:], wgs_neg[:], MULT)
 
@@ -280,8 +293,11 @@ def tile_list_plate_proofing_kernel(
 
         load_ref(0)
         for q in range(4):
-            respond(0, q)
-            magnitude(0, first_mags[q][:], (q,))
+            if q:
+                respond(0, q)
+                magnitude(0, first_mags[q][:], (q,))
+            else:
+                first_magnitude()
             place_first(q)
         load_ref(1)
         for i in range(1, 1 + AHEAD):

@@ -159,6 +159,7 @@ def tile_list_plate_proofing_kernel(
         quantise_w1(2, nc.vector.tensor_copy)
 
         refs = {}
+        last = ROW_TILES - 1
 
         def load_ref(i):
             refs[i] = row_tile(i, f"ref{i}")
@@ -193,11 +194,11 @@ def tile_list_plate_proofing_kernel(
                     )
             nc.scalar.activation(square_tile(i, q)[:], acc[:], ACT.Square)
 
-        def add_transposed(acc, blocks):
+        def add_transposed(acc, blocks, opens=True, closes=True, identity=ident):
             for k, (jj, block) in enumerate(blocks):
                 nc.tensor.matmul(
-                    acc[:, jj * P : (jj + 1) * P], block, ident[:], is_transpose=True,
-                    start=(k == 0), stop=(k == len(blocks) - 1),
+                    acc[:, jj * P : (jj + 1) * P], block, identity[:], is_transpose=True,
+                    start=(opens and k == 0), stop=(closes and k == len(blocks) - 1),
                 )
 
         def blocks_of(tile, count=BLOCKS, first=0, to=0):
@@ -245,7 +246,10 @@ def tile_list_plate_proofing_kernel(
                 z_t[b, g] = sb([P, BLOCKS, 2, P, 2], BF16, f"z_t{b}_{g}")
             acc = mx_banks[g] if i >= ROW_TILES - AHEAD else turn_bank()
             cols = slice(g * BANK, (g + 1) * BANK)
-            add_transposed(acc, blocks_of(refs[i][:, cols]) + blocks_of(pages[i % RING][:, cols]))
+            if i < last:
+                add_transposed(acc, blocks_of(refs[i][:, cols]) + blocks_of(pages[i % RING][:, cols]))
+            else:
+                add_transposed(acc, blocks_of(pages[i % RING][:, cols]), opens=False, identity=late_ident)
             nc.scalar.copy(
                 out=z_t[b, g][:, :, :, 32 * quarter : 32 * quarter + 32, :],
                 in_=acc[:].rearrange("s (tb p u e) -> s tb u p e", tb=BLOCKS, u=2, e=2),
@@ -284,7 +288,10 @@ def tile_list_plate_proofing_kernel(
         def round_w3(b):
             raw = sb([P, PACK, N], F32, f"w3_raw{b}", tag=f"v_w{b}")
             nc.sync.dma_start(raw[:], w3[b * PASS : (b + 1) * PASS, :].rearrange("(p j) n -> p j n", j=PACK))
-            round_and_interleave(nc.scalar.copy, w3_bf[:, b * N : (b + 1) * N, :], raw[:])
+            on_scalar = N // 2 if b else N
+            round_and_interleave(nc.scalar.copy, w3_bf[:, b * N : b * N + on_scalar, :], raw[:, :, :on_scalar])
+            if on_scalar < N:
+                round_and_interleave(nc.vector.tensor_copy, w3_bf[:, b * N + on_scalar :, :], raw[:, :, on_scalar:])
 
         def quantise_w3():
             flat = w3_bf[:].rearrange("p c j -> p (c j)")
@@ -321,12 +328,17 @@ def tile_list_plate_proofing_kernel(
                         half_magnitude(ahead, 0)
                 deviation(i - 1, 2 * hh)
                 deviation(i - 1, 2 * hh + 1)
-                if ahead in (ROW_TILES - 1, ROW_TILES):
-                    turn_back(0, 2 * (ahead - ROW_TILES + 1) + hh, nc.scalar.copy)
             if ahead < ROW_TILES:
                 half_magnitude(ahead, 1)
-            else:
+            if ahead in (last, last + 1):
+                for hh in range(2):
+                    turn_back(0, 2 * (ahead - last) + hh, nc.scalar.copy)
+            if ahead > last:
                 round_w3(ahead - ROW_TILES)
+        for g in range(GROUPS):
+            add_transposed(mx_banks[g], blocks_of(refs[last][:, g * BANK : (g + 1) * BANK]), closes=False)
+        late_ident = placed([P, P], F32, "late_ident", ROWS_AT[(last - 1) % RING])
+        nc.scalar.copy(out=late_ident[:], in_=ident[:])
         out_pages = [zeroed(nc.gpsimd, f"out_page{hh}", tag=f"v_s{hh}") for hh in range(2)]
         for g in range(GROUPS):
             quantise_z(0, g)
@@ -352,7 +364,6 @@ def tile_list_plate_proofing_kernel(
             else:
                 nc.scalar.activation(target, mx_banks[g][:], ACT.Copy, scale=-1.0)
 
-        last = ROW_TILES - 1
         deviation(last, 0)
         for g in range(GROUPS):
             if g + 1 < GROUPS:

@@ -61,13 +61,12 @@ def tile_list_plate_proofing_kernel(
         def row_tile(k, name):
             return placed([P, T2], F32, name, ROWS_AT[k % RING], tag=f"rows{k % RING}")
 
-        mx_banks = [psum.tile([P, BANK], F32, name=f"mx_bank{k}") for k in range(4)]
-        turn_banks = [psum.tile([P, BANK], F32, name=f"turn_bank{k}") for k in range(4)]
-        turn_uses = []
+        banks = [psum.tile([P, BANK], F32, name=f"bank{k}") for k in range(8)]
+        bank_uses = []
 
-        def turn_bank():
-            turn_uses.append(None)
-            return turn_banks[(len(turn_uses) - 1) % len(turn_banks)]
+        def next_bank():
+            bank_uses.append(None)
+            return banks[(len(bank_uses) - 1) % len(banks)]
 
         def load_list(src, name):
             tile = held.tile([P, S // 16], U16, name=name)
@@ -178,7 +177,7 @@ def tile_list_plate_proofing_kernel(
             return early_squares.get((i, q), squares[q])
 
         def respond(i, q):
-            acc = mx_banks[q]
+            acc = next_bank()
             hh = q // 2
             operands = (
                 (w2_w[:, 2 * P * i : 2 * P * (i + 1)].bitcast(FP4X4), w2_s[:, P * i : P * (i + 1)]),
@@ -194,10 +193,10 @@ def tile_list_plate_proofing_kernel(
                     )
             nc.scalar.activation(square_tile(i, q)[:], acc[:], ACT.Square)
 
-        def add_transposed(acc, blocks, opens=True, closes=True, identity=ident):
+        def add_transposed(acc, blocks, opens=True, closes=True):
             for k, (jj, block) in enumerate(blocks):
                 nc.tensor.matmul(
-                    acc[:, jj * P : (jj + 1) * P], block, identity[:], is_transpose=True,
+                    acc[:, jj * P : (jj + 1) * P], block, ident[:], is_transpose=True,
                     start=(opens and k == 0), stop=(closes and k == len(blocks) - 1),
                 )
 
@@ -205,7 +204,7 @@ def tile_list_plate_proofing_kernel(
             return [(to + jj, tile[:, (first + jj) * P : (first + jj + 1) * P]) for jj in range(count)]
 
         def magnitude(i, target, quarters):
-            total = turn_bank()
+            total = next_bank()
             blocks = []
             for k, q in enumerate(quarters):
                 square = square_tile(i, q)
@@ -217,7 +216,7 @@ def tile_list_plate_proofing_kernel(
             magnitude(i, mags[i % RING][:, hh * BANK : (hh + 1) * BANK], (2 * hh, 2 * hh + 1))
 
         def first_magnitude():
-            acc, square, mag = mx_banks[0], squares[0], first_mags[0]
+            acc, square, mag = next_bank(), squares[0], first_mags[0]
             weights = ((w1_q[0][0].bitcast(FP8X4), w1_q[0][1]), (w2_w[:, : 2 * P].bitcast(FP4X4), w2_s[:, :P]))
             for which, (lhsT, lhsT_scale) in enumerate(weights):
                 nc.tensor.matmul_mx(
@@ -240,16 +239,17 @@ def tile_list_plate_proofing_kernel(
 
         z_t = {}
 
-        def deviation(i, g):
+        def deviation(i, g, opened=None):
             b, quarter = divmod(i, TILES_PER_PASS)
             if quarter == 0:
                 z_t[b, g] = sb([P, BLOCKS, 2, P, 2], BF16, f"z_t{b}_{g}")
-            acc = mx_banks[g] if i >= ROW_TILES - AHEAD else turn_bank()
             cols = slice(g * BANK, (g + 1) * BANK)
-            if i < last:
+            if opened is None:
+                acc = next_bank()
                 add_transposed(acc, blocks_of(refs[i][:, cols]) + blocks_of(pages[i % RING][:, cols]))
             else:
-                add_transposed(acc, blocks_of(pages[i % RING][:, cols]), opens=False, identity=late_ident)
+                acc = opened
+                add_transposed(acc, blocks_of(pages[i % RING][:, cols]), opens=False)
             nc.scalar.copy(
                 out=z_t[b, g][:, :, :, 32 * quarter : 32 * quarter + 32, :],
                 in_=acc[:].rearrange("s (tb p u e) -> s tb u p e", tb=BLOCKS, u=2, e=2),
@@ -262,7 +262,7 @@ def tile_list_plate_proofing_kernel(
             words = z_t[b, g][:].rearrange("s tb u p e -> s (tb u p e)").bitcast(F32)
             grouped_words = z_bf[g][:].bitcast(F32)
             for half in range(2):
-                acc = turn_bank()
+                acc = next_bank()
                 for k in range(BLOCKS):
                     src = words[:, (BLOCKS * half + k) * P : (BLOCKS * half + k + 1) * P]
                     nc.tensor.transpose(acc[:, k * P : (k + 1) * P], src, ident[:])
@@ -281,22 +281,24 @@ def tile_list_plate_proofing_kernel(
             nc.vector.quantize_mx(codes[:].bitcast(FP8X4), plane[:], z_bf[g][:])
             z_q[b, g] = (codes, plane)
 
-        w3_bf = sb([P, 2 * N, PACK], BF16, "w3_bf")
-        w3_c = sb([P, 2 * N], U32, "w3_c")
-        w3_s = placed([P, 2 * N], U8, "w3_s", WGS_NEG_AT + GROUPS * BANK)
+        w3_raw = {}
+        w3_q = {}
 
-        def round_w3(b):
-            raw = sb([P, PACK, N], F32, f"w3_raw{b}", tag=f"v_w{b}")
-            nc.sync.dma_start(raw[:], w3[b * PASS : (b + 1) * PASS, :].rearrange("(p j) n -> p j n", j=PACK))
-            on_scalar = N // 2 if b else N
-            round_and_interleave(nc.scalar.copy, w3_bf[:, b * N : b * N + on_scalar, :], raw[:, :, :on_scalar])
-            if on_scalar < N:
-                round_and_interleave(nc.vector.tensor_copy, w3_bf[:, b * N + on_scalar :, :], raw[:, :, on_scalar:])
+        def load_w3(b):
+            w3_raw[b] = sb([P, PACK, N], F32, f"w3_raw{b}", tag=f"v_w{b}")
+            nc.sync.dma_start(w3_raw[b][:], w3[b * PASS : (b + 1) * PASS, :].rearrange("(p j) n -> p j n", j=PACK))
 
-        def quantise_w3():
-            flat = w3_bf[:].rearrange("p c j -> p (c j)")
-            for c0, c1 in ((0, BANK), (BANK, 2 * N)):
-                nc.vector.quantize_mx(w3_c[:, c0:c1].bitcast(FP8X4), w3_s[:, c0:c1], flat[:, PACK * c0 : PACK * c1])
+        def quantise_w3(n):
+            late = n == SCORE_TILES - 1
+            grouped = sb([P, 2 * P, PACK], BF16, f"w3_bf{n}", tag="w3_c0" if late else None)
+            for b in range(2):
+                round_and_interleave(
+                    nc.scalar.copy, grouped[:, b * P : (b + 1) * P, :], w3_raw[b][:, :, n * P : (n + 1) * P]
+                )
+            codes = sb([P, 2 * P], U32, f"w3_c{n}")
+            plane = placed([P, 2 * P], U8, f"w3_s{n}", WGS_NEG_AT + GROUPS * BANK + n * 2 * P)
+            nc.vector.quantize_mx(codes[:].bitcast(FP8X4), plane[:], grouped[:].rearrange("p c j -> p (c j)"))
+            w3_q[n] = (codes, plane)
 
         load_ref(0)
         for q in range(4):
@@ -319,30 +321,28 @@ def tile_list_plate_proofing_kernel(
             place(i)
             if i + 1 < ROW_TILES:
                 load_ref(i + 1)
-            ahead = i + AHEAD
-            for hh in range(2):
-                if ahead < ROW_TILES:
-                    respond(ahead, 2 * hh)
-                    respond(ahead, 2 * hh + 1)
-                    if hh:
-                        half_magnitude(ahead, 0)
-                deviation(i - 1, 2 * hh)
-                deviation(i - 1, 2 * hh + 1)
-            if ahead < ROW_TILES:
-                half_magnitude(ahead, 1)
-            if ahead in (last, last + 1):
+            ahead = min(i + AHEAD, last)
+            halves_now = [0, 1] if i + AHEAD < last else [i + AHEAD - last] if i < last else []
+            for hh in halves_now:
+                respond(ahead, 2 * hh)
+                respond(ahead, 2 * hh + 1)
+            for g in range(GROUPS):
+                deviation(i - 1, g)
+            for hh in halves_now:
+                half_magnitude(ahead, hh)
+            if i + AHEAD in (last, last + 1):
+                load_w3(i + AHEAD - last)
                 for hh in range(2):
-                    turn_back(0, 2 * (ahead - last) + hh, nc.scalar.copy)
-            if ahead > last:
-                round_w3(ahead - ROW_TILES)
+                    turn_back(0, 2 * (i + AHEAD - last) + hh, nc.scalar.copy)
+
+        opened = [next_bank() for g in range(GROUPS)]
         for g in range(GROUPS):
-            add_transposed(mx_banks[g], blocks_of(refs[last][:, g * BANK : (g + 1) * BANK]), closes=False)
-        late_ident = placed([P, P], F32, "late_ident", ROWS_AT[(last - 1) % RING])
-        nc.scalar.copy(out=late_ident[:], in_=ident[:])
+            add_transposed(opened[g], blocks_of(refs[last][:, g * BANK : (g + 1) * BANK]), closes=False)
         out_pages = [zeroed(nc.gpsimd, f"out_page{hh}", tag=f"v_s{hh}") for hh in range(2)]
         for g in range(GROUPS):
             quantise_z(0, g)
-        quantise_w3()
+        for n in range(SCORE_TILES - 1):
+            quantise_w3(n)
 
         sens_t = sb([P, SCORE_TILES, M], F32, "sens_t", tag="w2_w")
         nc.sync.dma_start(sens_t[:], sens.rearrange("(n p) m -> p n m", p=P))
@@ -352,25 +352,33 @@ def tile_list_plate_proofing_kernel(
         scores = [row_tile(ROW_TILES + n, f"score{n}") for n in range(SCORE_TILES)]
 
         def score(n, g):
+            acc = next_bank()
+            codes, plane = w3_q[n]
             for b in range(2):
-                cols = slice(b * N + n * P, b * N + (n + 1) * P)
+                cols = slice(b * P, (b + 1) * P)
                 nc.tensor.matmul_mx(
-                    out=mx_banks[g][:], lhsT=w3_c[:, cols].bitcast(FP8X4), lhsT_scale=w3_s[:, cols],
+                    out=acc[:], lhsT=codes[:, cols].bitcast(FP8X4), lhsT_scale=plane[:, cols],
                     rhs=z_q[b, g][0][:].bitcast(FP8X4), rhs_scale=z_q[b, g][1][:], start=(b == 0), stop=(b == 1),
                 )
             target = scores[n][:, g * BANK : (g + 1) * BANK]
             if (n, g) == (0, GROUPS - 1):
-                nc.vector.tensor_scalar_mul(target, mx_banks[g][:], -1.0)
+                nc.vector.tensor_scalar_mul(target, acc[:], -1.0)
             else:
-                nc.scalar.activation(target, mx_banks[g][:], ACT.Copy, scale=-1.0)
+                nc.scalar.activation(target, acc[:], ACT.Copy, scale=-1.0)
 
-        deviation(last, 0)
         for g in range(GROUPS):
-            if g + 1 < GROUPS:
-                deviation(last, g + 1)
-            turn_back(1, g, nc.vector.tensor_copy if 0 < g < GROUPS - 1 else nc.scalar.copy)
-            quantise_z(1, g)
-        for n in range(SCORE_TILES):
+            deviation(last, g, opened[g])
+        for g in range(GROUPS):
+            turn_back(1, g, nc.vector.tensor_copy if g < 2 else nc.scalar.copy)
+            if g:
+                quantise_z(1, g - 1)
+            if g == GROUPS - 2:
+                score(0, 0)
+        quantise_z(1, GROUPS - 1)
+        for g in range(1, GROUPS):
+            score(0, g)
+        quantise_w3(SCORE_TILES - 1)
+        for n in range(1, SCORE_TILES):
             for g in range(GROUPS):
                 score(n, g)
 

@@ -272,13 +272,18 @@ def tile_list_plate_proofing_kernel(
                     in_=acc[:].rearrange("p (tb u s) -> p tb s u", tb=2, u=2),
                 )
 
-        def quantise_z(b, g):
+        def quantise_z(b, g, pieces=1):
             codes = sb([P, BANK], U32, f"z_c{b}_{g}")
             if b:
                 plane = sb([P, BANK], U8, f"z_s{b}_{g}")
             else:
                 plane = placed([P, BANK], U8, f"z_s{b}_{g}", WGS_NEG_AT + g * BANK)
-            nc.vector.quantize_mx(codes[:].bitcast(FP8X4), plane[:], z_bf[g][:])
+            width = BANK // pieces
+            for c0 in range(0, BANK, width):
+                cols = slice(c0, c0 + width)
+                nc.vector.quantize_mx(
+                    codes[:, cols].bitcast(FP8X4), plane[:, cols], z_bf[g][:, PACK * c0 : PACK * (c0 + width)]
+                )
             z_q[b, g] = (codes, plane)
 
         w3_raw = {}
@@ -321,23 +326,27 @@ def tile_list_plate_proofing_kernel(
             place(i)
             if i + 1 < ROW_TILES:
                 load_ref(i + 1)
-            ahead = min(i + AHEAD, last)
-            halves_now = [0, 1] if i + AHEAD < last else [i + AHEAD - last] if i < last else []
-            for hh in halves_now:
-                respond(ahead, 2 * hh)
-                respond(ahead, 2 * hh + 1)
+            ahead = i + AHEAD
+            if ahead < ROW_TILES:
+                for q in range(4):
+                    respond(ahead, q)
             for g in range(GROUPS):
                 deviation(i - 1, g)
-            for hh in halves_now:
-                half_magnitude(ahead, hh)
-            if i + AHEAD in (last, last + 1):
-                load_w3(i + AHEAD - last)
+            if ahead < ROW_TILES:
                 for hh in range(2):
-                    turn_back(0, 2 * (i + AHEAD - last) + hh, nc.scalar.copy)
-
+                    half_magnitude(ahead, hh)
+            if ahead == last:
+                load_w3(0)
+                load_w3(1)
+            if ahead == ROW_TILES:
+                for g in range(GROUPS // 2):
+                    turn_back(0, g, nc.scalar.copy)
         opened = [next_bank() for g in range(GROUPS)]
         for g in range(GROUPS):
             add_transposed(opened[g], blocks_of(refs[last][:, g * BANK : (g + 1) * BANK]), closes=False)
+        for g in range(GROUPS // 2, GROUPS):
+            turn_back(0, g, nc.scalar.copy)
+        bank_uses.extend(opened)
         out_pages = [zeroed(nc.gpsimd, f"out_page{hh}", tag=f"v_s{hh}") for hh in range(2)]
         for g in range(GROUPS):
             quantise_z(0, g)
@@ -351,20 +360,21 @@ def tile_list_plate_proofing_kernel(
 
         scores = [row_tile(ROW_TILES + n, f"score{n}") for n in range(SCORE_TILES)]
 
-        def score(n, g):
+        def score(n, g, first=0, width=BANK, on_vector=False):
             acc = next_bank()
             codes, plane = w3_q[n]
             for b in range(2):
                 cols = slice(b * P, (b + 1) * P)
                 nc.tensor.matmul_mx(
-                    out=acc[:], lhsT=codes[:, cols].bitcast(FP8X4), lhsT_scale=plane[:, cols],
-                    rhs=z_q[b, g][0][:].bitcast(FP8X4), rhs_scale=z_q[b, g][1][:], start=(b == 0), stop=(b == 1),
+                    out=acc[:, :width], lhsT=codes[:, cols].bitcast(FP8X4), lhsT_scale=plane[:, cols],
+                    rhs=z_q[b, g][0][:, first : first + width].bitcast(FP8X4),
+                    rhs_scale=z_q[b, g][1][:, first : first + width], start=(b == 0), stop=(b == 1),
                 )
-            target = scores[n][:, g * BANK : (g + 1) * BANK]
-            if (n, g) == (0, GROUPS - 1):
-                nc.vector.tensor_scalar_mul(target, acc[:], -1.0)
+            target = scores[n][:, g * BANK + first : g * BANK + first + width]
+            if on_vector:
+                nc.vector.tensor_scalar_mul(target, acc[:, :width], -1.0)
             else:
-                nc.scalar.activation(target, acc[:], ACT.Copy, scale=-1.0)
+                nc.scalar.activation(target, acc[:, :width], ACT.Copy, scale=-1.0)
 
         for g in range(GROUPS):
             deviation(last, g, opened[g])
@@ -372,19 +382,27 @@ def tile_list_plate_proofing_kernel(
             turn_back(1, g, nc.vector.tensor_copy if g < 2 else nc.scalar.copy)
             if g:
                 quantise_z(1, g - 1)
-            if g == GROUPS - 2:
-                score(0, 0)
-        quantise_z(1, GROUPS - 1)
-        for g in range(1, GROUPS):
-            score(0, g)
+        quantise_z(1, GROUPS - 1, pieces=2)
+        for g in range(GROUPS - 1):
+            score(0, g, on_vector=(g == GROUPS - 2))
+        for first in (0, BANK // 2):
+            score(0, GROUPS - 1, first, BANK // 2)
         quantise_w3(SCORE_TILES - 1)
         for n in range(1, SCORE_TILES):
             for g in range(GROUPS):
                 score(n, g)
 
-        for n in range(SCORE_TILES):
-            picked = mags[n]
+        def pick(n, picked):
             nc.vector.tensor_tensor(picked[:], scores[n][:].indirect(list3[:]), sens_t[:, n, :], MULT)
-            page = out_pages[n % len(out_pages)]
+
+        def put(n, picked, page):
             nc.vector.tensor_tensor(page[:].indirect(list4[:]), picked[:], wgo_t[:], MULT)
             nc.sync.dma_start(out[n * P : (n + 1) * P, :], page[:])
+
+        pick(0, mags[0])
+        put(0, mags[0], out_pages[0])
+        pick(2, mags[2])
+        picked = placed([P, M], F32, "picked1", ROWS_AT[(ROW_TILES + 2) % RING])
+        pick(1, picked)
+        put(2, mags[2], out_pages[1])
+        put(1, picked, out_pages[0])

@@ -34,6 +34,7 @@ RING = 3
 AHEAD = 2
 
 KIB = 1024
+W3_RAW_AT = 17 * KIB + 512
 TABLE_WORDS_AT = 0
 TABLE_SCALES_AT = 24 * KIB
 WGS_AT = 27 * KIB
@@ -171,6 +172,8 @@ def tile_list_plate_proofing_kernel(
         early_squares = {
             (1, 0): sb([P, BANK], F32, "early_square1", tag="page2"),
             (2, 0): sb([P, BANK], F32, "early_square2", tag="early_square"),
+            (5, 0): sb([P, BANK], F32, "early_square5"),
+            (6, 0): sb([P, BANK], F32, "early_square6"),
         }
 
         def square_tile(i, q):
@@ -289,17 +292,26 @@ def tile_list_plate_proofing_kernel(
         w3_raw = {}
         w3_q = {}
 
-        def load_w3(b):
-            w3_raw[b] = sb([P, PACK, N], F32, f"w3_raw{b}", tag=f"v_w{b}")
-            nc.sync.dma_start(w3_raw[b][:], w3[b * PASS : (b + 1) * PASS, :].rearrange("(p j) n -> p j n", j=PACK))
+        def load_w3(b, late):
+            rows = w3[b * PASS : (b + 1) * PASS, :].rearrange("(p j) n -> p j n", j=PACK)
+            if late:
+                w3_raw[b, late] = sb([P, PACK, P], F32, f"w3_late{b}", tag=f"v_w{b}")
+                nc.sync.dma_start(w3_raw[b, late][:], rows[:, :, 2 * P :])
+            else:
+                w3_raw[b, late] = placed([P, PACK, 2 * P], F32, f"w3_raw{b}", W3_RAW_AT + b * 4 * KIB)
+                nc.sync.dma_start(w3_raw[b, late][:], rows[:, :, : 2 * P])
+
+        w3_bf = {}
+
+        def round_w3(n, tag):
+            late = n == SCORE_TILES - 1
+            w3_bf[n] = sb([P, 2 * P, PACK], BF16, f"w3_bf{n}", tag=tag)
+            for b in range(2):
+                raw = w3_raw[b, late][:] if late else w3_raw[b, late][:, :, n * P : (n + 1) * P]
+                round_and_interleave(nc.scalar.copy, w3_bf[n][:, b * P : (b + 1) * P, :], raw)
 
         def quantise_w3(n):
-            late = n == SCORE_TILES - 1
-            grouped = sb([P, 2 * P, PACK], BF16, f"w3_bf{n}", tag="w3_c0" if late else None)
-            for b in range(2):
-                round_and_interleave(
-                    nc.scalar.copy, grouped[:, b * P : (b + 1) * P, :], w3_raw[b][:, :, n * P : (n + 1) * P]
-                )
+            grouped = w3_bf[n]
             codes = sb([P, 2 * P], U32, f"w3_c{n}")
             plane = placed([P, 2 * P], U8, f"w3_s{n}", WGS_NEG_AT + GROUPS * BANK + n * 2 * P)
             nc.vector.quantize_mx(codes[:].bitcast(FP8X4), plane[:], grouped[:].rearrange("p c j -> p (c j)"))
@@ -322,6 +334,8 @@ def tile_list_plate_proofing_kernel(
                 half_magnitude(i, hh)
         quantise_w1(3, nc.scalar.copy)
         pages.append(zeroed(nc.gpsimd, "page2"))
+        load_w3(0, False)
+        load_w3(1, False)
         for i in range(1, ROW_TILES):
             place(i)
             if i + 1 < ROW_TILES:
@@ -335,9 +349,11 @@ def tile_list_plate_proofing_kernel(
             if ahead < ROW_TILES:
                 for hh in range(2):
                     half_magnitude(ahead, hh)
+            if ahead in (5, 6):
+                round_w3(ahead - 5, f"early_square{ahead}")
             if ahead == last:
-                load_w3(0)
-                load_w3(1)
+                load_w3(0, True)
+                load_w3(1, True)
             if ahead == ROW_TILES:
                 for g in range(GROUPS // 2):
                     turn_back(0, g, nc.scalar.copy)
@@ -387,6 +403,7 @@ def tile_list_plate_proofing_kernel(
             score(0, g, on_vector=(g == GROUPS - 2))
         for first in (0, BANK // 2):
             score(0, GROUPS - 1, first, BANK // 2)
+        round_w3(SCORE_TILES - 1, "w3_c0")
         quantise_w3(SCORE_TILES - 1)
         for n in range(1, SCORE_TILES):
             for g in range(GROUPS):

@@ -75,8 +75,8 @@ def tile_list_plate_proofing_kernel(
             return tile
 
         def load_scale_rows(queue, plane, rows):
-            for q in range(4):
-                queue.dma_start(plane[32 * q : 32 * q + 4, :].bitcast(I32), rows[4 * q : 4 * q + 4, :].bitcast(I32))
+            for r in range(4):
+                queue.dma_start(plane[r:P:32, :].bitcast(I32), rows[r:16:4, :].bitcast(I32))
 
         def round_and_interleave(copy, grouped, raw):
             copy(

@@ -166,11 +166,11 @@ def tile_list_plate_proofing_kernel(
             nc.sync.dma_start(refs[i][:], ref[i * P : (i + 1) * P, :])
 
         mags = [sb([P, S], F32, f"mag{k}") for k in range(RING)]
-        first_mags = [sb([P, QUARTER], F32, f"first_mag{q}") for q in range(4)]
+        first_mags = [sb([P, QUARTER], F32, f"first_mag{q}") for q in range(3)]
+        first_mags.append(sb([P, QUARTER], F32, "first_mag3", tag="page2"))
         squares = [sb([P, BANK], F32, f"square{q}") for q in range(4)]
 
         early_squares = {
-            (1, 0): sb([P, BANK], F32, "early_square1", tag="page2"),
             (2, 0): sb([P, BANK], F32, "early_square2", tag="early_square"),
             (5, 0): sb([P, BANK], F32, "early_square5"),
             (6, 0): sb([P, BANK], F32, "early_square6"),

@@ -29,19 +29,20 @@ TILES_PER_PASS = PASS // P
 GROUPS = T2 // BANK
 SCORE_TILES = N // P
 QUARTER = 2 * P
-W1_RUNS = ((0, 1), (1, 2), (2, 4), (4, ROW_TILES))
+W1_RUNS = ((0, 1), (1, 2), (2, 3), (3, 5), (5, ROW_TILES))
 RING = 3
-AHEAD = 2
 
 KIB = 1024
 W3_RAW_AT = 17 * KIB + 512
 TABLE_WORDS_AT = 0
 TABLE_SCALES_AT = 24 * KIB
-WGS_AT = 27 * KIB
-W1_RAW_AT = (44 * KIB, 25 * KIB, 21 * KIB, 8 * KIB)
-W1_BF_AT = (46 * KIB, 47 * KIB, 32 * KIB)
+WGS_AT = 28 * KIB
+W1_RAW_AT = (44 * KIB, 20 * KIB, 22 * KIB, 8 * KIB, 12 * KIB)
 WGS_NEG_AT = 40 * KIB
-ROWS_AT = (TABLE_WORDS_AT, 32 * KIB, W1_RAW_AT[3])
+ROWS_AT = (TABLE_WORDS_AT, 32 * KIB, 48 * KIB)
+ROUNDED_ON = {1: (0, 0), 2: (0, 2), 3: (2, 0), 4: (4, 0)}
+FIRST_SUM_AT = ROWS_AT[1] + 3 * KIB // 2
+SQUARE_AT = {(0, 0): WGS_NEG_AT + 3 * KIB, (0, 2): ROWS_AT[1], (0, 3): ROWS_AT[1] + 2 * KIB, (2, 0): ROWS_AT[2], (4, 0): 56 * KIB}
 
 
 def tile_list_plate_proofing_kernel(
@@ -109,30 +110,38 @@ def tile_list_plate_proofing_kernel(
         load_scale_rows(nc.sync, tab_s, tab_scales[0])
         tab_w = placed([P, T], U32, "tab_w", TABLE_WORDS_AT)
         nc.sync.dma_start(tab_w[:].bitcast(I32), tab_words[0].rearrange("p t i -> p (t i)").bitcast(I32))
+        load_scale_rows(nc.sync, w2_s, w2_scales[0])
         w2_w = sb([P, 2 * H], U8, "w2_w")
         nc.sync.dma_start(w2_w[:].bitcast(I32), w2_words[0].bitcast(I32))
+        wgs_raw = placed([P, S], F32, "wgs_raw", WGS_AT)
+        nc.sync.dma_start(wgs_raw[:], wgs)
+        load_w1(1)
+        load_w1(2)
         list3 = load_list(offs3, "list3")
         list4 = load_list(offs4, "list4")
 
         ident = sb([P, P], F32, "ident")
         make_identity(nc, ident[:])
-        load_scale_rows(nc.gpsimd, w2_s, w2_scales[0])
         pages = [zeroed(nc.vector, "page0"), zeroed(nc.vector, "page1")]
 
         halves = [list1[:, hh * HALF_LIST : (hh + 1) * HALF_LIST] for hh in range(2)]
         v_s = [sb([P, BANK], U8, f"v_s{hh}") for hh in range(2)]
-        v_w = [sb([P, BANK], U32, f"v_w{hh}") for hh in range(2)]
+        v_w = [sb([P, QUARTER], U32, "v_w0"), sb([P, QUARTER], U32, "v_w1"), sb([P, BANK], U32, "v_w2")]
+
+        def picked_words(q):
+            return v_w[q][:] if q < 2 else v_w[2][:, (q - 2) * QUARTER : (q - 1) * QUARTER]
 
         w1_q = {}
 
-        def quantise_w1(c, copy):
+        def quantise_w1(c):
             first, end = W1_RUNS[c]
             width = (end - first) * P
-            if c < len(W1_BF_AT):
-                grouped = placed([P, width, PACK], BF16, f"w1_bf{c}", W1_BF_AT[c])
+            if c:
+                at = SQUARE_AT[ROUNDED_ON[c]] + (KIB if c == 1 else 0)
+                grouped = placed([P, width, PACK], BF16, f"w1_bf{c}", at)
             else:
-                grouped = sb([P, width, PACK], BF16, f"w1_bf{c}", tag="early_square")
-            round_and_interleave(copy, grouped[:], w1_raw[c][:])
+                grouped = sb([P, width, PACK], BF16, f"w1_bf{c}")
+            round_and_interleave(nc.scalar.copy, grouped[:], w1_raw[c][:])
             codes = sb([P, width], U32, f"w1_c{c}")
             plane = sb([P, width], U8, f"w1_s{c}")
             flat = grouped[:].rearrange("p c j -> p (c j)")
@@ -143,20 +152,16 @@ def tile_list_plate_proofing_kernel(
                 cols = slice(k * P, (k + 1) * P)
                 w1_q[first + k] = (codes[:, cols], plane[:, cols])
 
-        quantise_w1(0, nc.scalar.copy)
+        quantise_w1(0)
         for hh in range(2):
             nc.vector.tensor_copy(v_s[hh][:], tab_s[:].indirect(halves[hh]))
-        wgs_raw = placed([P, S], F32, "wgs_raw", WGS_AT)
-        nc.sync.dma_start(wgs_raw[:], wgs)
-        load_w1(1)
-        load_w1(2)
-        for hh in range(2):
-            nc.vector.tensor_copy(v_w[hh][:], tab_w[:].indirect(halves[hh]))
+        columns = QUARTER // 16
+        for q in range(2):
+            nc.vector.tensor_copy(v_w[q][:], tab_w[:].indirect(list1[:, q * columns : (q + 1) * columns]))
+        nc.vector.tensor_copy(v_w[2][:], tab_w[:].indirect(halves[1]))
         load_w1(3)
-        wgs_neg = placed([P, S], F32, "wgs_neg", WGS_NEG_AT)
-        nc.vector.tensor_scalar_mul(wgs_neg[:], wgs_raw[:], -1.0)
-        quantise_w1(1, nc.vector.tensor_copy)
-        quantise_w1(2, nc.vector.tensor_copy)
+        first_neg = sb([P, QUARTER], F32, "first_neg")
+        nc.vector.tensor_scalar_mul(first_neg[:], wgs_raw[:, :QUARTER], -1.0)
 
         refs = {}
         last = ROW_TILES - 1
@@ -170,11 +175,8 @@ def tile_list_plate_proofing_kernel(
         first_mags.append(sb([P, QUARTER], F32, "first_mag3", tag="page2"))
         squares = [sb([P, BANK], F32, f"square{q}") for q in range(4)]
 
-        early_squares = {
-            (2, 0): sb([P, BANK], F32, "early_square2", tag="early_square"),
-            (5, 0): sb([P, BANK], F32, "early_square5"),
-            (6, 0): sb([P, BANK], F32, "early_square6"),
-        }
+        early_squares = {key: placed([P, BANK], F32, f"early_square{key[0]}_{key[1]}", at) for key, at in SQUARE_AT.items()}
+        early_squares[last, 0] = sb([P, BANK], F32, "last_square")
 
         def square_tile(i, q):
             return early_squares.get((i, q), squares[q])
@@ -189,9 +191,10 @@ def tile_list_plate_proofing_kernel(
             for which, (rhs, rhs_scale) in enumerate(operands):
                 for jj in range(2):
                     entries = slice((2 * (q % 2) + jj) * P, (2 * (q % 2) + jj + 1) * P)
+                    words = picked_words(q)[:, jj * P : (jj + 1) * P]
                     nc.tensor.matmul_mx(
                         out=acc[:, (2 * which + jj) * P : (2 * which + jj + 1) * P],
-                        lhsT=v_w[hh][:, entries].bitcast(FP8X4), lhsT_scale=v_s[hh][:, entries],
+                        lhsT=words.bitcast(FP8X4), lhsT_scale=v_s[hh][:, entries],
                         rhs=rhs, rhs_scale=rhs_scale, start=True, stop=True,
                     )
             nc.scalar.activation(square_tile(i, q)[:], acc[:], ACT.Square)
@@ -218,40 +221,39 @@ def tile_list_plate_proofing_kernel(
         def half_magnitude(i, hh):
             magnitude(i, mags[i % RING][:, hh * BANK : (hh + 1) * BANK], (2 * hh, 2 * hh + 1))
 
+        first_sum = placed([P, QUARTER], F32, "first_sum", FIRST_SUM_AT)
+
         def first_magnitude():
-            acc, square, mag = next_bank(), squares[0], first_mags[0]
+            acc, square = next_bank(), square_tile(0, 0)
             weights = ((w1_q[0][0].bitcast(FP8X4), w1_q[0][1]), (w2_w[:, : 2 * P].bitcast(FP4X4), w2_s[:, :P]))
             for which, (lhsT, lhsT_scale) in enumerate(weights):
                 nc.tensor.matmul_mx(
                     out=acc[:, which * QUARTER : (which + 1) * QUARTER], lhsT=lhsT, lhsT_scale=lhsT_scale,
-                    rhs=v_w[0][:, :QUARTER].bitcast(FP8X4), rhs_scale=v_s[0][:, :QUARTER], start=True, stop=True,
+                    rhs=v_w[0][:].bitcast(FP8X4), rhs_scale=v_s[0][:, :QUARTER], start=True, stop=True,
                 )
             nc.scalar.activation(square[:], acc[:], ACT.Square)
-            nc.vector.tensor_tensor(mag[:], square[:, :QUARTER], square[:, QUARTER:], ADD)
-            nc.scalar.activation(mag[:], mag[:], ACT.Sqrt)
+            nc.vector.tensor_tensor(first_sum[:], square[:, :QUARTER], square[:, QUARTER:], ADD)
 
         def place(i):
             nc.vector.tensor_tensor(pages[i % RING][:].indirect(list2[:]), mags[i % RING][:], wgs_neg[:], MULT)
 
         def place_first(q):
-            columns = QUARTER // 16
             nc.vector.tensor_tensor(
                 pages[0][:].indirect(list2[:, q * columns : (q + 1) * columns]), first_mags[q][:],
-                wgs_neg[:, q * QUARTER : (q + 1) * QUARTER], MULT,
+                wgs_neg[:, q * QUARTER : (q + 1) * QUARTER] if q else first_neg[:], MULT,
             )
 
         z_t = {}
 
-        def deviation(i, g, opened=None):
+        def deviation(i, g, acc=None):
             b, quarter = divmod(i, TILES_PER_PASS)
             if quarter == 0:
                 z_t[b, g] = sb([P, BLOCKS, 2, P, 2], BF16, f"z_t{b}_{g}")
             cols = slice(g * BANK, (g + 1) * BANK)
-            if opened is None:
+            if acc is None:
                 acc = next_bank()
                 add_transposed(acc, blocks_of(refs[i][:, cols]) + blocks_of(pages[i % RING][:, cols]))
             else:
-                acc = opened
                 add_transposed(acc, blocks_of(pages[i % RING][:, cols]), opens=False)
             nc.scalar.copy(
                 out=z_t[b, g][:, :, :, 32 * quarter : 32 * quarter + 32, :],
@@ -261,11 +263,10 @@ def tile_list_plate_proofing_kernel(
         z_q = {}
         z_bf = [sb([P, BANK * PACK], BF16, f"z_bf{g}") for g in range(GROUPS)]
 
-        def turn_back(b, g, second_copy):
+        def turn_back(b, g, second_copy, pair):
             words = z_t[b, g][:].rearrange("s tb u p e -> s (tb u p e)").bitcast(F32)
             grouped_words = z_bf[g][:].bitcast(F32)
-            for half in range(2):
-                acc = next_bank()
+            for half, acc in enumerate(pair):
                 for k in range(BLOCKS):
                     src = words[:, (BLOCKS * half + k) * P : (BLOCKS * half + k + 1) * P]
                     nc.tensor.transpose(acc[:, k * P : (k + 1) * P], src, ident[:])
@@ -276,7 +277,7 @@ def tile_list_plate_proofing_kernel(
                 )
 
         def quantise_z(b, g, pieces=1):
-            codes = sb([P, BANK], U32, f"z_c{b}_{g}")
+            codes = sb([P, BANK], U32, f"z_c{b}_{g}", tag=f"z_t{b}_{g}")
             if b:
                 plane = sb([P, BANK], U8, f"z_s{b}_{g}")
             else:
@@ -295,7 +296,7 @@ def tile_list_plate_proofing_kernel(
         def load_w3(b, late):
             rows = w3[b * PASS : (b + 1) * PASS, :].rearrange("(p j) n -> p j n", j=PACK)
             if late:
-                w3_raw[b, late] = sb([P, PACK, P], F32, f"w3_late{b}", tag=f"v_w{b}")
+                w3_raw[b, late] = sb([P, PACK, P], F32, f"w3_late{b}", tag=f"v_w{2 * b}")
                 nc.sync.dma_start(w3_raw[b, late][:], rows[:, :, 2 * P :])
             else:
                 w3_raw[b, late] = placed([P, PACK, 2 * P], F32, f"w3_raw{b}", W3_RAW_AT + b * 4 * KIB)
@@ -303,12 +304,12 @@ def tile_list_plate_proofing_kernel(
 
         w3_bf = {}
 
-        def round_w3(n, tag):
+        def round_w3(n, tag, copy):
             late = n == SCORE_TILES - 1
             w3_bf[n] = sb([P, 2 * P, PACK], BF16, f"w3_bf{n}", tag=tag)
             for b in range(2):
                 raw = w3_raw[b, late][:] if late else w3_raw[b, late][:, :, n * P : (n + 1) * P]
-                round_and_interleave(nc.scalar.copy, w3_bf[n][:, b * P : (b + 1) * P, :], raw)
+                round_and_interleave(copy, w3_bf[n][:, b * P : (b + 1) * P, :], raw)
 
         def quantise_w3(n):
             grouped = w3_bf[n]
@@ -318,84 +319,120 @@ def tile_list_plate_proofing_kernel(
             w3_q[n] = (codes, plane)
 
         load_ref(0)
-        for q in range(4):
-            if q:
-                respond(0, q)
-                magnitude(0, first_mags[q][:], (q,))
-            else:
-                first_magnitude()
-            place_first(q)
+        load_w1(4)
+        first_magnitude()
+        respond(0, 1)
+        nc.scalar.activation(first_mags[0][:], first_sum[:], ACT.Sqrt)
+        wgs_neg = placed([P, S], F32, "wgs_neg", WGS_NEG_AT)
+        nc.vector.tensor_scalar_mul(wgs_neg[:], wgs_raw[:], -1.0)
+        place_first(0)
+        quantise_w1(1)
+        magnitude(0, first_mags[1][:], (1,))
+        place_first(1)
+        respond(0, 2)
+        respond(0, 3)
+        magnitude(0, first_mags[2][:], (2,))
+        place_first(2)
+        quantise_w1(2)
+        magnitude(0, first_mags[3][:], (3,))
+        place_first(3)
         load_ref(1)
-        for i in range(1, 1 + AHEAD):
-            for hh in range(2):
-                respond(i, 2 * hh)
-                respond(i, 2 * hh + 1)
-            for hh in range(2):
-                half_magnitude(i, hh)
-        quantise_w1(3, nc.scalar.copy)
+
+        def magnitudes(i):
+            for q in range(4):
+                respond(i, q)
+            half_magnitude(i, 0)
+            for c, (tile, q) in ROUNDED_ON.items():
+                if tile == i:
+                    quantise_w1(c)
+            half_magnitude(i, 1)
+
+        magnitudes(1)
         pages.append(zeroed(nc.gpsimd, "page2"))
         load_w3(0, False)
         load_w3(1, False)
-        for i in range(1, ROW_TILES):
-            place(i)
-            if i + 1 < ROW_TILES:
-                load_ref(i + 1)
-            ahead = i + AHEAD
-            if ahead < ROW_TILES:
-                for q in range(4):
-                    respond(ahead, q)
+
+        def deviations(i):
             for g in range(GROUPS):
-                deviation(i - 1, g)
-            if ahead < ROW_TILES:
-                for hh in range(2):
-                    half_magnitude(ahead, hh)
-            if ahead in (5, 6):
-                round_w3(ahead - 5, f"early_square{ahead}")
-            if ahead == last:
-                load_w3(0, True)
-                load_w3(1, True)
-            if ahead == ROW_TILES:
-                for g in range(GROUPS // 2):
-                    turn_back(0, g, nc.scalar.copy)
+                deviation(i, g)
+
+        def pass_over(count):
+            bank_uses.extend([None] * count)
+
+        place(1)
+        pass_over(len(banks) - 2)
+        magnitudes(2)
+        load_ref(2)
+        pass_over(2)
+        deviations(0)
+        load_ref(3)
+        magnitudes(3)
+        place(2)
+        magnitudes(4)
+        place(3)
+        deviations(1)
+        load_ref(4)
+        deviations(2)
+        load_ref(5)
+        place(4)
+        magnitudes(5)
+        place(5)
+        magnitudes(6)
+        deviations(3)
+        load_ref(6)
+        place(6)
+        magnitudes(last)
+        load_w3(0, True)
+        load_w3(1, True)
+        deviations(4)
+        load_ref(last)
+        place(last)
+        for g in range(GROUPS):
+            turn_back(0, g, nc.scalar.copy, (next_bank(), next_bank()))
+        deviations(5)
+        round_w3(0, "last_square", nc.scalar.copy)
+        deviations(last - 1)
         opened = [next_bank() for g in range(GROUPS)]
         for g in range(GROUPS):
             add_transposed(opened[g], blocks_of(refs[last][:, g * BANK : (g + 1) * BANK]), closes=False)
-        for g in range(GROUPS // 2, GROUPS):
-            turn_back(0, g, nc.scalar.copy)
-        bank_uses.extend(opened)
         out_pages = [zeroed(nc.gpsimd, f"out_page{hh}", tag=f"v_s{hh}") for hh in range(2)]
         for g in range(GROUPS):
             quantise_z(0, g)
-        for n in range(SCORE_TILES - 1):
-            quantise_w3(n)
+        quantise_w3(0)
 
         sens_t = sb([P, SCORE_TILES, M], F32, "sens_t", tag="w2_w")
         nc.sync.dma_start(sens_t[:], sens.rearrange("(n p) m -> p n m", p=P))
-        wgo_t = sb([P, M], F32, "wgo_t", tag="w1_c3")
+        wgo_t = sb([P, M], F32, "wgo_t", tag=f"w1_c{len(W1_RUNS) - 1}")
         nc.sync.dma_start(wgo_t[:], wgo)
 
         scores = [row_tile(ROW_TILES + n, f"score{n}") for n in range(SCORE_TILES)]
 
-        def score(n, g, first=0, width=BANK, on_vector=False):
-            acc = next_bank()
+        def multiply(acc, n, g, b, first=0, width=BANK):
             codes, plane = w3_q[n]
-            for b in range(2):
-                cols = slice(b * P, (b + 1) * P)
-                nc.tensor.matmul_mx(
-                    out=acc[:, :width], lhsT=codes[:, cols].bitcast(FP8X4), lhsT_scale=plane[:, cols],
-                    rhs=z_q[b, g][0][:, first : first + width].bitcast(FP8X4),
-                    rhs_scale=z_q[b, g][1][:, first : first + width], start=(b == 0), stop=(b == 1),
-                )
+            cols = slice(b * P, (b + 1) * P)
+            nc.tensor.matmul_mx(
+                out=acc[:, :width], lhsT=codes[:, cols].bitcast(FP8X4), lhsT_scale=plane[:, cols],
+                rhs=z_q[b, g][0][:, first : first + width].bitcast(FP8X4),
+                rhs_scale=z_q[b, g][1][:, first : first + width], start=(b == 0), stop=(b == 1),
+            )
+
+        def empty(acc, n, g, first=0, width=BANK, on_vector=False):
             target = scores[n][:, g * BANK + first : g * BANK + first + width]
             if on_vector:
                 nc.vector.tensor_scalar_mul(target, acc[:, :width], -1.0)
             else:
                 nc.scalar.activation(target, acc[:, :width], ACT.Copy, scale=-1.0)
 
+        def score(n, g, first=0, width=BANK, on_vector=False):
+            acc = next_bank()
+            for b in range(2):
+                multiply(acc, n, g, b, first, width)
+            empty(acc, n, g, first, width, on_vector)
+
         for g in range(GROUPS):
             deviation(last, g, opened[g])
         for g in range(GROUPS):
-            turn_back(1, g, nc.vector.tensor_copy if g < 2 else nc.scalar.copy)
+            turn_back(1, g, nc.vector.tensor_copy if g < 2 else nc.scalar.copy, (next_bank(), next_bank()))
             if g:
                 quantise_z(1, g - 1)
         quantise_z(1, GROUPS - 1, pieces=2)
@@ -403,7 +440,9 @@ def tile_list_plate_proofing_kernel(
             score(0, g, on_vector=(g == GROUPS - 2))
         for first in (0, BANK // 2):
             score(0, GROUPS - 1, first, BANK // 2)
-        round_w3(SCORE_TILES - 1, "w3_c0")
+        round_w3(1, f"z_bf{GROUPS - 1}", nc.vector.tensor_copy)
+        quantise_w3(1)
+        round_w3(SCORE_TILES - 1, "w3_c0", nc.scalar.copy)
         quantise_w3(SCORE_TILES - 1)
         for n in range(1, SCORE_TILES):
             for g in range(GROUPS):

@@ -104,17 +104,21 @@ def tile_list_plate_proofing_kernel(
         warm = sb([P, 2], F32, "warm")
         nc.vector.memset(warm[:, 0:1], 1.0)
         nc.scalar.activation(warm[:, 1:2], warm[:, 0:1], ACT.Sqrt)
+        w2_rows = sb([4, 4, H], U8, "w2_rows")
+        nc.scalar.dma_start(
+            w2_rows[:].rearrange("r q c -> r (q c)").bitcast(I32).rearrange("r (q c) -> r q c", q=4),
+            w2_scales[0].bitcast(I32).rearrange("(q r) c -> r q c", r=4),
+        )
         list1 = load_list(offs, "list1")
-        list2 = load_list(offs2, "list2")
         load_w1(0)
         load_scale_rows(nc.sync, tab_s, tab_scales[0])
         tab_w = placed([P, T], U32, "tab_w", TABLE_WORDS_AT)
         nc.sync.dma_start(tab_w[:].bitcast(I32), tab_words[0].rearrange("p t i -> p (t i)").bitcast(I32))
-        load_scale_rows(nc.sync, w2_s, w2_scales[0])
         w2_w = sb([P, 2 * H], U8, "w2_w")
         nc.sync.dma_start(w2_w[:].bitcast(I32), w2_words[0].bitcast(I32))
         wgs_raw = placed([P, S], F32, "wgs_raw", WGS_AT)
         nc.sync.dma_start(wgs_raw[:], wgs)
+        list2 = load_list(offs2, "list2")
         load_w1(1)
         load_w1(2)
         list3 = load_list(offs3, "list3")
@@ -122,6 +126,8 @@ def tile_list_plate_proofing_kernel(
 
         ident = sb([P, P], F32, "ident")
         make_identity(nc, ident[:])
+        for q in range(4):
+            nc.vector.tensor_copy(w2_s[32 * q : 32 * q + 4, :].bitcast(I32), w2_rows[:, q, :].bitcast(I32))
         pages = [zeroed(nc.vector, "page0"), zeroed(nc.vector, "page1")]
 
         halves = [list1[:, hh * HALF_LIST : (hh + 1) * HALF_LIST] for hh in range(2)]
@@ -338,8 +344,13 @@ def tile_list_plate_proofing_kernel(
         place_first(3)
         load_ref(1)
 
-        def magnitudes(i):
+        def pass_over(count):
+            bank_uses.extend([None] * count)
+
+        def magnitudes(i, back=0):
             for q in range(4):
+                if back and q % 2 == 0:
+                    pass_over(len(banks) - back)
                 respond(i, q)
             half_magnitude(i, 0)
             for c, (tile, q) in ROUNDED_ON.items():
@@ -356,14 +367,10 @@ def tile_list_plate_proofing_kernel(
             for g in range(GROUPS):
                 deviation(i, g)
 
-        def pass_over(count):
-            bank_uses.extend([None] * count)
-
         place(1)
-        pass_over(len(banks) - 2)
-        magnitudes(2)
+        magnitudes(2, back=2)
         load_ref(2)
-        pass_over(2)
+        pass_over(len(banks) - 4)
         deviations(0)
         load_ref(3)
         magnitudes(3)

@@ -29,20 +29,25 @@ TILES_PER_PASS = PASS // P
 GROUPS = T2 // BANK
 SCORE_TILES = N // P
 QUARTER = 2 * P
-W1_RUNS = ((0, 1), (1, 2), (2, 3), (3, 5), (5, ROW_TILES))
+W1_RUNS = ((0, 1), (1, 2), (2, 4), (4, 6), (6, ROW_TILES))
 RING = 3
+AHEAD = 2
 
 KIB = 1024
-W3_RAW_AT = 17 * KIB + 512
 TABLE_WORDS_AT = 0
 TABLE_SCALES_AT = 24 * KIB
 WGS_AT = 28 * KIB
-W1_RAW_AT = (44 * KIB, 20 * KIB, 22 * KIB, 8 * KIB, 12 * KIB)
+W1_RAW_AT = (44 * KIB, 16 * KIB, 18 * KIB, 8 * KIB, 12 * KIB)
+W3_RAW_AT = (W1_RAW_AT[2], W1_RAW_AT[4])
 WGS_NEG_AT = 40 * KIB
 ROWS_AT = (TABLE_WORDS_AT, 32 * KIB, 48 * KIB)
-ROUNDED_ON = {1: (0, 0), 2: (0, 2), 3: (2, 0), 4: (4, 0)}
 FIRST_SUM_AT = ROWS_AT[1] + 3 * KIB // 2
-SQUARE_AT = {(0, 0): WGS_NEG_AT + 3 * KIB, (0, 2): ROWS_AT[1], (0, 3): ROWS_AT[1] + 2 * KIB, (2, 0): ROWS_AT[2], (4, 0): 56 * KIB}
+SQUARE_AT = {(0, 0): 46 * KIB, (0, 2): ROWS_AT[1], (0, 3): ROWS_AT[1] + 2 * KIB, (2, 0): ROWS_AT[2], (3, 0): 56 * KIB}
+PAGE2_AT = 60 * KIB
+FIRST_MAG_AT = (58 * KIB, SQUARE_AT[0, 0] + KIB, 68 * KIB, PAGE2_AT + KIB)
+W1_BF_AT = (None, SQUARE_AT[0, 0], FIRST_MAG_AT[0] + KIB // 2, SQUARE_AT[2, 0], SQUARE_AT[3, 0])
+W1_CODES_AT = (None, FIRST_MAG_AT[0], FIRST_MAG_AT[1], None, None)
+ROUNDED_IN = {2: 3, 3: 4}
 
 
 def tile_list_plate_proofing_kernel(
@@ -115,11 +120,12 @@ def tile_list_plate_proofing_kernel(
         tab_w = placed([P, T], U32, "tab_w", TABLE_WORDS_AT)
         nc.sync.dma_start(tab_w[:].bitcast(I32), tab_words[0].rearrange("p t i -> p (t i)").bitcast(I32))
         w2_w = sb([P, 2 * H], U8, "w2_w")
-        nc.sync.dma_start(w2_w[:].bitcast(I32), w2_words[0].bitcast(I32))
+        nc.sync.dma_start(w2_w[:, : 2 * P].bitcast(I32), w2_words[0][:, : 2 * P].bitcast(I32))
         wgs_raw = placed([P, S], F32, "wgs_raw", WGS_AT)
         nc.sync.dma_start(wgs_raw[:], wgs)
-        list2 = load_list(offs2, "list2")
         load_w1(1)
+        list2 = load_list(offs2, "list2")
+        nc.sync.dma_start(w2_w[:, 2 * P :].bitcast(I32), w2_words[0][:, 2 * P :].bitcast(I32))
         load_w1(2)
         list3 = load_list(offs3, "list3")
         list4 = load_list(offs4, "list4")
@@ -139,18 +145,23 @@ def tile_list_plate_proofing_kernel(
 
         w1_q = {}
 
+        w1_bf = {}
+
+        def round_w1(c, copy):
+            first, end = W1_RUNS[c]
+            shape = [P, (end - first) * P, PACK]
+            w1_bf[c] = placed(shape, BF16, f"w1_bf{c}", W1_BF_AT[c]) if c else sb(shape, BF16, f"w1_bf{c}")
+            round_and_interleave(copy, w1_bf[c][:], w1_raw[c][:])
+
         def quantise_w1(c):
             first, end = W1_RUNS[c]
             width = (end - first) * P
-            if c:
-                at = SQUARE_AT[ROUNDED_ON[c]] + (KIB if c == 1 else 0)
-                grouped = placed([P, width, PACK], BF16, f"w1_bf{c}", at)
+            if W1_CODES_AT[c] is None:
+                codes = sb([P, width], U32, f"w1_c{c}")
             else:
-                grouped = sb([P, width, PACK], BF16, f"w1_bf{c}")
-            round_and_interleave(nc.scalar.copy, grouped[:], w1_raw[c][:])
-            codes = sb([P, width], U32, f"w1_c{c}")
+                codes = placed([P, width], U32, f"w1_c{c}", W1_CODES_AT[c])
             plane = sb([P, width], U8, f"w1_s{c}")
-            flat = grouped[:].rearrange("p c j -> p (c j)")
+            flat = w1_bf[c][:].rearrange("p c j -> p (c j)")
             for c0 in range(0, width, BANK):
                 c1 = min(c0 + BANK, width)
                 nc.vector.quantize_mx(codes[:, c0:c1].bitcast(FP8X4), plane[:, c0:c1], flat[:, PACK * c0 : PACK * c1])
@@ -158,6 +169,7 @@ def tile_list_plate_proofing_kernel(
                 cols = slice(k * P, (k + 1) * P)
                 w1_q[first + k] = (codes[:, cols], plane[:, cols])
 
+        round_w1(0, nc.scalar.copy)
         quantise_w1(0)
         for hh in range(2):
             nc.vector.tensor_copy(v_s[hh][:], tab_s[:].indirect(halves[hh]))
@@ -166,8 +178,8 @@ def tile_list_plate_proofing_kernel(
             nc.vector.tensor_copy(v_w[q][:], tab_w[:].indirect(list1[:, q * columns : (q + 1) * columns]))
         nc.vector.tensor_copy(v_w[2][:], tab_w[:].indirect(halves[1]))
         load_w1(3)
-        first_neg = sb([P, QUARTER], F32, "first_neg")
-        nc.vector.tensor_scalar_mul(first_neg[:], wgs_raw[:, :QUARTER], -1.0)
+        wgs_neg = placed([P, S], F32, "wgs_neg", WGS_NEG_AT)
+        nc.gpsimd.tensor_scalar(wgs_neg[:], wgs_raw[:], -1.0, 0.0, MULT, ADD)
 
         refs = {}
         last = ROW_TILES - 1
@@ -177,12 +189,12 @@ def tile_list_plate_proofing_kernel(
             nc.sync.dma_start(refs[i][:], ref[i * P : (i + 1) * P, :])
 
         mags = [sb([P, S], F32, f"mag{k}") for k in range(RING)]
-        first_mags = [sb([P, QUARTER], F32, f"first_mag{q}") for q in range(3)]
-        first_mags.append(sb([P, QUARTER], F32, "first_mag3", tag="page2"))
+        first_mags = [placed([P, QUARTER], F32, f"first_mag{q}", at) for q, at in enumerate(FIRST_MAG_AT)]
         squares = [sb([P, BANK], F32, f"square{q}") for q in range(4)]
 
         early_squares = {key: placed([P, BANK], F32, f"early_square{key[0]}_{key[1]}", at) for key, at in SQUARE_AT.items()}
-        early_squares[last, 0] = sb([P, BANK], F32, "last_square")
+        early_squares[5, 0] = sb([P, BANK], F32, "early_square5")
+        early_squares[6, 0] = sb([P, BANK], F32, "early_square6")
 
         def square_tile(i, q):
             return early_squares.get((i, q), squares[q])
@@ -246,7 +258,7 @@ def tile_list_plate_proofing_kernel(
         def place_first(q):
             nc.vector.tensor_tensor(
                 pages[0][:].indirect(list2[:, q * columns : (q + 1) * columns]), first_mags[q][:],
-                wgs_neg[:, q * QUARTER : (q + 1) * QUARTER] if q else first_neg[:], MULT,
+                wgs_neg[:, q * QUARTER : (q + 1) * QUARTER], MULT,
             )
 
         z_t = {}
@@ -305,14 +317,14 @@ def tile_list_plate_proofing_kernel(
                 w3_raw[b, late] = sb([P, PACK, P], F32, f"w3_late{b}", tag=f"v_w{2 * b}")
                 nc.sync.dma_start(w3_raw[b, late][:], rows[:, :, 2 * P :])
             else:
-                w3_raw[b, late] = placed([P, PACK, 2 * P], F32, f"w3_raw{b}", W3_RAW_AT + b * 4 * KIB)
+                w3_raw[b, late] = placed([P, PACK, 2 * P], F32, f"w3_raw{b}", W3_RAW_AT[b])
                 nc.sync.dma_start(w3_raw[b, late][:], rows[:, :, : 2 * P])
 
         w3_bf = {}
 
         def round_w3(n, tag, copy):
             late = n == SCORE_TILES - 1
-            w3_bf[n] = sb([P, 2 * P, PACK], BF16, f"w3_bf{n}", tag=tag)
+            w3_bf[n] = sb([P, 2 * P, PACK], BF16, f"w3_bf{n}", tag=tag)[:]
             for b in range(2):
                 raw = w3_raw[b, late][:] if late else w3_raw[b, late][:, :, n * P : (n + 1) * P]
                 round_and_interleave(copy, w3_bf[n][:, b * P : (b + 1) * P, :], raw)
@@ -321,91 +333,81 @@ def tile_list_plate_proofing_kernel(
             grouped = w3_bf[n]
             codes = sb([P, 2 * P], U32, f"w3_c{n}")
             plane = placed([P, 2 * P], U8, f"w3_s{n}", WGS_NEG_AT + GROUPS * BANK + n * 2 * P)
-            nc.vector.quantize_mx(codes[:].bitcast(FP8X4), plane[:], grouped[:].rearrange("p c j -> p (c j)"))
+            nc.vector.quantize_mx(codes[:].bitcast(FP8X4), plane[:], grouped.rearrange("p c j -> p (c j)"))
             w3_q[n] = (codes, plane)
+
+        def pass_over(count):
+            bank_uses.extend([None] * count)
+
+        def both_magnitudes(i):
+            half_magnitude(i, 0)
+            if i in ROUNDED_IN:
+                round_w1(ROUNDED_IN[i], nc.scalar.copy)
+                quantise_w1(ROUNDED_IN[i])
+            half_magnitude(i, 1)
 
         load_ref(0)
         load_w1(4)
         first_magnitude()
         respond(0, 1)
         nc.scalar.activation(first_mags[0][:], first_sum[:], ACT.Sqrt)
-        wgs_neg = placed([P, S], F32, "wgs_neg", WGS_NEG_AT)
-        nc.vector.tensor_scalar_mul(wgs_neg[:], wgs_raw[:], -1.0)
+        round_w1(1, nc.vector.tensor_copy)
         place_first(0)
         quantise_w1(1)
+        round_w1(2, nc.vector.tensor_copy)
         magnitude(0, first_mags[1][:], (1,))
         place_first(1)
+        quantise_w1(2)
         respond(0, 2)
         respond(0, 3)
+        pass_over(2)
         magnitude(0, first_mags[2][:], (2,))
         place_first(2)
-        quantise_w1(2)
         magnitude(0, first_mags[3][:], (3,))
         place_first(3)
         load_ref(1)
-
-        def pass_over(count):
-            bank_uses.extend([None] * count)
-
-        def magnitudes(i, back=0):
-            for q in range(4):
-                if back and q % 2 == 0:
-                    pass_over(len(banks) - back)
-                respond(i, q)
-            half_magnitude(i, 0)
-            for c, (tile, q) in ROUNDED_ON.items():
-                if tile == i:
-                    quantise_w1(c)
-            half_magnitude(i, 1)
-
-        magnitudes(1)
-        pages.append(zeroed(nc.gpsimd, "page2"))
+        pass_over(len(banks) - 2)
+        for q in range(4):
+            respond(1, q)
+        both_magnitudes(1)
+        for q in range(4):
+            respond(2, q)
+        both_magnitudes(2)
+        pages.append(placed([P, T2], F32, "page2", PAGE2_AT))
+        nc.gpsimd.memset(pages[2][:], 0.0)
         load_w3(0, False)
         load_w3(1, False)
-
-        def deviations(i):
+        for i in range(1, ROW_TILES):
+            place(i)
+            if i + 1 < ROW_TILES:
+                load_ref(i + 1)
+            ahead = i + AHEAD
+            if ahead < ROW_TILES:
+                for q in range(4):
+                    respond(ahead, q)
             for g in range(GROUPS):
-                deviation(i, g)
-
-        place(1)
-        magnitudes(2, back=2)
-        load_ref(2)
-        pass_over(len(banks) - 4)
-        deviations(0)
-        load_ref(3)
-        magnitudes(3)
-        place(2)
-        magnitudes(4)
-        place(3)
-        deviations(1)
-        load_ref(4)
-        deviations(2)
-        load_ref(5)
-        place(4)
-        magnitudes(5)
-        place(5)
-        magnitudes(6)
-        deviations(3)
-        load_ref(6)
-        place(6)
-        magnitudes(last)
-        load_w3(0, True)
-        load_w3(1, True)
-        deviations(4)
-        load_ref(last)
-        place(last)
-        for g in range(GROUPS):
-            turn_back(0, g, nc.scalar.copy, (next_bank(), next_bank()))
-        deviations(5)
-        round_w3(0, "last_square", nc.scalar.copy)
-        deviations(last - 1)
+                deviation(i - 1, g)
+            if ahead < ROW_TILES:
+                both_magnitudes(ahead)
+            if ahead in (5, 6):
+                round_w3(ahead - 5, f"early_square{ahead}", nc.scalar.copy)
+            if ahead == last:
+                load_w3(0, True)
+                load_w3(1, True)
+            if ahead == ROW_TILES:
+                for g in range(GROUPS // 2):
+                    turn_back(0, g, nc.scalar.copy, (next_bank(), next_bank()))
         opened = [next_bank() for g in range(GROUPS)]
         for g in range(GROUPS):
             add_transposed(opened[g], blocks_of(refs[last][:, g * BANK : (g + 1) * BANK]), closes=False)
+        for g in range(GROUPS // 2, GROUPS):
+            turn_back(0, g, nc.scalar.copy, (next_bank(), next_bank()))
+        pass_over(len(opened))
         out_pages = [zeroed(nc.gpsimd, f"out_page{hh}", tag=f"v_s{hh}") for hh in range(2)]
         for g in range(GROUPS):
             quantise_z(0, g)
-        quantise_w3(0)
+        for n in range(SCORE_TILES - 1):
+            quantise_w3(n)
 
         sens_t = sb([P, SCORE_TILES, M], F32, "sens_t", tag="w2_w")
         nc.sync.dma_start(sens_t[:], sens.rearrange("(n p) m -> p n m", p=P))
@@ -447,8 +449,6 @@ def tile_list_plate_proofing_kernel(
             score(0, g, on_vector=(g == GROUPS - 2))
         for first in (0, BANK // 2):
             score(0, GROUPS - 1, first, BANK // 2)
-        round_w3(1, f"z_bf{GROUPS - 1}", nc.vector.tensor_copy)
-        quantise_w3(1)
         round_w3(SCORE_TILES - 1, "w3_c0", nc.scalar.copy)
         quantise_w3(SCORE_TILES - 1)
         for n in range(1, SCORE_TILES):

@@ -42,10 +42,11 @@ W3_RAW_AT = (W1_RAW_AT[2], W1_RAW_AT[4])
 WGS_NEG_AT = 40 * KIB
 ROWS_AT = (TABLE_WORDS_AT, 32 * KIB, 48 * KIB)
 FIRST_SUM_AT = ROWS_AT[1] + 3 * KIB // 2
-SQUARE_AT = {(0, 0): 46 * KIB, (0, 2): ROWS_AT[1], (0, 3): ROWS_AT[1] + 2 * KIB, (2, 0): ROWS_AT[2], (3, 0): 56 * KIB}
+SQUARE_AT = {(0, 0): 46 * KIB, (0, 2): ROWS_AT[1], (0, 3): ROWS_AT[1] + 2 * KIB, (2, 0): ROWS_AT[2], (3, 0): 58 * KIB}
 PAGE2_AT = 60 * KIB
-FIRST_MAG_AT = (58 * KIB, SQUARE_AT[0, 0] + KIB, 68 * KIB, PAGE2_AT + KIB)
-W1_BF_AT = (None, SQUARE_AT[0, 0], FIRST_MAG_AT[0] + KIB // 2, SQUARE_AT[2, 0], SQUARE_AT[3, 0])
+FIRST_PARTS = ((0,), (1,), (2, 3))
+FIRST_MAG_AT = (56 * KIB, 57 * KIB, PAGE2_AT)
+W1_BF_AT = (None, None, SQUARE_AT[0, 0], SQUARE_AT[2, 0], SQUARE_AT[3, 0])
 W1_CODES_AT = (None, FIRST_MAG_AT[0], FIRST_MAG_AT[1], None, None)
 ROUNDED_IN = {2: 3, 3: 4}
 
@@ -124,9 +125,9 @@ def tile_list_plate_proofing_kernel(
         wgs_raw = placed([P, S], F32, "wgs_raw", WGS_AT)
         nc.sync.dma_start(wgs_raw[:], wgs)
         load_w1(1)
+        load_w1(2)
         list2 = load_list(offs2, "list2")
         nc.sync.dma_start(w2_w[:, 2 * P :].bitcast(I32), w2_words[0][:, 2 * P :].bitcast(I32))
-        load_w1(2)
         list3 = load_list(offs3, "list3")
         list4 = load_list(offs4, "list4")
 
@@ -150,7 +151,10 @@ def tile_list_plate_proofing_kernel(
         def round_w1(c, copy):
             first, end = W1_RUNS[c]
             shape = [P, (end - first) * P, PACK]
-            w1_bf[c] = placed(shape, BF16, f"w1_bf{c}", W1_BF_AT[c]) if c else sb(shape, BF16, f"w1_bf{c}")
+            if W1_BF_AT[c] is None:
+                w1_bf[c] = sb(shape, BF16, f"w1_bf{c}")
+            else:
+                w1_bf[c] = placed(shape, BF16, f"w1_bf{c}", W1_BF_AT[c])
             round_and_interleave(copy, w1_bf[c][:], w1_raw[c][:])
 
         def quantise_w1(c):
@@ -189,7 +193,9 @@ def tile_list_plate_proofing_kernel(
             nc.sync.dma_start(refs[i][:], ref[i * P : (i + 1) * P, :])
 
         mags = [sb([P, S], F32, f"mag{k}") for k in range(RING)]
-        first_mags = [placed([P, QUARTER], F32, f"first_mag{q}", at) for q, at in enumerate(FIRST_MAG_AT)]
+        first_mags = [
+            placed([P, len(part) * QUARTER], F32, f"first_mag{k}", FIRST_MAG_AT[k]) for k, part in enumerate(FIRST_PARTS)
+        ]
         squares = [sb([P, BANK], F32, f"square{q}") for q in range(4)]
 
         early_squares = {key: placed([P, BANK], F32, f"early_square{key[0]}_{key[1]}", at) for key, at in SQUARE_AT.items()}
@@ -255,10 +261,11 @@ def tile_list_plate_proofing_kernel(
         def place(i):
             nc.vector.tensor_tensor(pages[i % RING][:].indirect(list2[:]), mags[i % RING][:], wgs_neg[:], MULT)
 
-        def place_first(q):
+        def place_first(k):
+            first, end = FIRST_PARTS[k][0], FIRST_PARTS[k][-1] + 1
             nc.vector.tensor_tensor(
-                pages[0][:].indirect(list2[:, q * columns : (q + 1) * columns]), first_mags[q][:],
-                wgs_neg[:, q * QUARTER : (q + 1) * QUARTER], MULT,
+                pages[0][:].indirect(list2[:, first * columns : end * columns]), first_mags[k][:],
+                wgs_neg[:, first * QUARTER : end * QUARTER], MULT,
             )
 
         z_t = {}
@@ -350,26 +357,26 @@ def tile_list_plate_proofing_kernel(
         load_w1(4)
         first_magnitude()
         respond(0, 1)
+        round_w1(1, nc.scalar.copy)
         nc.scalar.activation(first_mags[0][:], first_sum[:], ACT.Sqrt)
-        round_w1(1, nc.vector.tensor_copy)
+        round_w1(2, nc.vector.tensor_copy)
         place_first(0)
         quantise_w1(1)
-        round_w1(2, nc.vector.tensor_copy)
         magnitude(0, first_mags[1][:], (1,))
         place_first(1)
         quantise_w1(2)
         respond(0, 2)
         respond(0, 3)
-        pass_over(2)
-        magnitude(0, first_mags[2][:], (2,))
+        magnitude(0, first_mags[2][:], FIRST_PARTS[2])
         place_first(2)
-        magnitude(0, first_mags[3][:], (3,))
-        place_first(3)
         load_ref(1)
-        pass_over(len(banks) - 2)
         for q in range(4):
+            if q % 3 == 0:
+                pass_over(len(banks) - 3)
             respond(1, q)
+        pass_over(2)
         both_magnitudes(1)
+        pass_over(len(banks) - 4)
         for q in range(4):
             respond(2, q)
         both_magnitudes(2)
@@ -383,8 +390,12 @@ def tile_list_plate_proofing_kernel(
                 load_ref(i + 1)
             ahead = i + AHEAD
             if ahead < ROW_TILES:
+                if i <= 2:
+                    pass_over(2)
                 for q in range(4):
                     respond(ahead, q)
+                if i == 1:
+                    pass_over(len(banks) - 4)
             for g in range(GROUPS):
                 deviation(i - 1, g)
             if ahead < ROW_TILES:

@@ -42,7 +42,8 @@ W3_RAW_AT = (W1_RAW_AT[2], W1_RAW_AT[4])
 WGS_NEG_AT = 40 * KIB
 ROWS_AT = (TABLE_WORDS_AT, 32 * KIB, 48 * KIB)
 FIRST_SUM_AT = ROWS_AT[1] + 3 * KIB // 2
-SQUARE_AT = {(0, 0): 46 * KIB, (0, 2): ROWS_AT[1], (0, 3): ROWS_AT[1] + 2 * KIB, (2, 0): ROWS_AT[2], (3, 0): 58 * KIB}
+PAGE1_AT = 68 * KIB
+SQUARE_AT = {(0, 0): PAGE1_AT, (0, 2): ROWS_AT[1], (0, 3): ROWS_AT[1] + 2 * KIB, (2, 0): ROWS_AT[2], (3, 0): 58 * KIB}
 PAGE2_AT = 60 * KIB
 FIRST_PARTS = ((0,), (1,), (2, 3))
 FIRST_MAG_AT = (56 * KIB, 57 * KIB, PAGE2_AT)
@@ -135,7 +136,7 @@ def tile_list_plate_proofing_kernel(
         make_identity(nc, ident[:])
         for q in range(4):
             nc.vector.tensor_copy(w2_s[32 * q : 32 * q + 4, :].bitcast(I32), w2_rows[:, q, :].bitcast(I32))
-        pages = [zeroed(nc.vector, "page0"), zeroed(nc.vector, "page1")]
+        pages = [zeroed(nc.vector, "page0")]
 
         halves = [list1[:, hh * HALF_LIST : (hh + 1) * HALF_LIST] for hh in range(2)]
         v_s = [sb([P, BANK], U8, f"v_s{hh}") for hh in range(2)]
@@ -365,6 +366,8 @@ def tile_list_plate_proofing_kernel(
         magnitude(0, first_mags[1][:], (1,))
         place_first(1)
         quantise_w1(2)
+        pages.append(placed([P, T2], F32, "page1", PAGE1_AT))
+        nc.gpsimd.memset(pages[1][:], 0.0)
         respond(0, 2)
         respond(0, 3)
         magnitude(0, first_mags[2][:], FIRST_PARTS[2])
@@ -443,11 +446,11 @@ def tile_list_plate_proofing_kernel(
             else:
                 nc.scalar.activation(target, acc[:, :width], ACT.Copy, scale=-1.0)
 
-        def score(n, g, first=0, width=BANK, on_vector=False):
+        def score(n, g):
             acc = next_bank()
             for b in range(2):
-                multiply(acc, n, g, b, first, width)
-            empty(acc, n, g, first, width, on_vector)
+                multiply(acc, n, g, b)
+            empty(acc, n, g)
 
         for g in range(GROUPS):
             deviation(last, g, opened[g])
@@ -456,10 +459,13 @@ def tile_list_plate_proofing_kernel(
             if g:
                 quantise_z(1, g - 1)
         quantise_z(1, GROUPS - 1, pieces=2)
-        for g in range(GROUPS - 1):
-            score(0, g, on_vector=(g == GROUPS - 2))
-        for first in (0, BANK // 2):
-            score(0, GROUPS - 1, first, BANK // 2)
+        parts = [(next_bank(), g, 0, BANK) for g in range(GROUPS - 1)]
+        parts.extend((next_bank(), GROUPS - 1, first, BANK // 2) for first in (0, BANK // 2))
+        for acc, g, first, width in parts:
+            multiply(acc, 0, g, 0, first, width)
+        for acc, g, first, width in parts:
+            multiply(acc, 0, g, 1, first, width)
+            empty(acc, 0, g, first, width, on_vector=(g == GROUPS - 2))
         round_w3(SCORE_TILES - 1, "w3_c0", nc.scalar.copy)
         quantise_w3(SCORE_TILES - 1)
         for n in range(1, SCORE_TILES):

@@ -30,25 +30,27 @@ GROUPS = T2 // BANK
 SCORE_TILES = N // P
 QUARTER = 2 * P
 W1_RUNS = ((0, 1), (1, 2), (2, 4), (4, 6), (6, ROW_TILES))
+EARLY = 2 * P
 RING = 3
 AHEAD = 2
 
 KIB = 1024
 TABLE_WORDS_AT = 0
 TABLE_SCALES_AT = 24 * KIB
-WGS_AT = 28 * KIB
-W1_RAW_AT = (44 * KIB, 16 * KIB, 18 * KIB, 8 * KIB, 12 * KIB)
+WGS_AT = 44 * KIB
+W1_RAW_AT = (22 * KIB, 16 * KIB, 18 * KIB, 8 * KIB, 12 * KIB)
 W3_RAW_AT = (W1_RAW_AT[2], W1_RAW_AT[4])
 WGS_NEG_AT = 40 * KIB
 ROWS_AT = (TABLE_WORDS_AT, 32 * KIB, 48 * KIB)
-FIRST_SUM_AT = ROWS_AT[1] + 3 * KIB // 2
+FIRST_SUM_ROOM = 3 * QUARTER
+FIRST_SUM_AT = ROWS_AT[1] - 5 * KIB // 2
 PAGE1_AT = 68 * KIB
-SQUARE_AT = {(0, 0): PAGE1_AT, (0, 2): ROWS_AT[1], (0, 3): ROWS_AT[1] + 2 * KIB, (2, 0): ROWS_AT[2], (3, 0): 58 * KIB}
+SQUARE_AT = {(0, 2): FIRST_SUM_AT - 2 * KIB + 64, (0, 3): ROWS_AT[1], (2, 0): ROWS_AT[2], (3, 0): 58 * KIB}
 PAGE2_AT = 60 * KIB
 FIRST_PARTS = ((0,), (1,), (2, 3))
 FIRST_MAG_AT = (56 * KIB, 57 * KIB, PAGE2_AT)
-W1_BF_AT = (None, None, SQUARE_AT[0, 0], SQUARE_AT[2, 0], SQUARE_AT[3, 0])
-W1_CODES_AT = (None, FIRST_MAG_AT[0], FIRST_MAG_AT[1], None, None)
+W1_BF_AT = (None, None, PAGE1_AT, SQUARE_AT[2, 0], SQUARE_AT[3, 0])
+W1_CODES_AT = (None, FIRST_SUM_AT + 64, FIRST_MAG_AT[0], None, None)
 ROUNDED_IN = {2: 3, 3: 4}
 
 
@@ -105,16 +107,16 @@ def tile_list_plate_proofing_kernel(
             nc.sync.dma_start(w1_raw[c][:], w1[:, first * P : end * P].rearrange("(p j) c -> p j c", j=PACK))
 
         tab_s = placed([P, T], U8, "tab_s", TABLE_SCALES_AT)
-        w2_s = sb([P, H], U8, "w2_s")
+        w2_s = [sb([P, EARLY], U8, "w2_s_early")]
         nc.gpsimd.memset(tab_s[:].bitcast(I32), 0)
-        nc.vector.memset(w2_s[:].bitcast(I32), 0)
+        nc.vector.memset(w2_s[0][:].bitcast(I32), 0)
         warm = sb([P, 2], F32, "warm")
         nc.vector.memset(warm[:, 0:1], 1.0)
         nc.scalar.activation(warm[:, 1:2], warm[:, 0:1], ACT.Sqrt)
-        w2_rows = sb([4, 4, H], U8, "w2_rows")
+        w2_rows = sb([4, 4, EARLY], U8, "w2_rows")
         nc.scalar.dma_start(
             w2_rows[:].rearrange("r q c -> r (q c)").bitcast(I32).rearrange("r (q c) -> r q c", q=4),
-            w2_scales[0].bitcast(I32).rearrange("(q r) c -> r q c", r=4),
+            w2_scales[0][:, :EARLY].bitcast(I32).rearrange("(q r) c -> r q c", r=4),
         )
         list1 = load_list(offs, "list1")
         load_w1(0)
@@ -125,9 +127,9 @@ def tile_list_plate_proofing_kernel(
         nc.sync.dma_start(w2_w[:, : 2 * P].bitcast(I32), w2_words[0][:, : 2 * P].bitcast(I32))
         wgs_raw = placed([P, S], F32, "wgs_raw", WGS_AT)
         nc.sync.dma_start(wgs_raw[:], wgs)
+        list2 = load_list(offs2, "list2")
         load_w1(1)
         load_w1(2)
-        list2 = load_list(offs2, "list2")
         nc.sync.dma_start(w2_w[:, 2 * P :].bitcast(I32), w2_words[0][:, 2 * P :].bitcast(I32))
         list3 = load_list(offs3, "list3")
         list4 = load_list(offs4, "list4")
@@ -135,7 +137,7 @@ def tile_list_plate_proofing_kernel(
         ident = sb([P, P], F32, "ident")
         make_identity(nc, ident[:])
         for q in range(4):
-            nc.vector.tensor_copy(w2_s[32 * q : 32 * q + 4, :].bitcast(I32), w2_rows[:, q, :].bitcast(I32))
+            nc.vector.tensor_copy(w2_s[0][32 * q : 32 * q + 4, :].bitcast(I32), w2_rows[:, q, :].bitcast(I32))
         pages = [zeroed(nc.vector, "page0")]
 
         halves = [list1[:, hh * HALF_LIST : (hh + 1) * HALF_LIST] for hh in range(2)]
@@ -185,6 +187,13 @@ def tile_list_plate_proofing_kernel(
         load_w1(3)
         wgs_neg = placed([P, S], F32, "wgs_neg", WGS_NEG_AT)
         nc.gpsimd.tensor_scalar(wgs_neg[:], wgs_raw[:], -1.0, 0.0, MULT, ADD)
+        w2_s.append(placed([P, H - EARLY], U8, "w2_s_late", WGS_AT))
+        nc.gpsimd.memset(w2_s[1][:].bitcast(I32), 0)
+        load_scale_rows(nc.gpsimd, w2_s[1], w2_scales[0][:, EARLY:])
+
+        def w2_plane(i):
+            first = P * i
+            return w2_s[0][:, first : first + P] if first < EARLY else w2_s[1][:, first - EARLY : first - EARLY + P]
 
         refs = {}
         last = ROW_TILES - 1
@@ -202,6 +211,7 @@ def tile_list_plate_proofing_kernel(
         early_squares = {key: placed([P, BANK], F32, f"early_square{key[0]}_{key[1]}", at) for key, at in SQUARE_AT.items()}
         early_squares[5, 0] = sb([P, BANK], F32, "early_square5")
         early_squares[6, 0] = sb([P, BANK], F32, "early_square6")
+        early_squares[last, 3] = sb([P, BANK], F32, "last_square")
 
         def square_tile(i, q):
             return early_squares.get((i, q), squares[q])
@@ -210,7 +220,7 @@ def tile_list_plate_proofing_kernel(
             acc = next_bank()
             hh = q // 2
             operands = (
-                (w2_w[:, 2 * P * i : 2 * P * (i + 1)].bitcast(FP4X4), w2_s[:, P * i : P * (i + 1)]),
+                (w2_w[:, 2 * P * i : 2 * P * (i + 1)].bitcast(FP4X4), w2_plane(i)),
                 (w1_q[i][0].bitcast(FP8X4), w1_q[i][1]),
             )
             for which, (rhs, rhs_scale) in enumerate(operands):
@@ -246,18 +256,18 @@ def tile_list_plate_proofing_kernel(
         def half_magnitude(i, hh):
             magnitude(i, mags[i % RING][:, hh * BANK : (hh + 1) * BANK], (2 * hh, 2 * hh + 1))
 
-        first_sum = placed([P, QUARTER], F32, "first_sum", FIRST_SUM_AT)
+        first_sum = placed([P, FIRST_SUM_ROOM], F32, "first_sum", FIRST_SUM_AT)[:, :QUARTER]
 
         def first_magnitude():
             acc, square = next_bank(), square_tile(0, 0)
-            weights = ((w1_q[0][0].bitcast(FP8X4), w1_q[0][1]), (w2_w[:, : 2 * P].bitcast(FP4X4), w2_s[:, :P]))
+            weights = ((w1_q[0][0].bitcast(FP8X4), w1_q[0][1]), (w2_w[:, : 2 * P].bitcast(FP4X4), w2_plane(0)))
             for which, (lhsT, lhsT_scale) in enumerate(weights):
                 nc.tensor.matmul_mx(
                     out=acc[:, which * QUARTER : (which + 1) * QUARTER], lhsT=lhsT, lhsT_scale=lhsT_scale,
                     rhs=v_w[0][:].bitcast(FP8X4), rhs_scale=v_s[0][:, :QUARTER], start=True, stop=True,
                 )
             nc.scalar.activation(square[:], acc[:], ACT.Square)
-            nc.vector.tensor_tensor(first_sum[:], square[:, :QUARTER], square[:, QUARTER:], ADD)
+            nc.vector.tensor_tensor(first_sum, square[:, :QUARTER], square[:, QUARTER:], ADD)
 
         def place(i):
             nc.vector.tensor_tensor(pages[i % RING][:].indirect(list2[:]), mags[i % RING][:], wgs_neg[:], MULT)
@@ -306,6 +316,8 @@ def tile_list_plate_proofing_kernel(
             codes = sb([P, BANK], U32, f"z_c{b}_{g}", tag=f"z_t{b}_{g}")
             if b:
                 plane = sb([P, BANK], U8, f"z_s{b}_{g}")
+            elif g == 0:
+                plane = sb([P, BANK], U8, f"z_s{b}_{g}", tag="last_square")
             else:
                 plane = placed([P, BANK], U8, f"z_s{b}_{g}", WGS_NEG_AT + g * BANK)
             width = BANK // pieces
@@ -359,17 +371,20 @@ def tile_list_plate_proofing_kernel(
         first_magnitude()
         respond(0, 1)
         round_w1(1, nc.scalar.copy)
-        nc.scalar.activation(first_mags[0][:], first_sum[:], ACT.Sqrt)
+        nc.scalar.activation(first_mags[0][:], first_sum, ACT.Sqrt)
         round_w1(2, nc.vector.tensor_copy)
         place_first(0)
         quantise_w1(1)
+        pass_over(1)
+        respond(0, 2)
+        respond(0, 3)
+        pass_over(len(banks) - 2)
         magnitude(0, first_mags[1][:], (1,))
+        pass_over(1)
         place_first(1)
         quantise_w1(2)
         pages.append(placed([P, T2], F32, "page1", PAGE1_AT))
         nc.gpsimd.memset(pages[1][:], 0.0)
-        respond(0, 2)
-        respond(0, 3)
         magnitude(0, first_mags[2][:], FIRST_PARTS[2])
         place_first(2)
         load_ref(1)

from contextlib import ExitStack

import concourse.mybir as mybir
from concourse.masks import make_identity

K, H, N, T, S, T2, M = 512, 1024, 384, 4096, 1024, 2048, 1024
FLOPS = 2 * K * H * S * 2 + 2 * H * N * T2

F32 = mybir.dt.float32
BF16 = mybir.dt.bfloat16
I32 = mybir.dt.int32
U32 = mybir.dt.uint32
U16 = mybir.dt.uint16
U8 = mybir.dt.uint8
FP8X4 = mybir.dt.float8_e4m3fn_x4
FP4X4 = mybir.dt.float4_e2m1fn_x4
ACT = mybir.ActivationFunctionType
MULT = mybir.AluOpType.mult
ADD = mybir.AluOpType.add

P = 128
BANK = 512
PACK = 4
PASS = P * PACK
BLOCKS = BANK // P
HALF_LIST = BANK // 16
ROW_TILES = H // P
TILES_PER_PASS = PASS // P
GROUPS = T2 // BANK
SCORE_TILES = N // P
QUARTER = 2 * P
W1_RUNS = ((0, 1), (1, 2), (2, 4), (4, 6), (6, ROW_TILES))
EARLY = 2 * P
RING = 3
AHEAD = 2

KIB = 1024
TABLE_WORDS_AT = 0
TABLE_SCALES_AT = 24 * KIB
WGS_AT = 44 * KIB
W1_RAW_AT = (22 * KIB, 16 * KIB, 18 * KIB, 8 * KIB, 12 * KIB)
W3_RAW_AT = (W1_RAW_AT[2], W1_RAW_AT[4])
WGS_NEG_AT = 40 * KIB
ROWS_AT = (TABLE_WORDS_AT, 32 * KIB, 48 * KIB)
FIRST_SUM_ROOM = 3 * QUARTER
FIRST_SUM_AT = ROWS_AT[1] - 5 * KIB // 2
PAGE1_AT = 68 * KIB
SQUARE_AT = {(0, 2): FIRST_SUM_AT - 2 * KIB + 64, (0, 3): ROWS_AT[1], (2, 0): ROWS_AT[2], (3, 0): 58 * KIB}
PAGE2_AT = 60 * KIB
FIRST_PARTS = ((0,), (1,), (2, 3))
FIRST_MAG_AT = (56 * KIB, 57 * KIB, PAGE2_AT)
W1_BF_AT = (None, None, PAGE1_AT, SQUARE_AT[2, 0], SQUARE_AT[3, 0])
W1_CODES_AT = (None, FIRST_SUM_AT + 64, FIRST_MAG_AT[0], None, None)
ROUNDED_IN = {2: 3, 3: 4}


def tile_list_plate_proofing_kernel(
    tc, tab_words, tab_scales, offs, w1, w2_words, w2_scales, offs2, wgs, ref, w3, offs3, sens, offs4, wgo, out
):
    nc = tc.nc
    with ExitStack() as ctx:
        held = ctx.enter_context(tc.tile_pool(name="held", bufs=1))
        shared = ctx.enter_context(tc.tile_pool(name="shared", bufs=1))
        psum = ctx.enter_context(tc.psum_pool(name="psum", bufs=1))

        def sb(shape, dtype, name, tag=None):
            return held.tile(shape, dtype, name=name, tag=tag or name, bufs=1, align_bytes=64)

        def placed(shape, dtype, name, offset, tag=None):
            return shared.tile(shape, dtype, name=name, tag=tag or name, offset=offset, align_bytes=64)

        def row_tile(k, name):
            return placed([P, T2], F32, name, ROWS_AT[k % RING], tag=f"rows{k % RING}")

        banks = [psum.tile([P, BANK], F32, name=f"bank{k}") for k in range(8)]
        bank_uses = []

        def next_bank():
            bank_uses.append(None)
            return banks[(len(bank_uses) - 1) % len(banks)]

        def load_list(src, name):
            tile = held.tile([P, S // 16], U16, name=name)
            nc.sync.dma_start(tile[:], src)
            return tile

        def load_scale_rows(queue, plane, rows):
            for r in range(4):
                queue.dma_start(plane[r:P:32, :].bitcast(I32), rows[r:16:4, :].bitcast(I32))

        def round_and_interleave(copy, grouped, raw):
            copy(
                out=grouped.rearrange("p (c i) j -> p c j i", i=4),
                in_=raw.rearrange("p j (c i) -> p c j i", i=4),
            )

        def zeroed(engine, name, tag=None):
            page = sb([P, T2], F32, name, tag=tag)
            engine.memset(page[:], 0.0)
            return page

        w1_raw = {}

        def load_w1(c):
            first, end = W1_RUNS[c]
            w1_raw[c] = placed([P, PACK, (end - first) * P], F32, f"w1_raw{c}", W1_RAW_AT[c])
            nc.sync.dma_start(w1_raw[c][:], w1[:, first * P : end * P].rearrange("(p j) c -> p j c", j=PACK))

        tab_s = placed([P, T], U8, "tab_s", TABLE_SCALES_AT)
        w2_s = [sb([P, EARLY], U8, "w2_s_early")]
        nc.gpsimd.memset(tab_s[:].bitcast(I32), 0)
        nc.vector.memset(w2_s[0][:].bitcast(I32), 0)
        warm = sb([P, 2], F32, "warm")
        nc.vector.memset(warm[:, 0:1], 1.0)
        nc.scalar.activation(warm[:, 1:2], warm[:, 0:1], ACT.Sqrt)
        w2_rows = sb([4, 4, EARLY], U8, "w2_rows")
        nc.scalar.dma_start(
            w2_rows[:].rearrange("r q c -> r (q c)").bitcast(I32).rearrange("r (q c) -> r q c", q=4),
            w2_scales[0][:, :EARLY].bitcast(I32).rearrange("(q r) c -> r q c", r=4),
        )
        list1 = load_list(offs, "list1")
        load_w1(0)
        load_scale_rows(nc.sync, tab_s, tab_scales[0])
        tab_w = placed([P, T], U32, "tab_w", TABLE_WORDS_AT)
        nc.sync.dma_start(tab_w[:].bitcast(I32), tab_words[0].rearrange("p t i -> p (t i)").bitcast(I32))
        w2_w = sb([P, 2 * H], U8, "w2_w")
        nc.sync.dma_start(w2_w[:, : 2 * P].bitcast(I32), w2_words[0][:, : 2 * P].bitcast(I32))
        wgs_raw = placed([P, S], F32, "wgs_raw", WGS_AT)
        nc.sync.dma_start(wgs_raw[:], wgs)
        list2 = load_list(offs2, "list2")
        load_w1(1)
        load_w1(2)
        nc.sync.dma_start(w2_w[:, 2 * P :].bitcast(I32), w2_words[0][:, 2 * P :].bitcast(I32))
        list3 = load_list(offs3, "list3")
        list4 = load_list(offs4, "list4")

        ident = sb([P, P], F32, "ident")
        make_identity(nc, ident[:])
        for q in range(4):
            nc.vector.tensor_copy(w2_s[0][32 * q : 32 * q + 4, :].bitcast(I32), w2_rows[:, q, :].bitcast(I32))
        pages = [zeroed(nc.vector, "page0")]

        halves = [list1[:, hh * HALF_LIST : (hh + 1) * HALF_LIST] for hh in range(2)]
        v_s = [sb([P, BANK], U8, f"v_s{hh}") for hh in range(2)]
        v_w = [sb([P, QUARTER], U32, "v_w0"), sb([P, QUARTER], U32, "v_w1"), sb([P, BANK], U32, "v_w2")]

        def picked_words(q):
            return v_w[q][:] if q < 2 else v_w[2][:, (q - 2) * QUARTER : (q - 1) * QUARTER]

        w1_q = {}

        w1_bf = {}

        def round_w1(c, copy):
            first, end = W1_RUNS[c]
            shape = [P, (end - first) * P, PACK]
            if W1_BF_AT[c] is None:
                w1_bf[c] = sb(shape, BF16, f"w1_bf{c}")
            else:
                w1_bf[c] = placed(shape, BF16, f"w1_bf{c}", W1_BF_AT[c])
            round_and_interleave(copy, w1_bf[c][:], w1_raw[c][:])

        def quantise_w1(c):
            first, end = W1_RUNS[c]
            width = (end - first) * P
            if W1_CODES_AT[c] is None:
                codes = sb([P, width], U32, f"w1_c{c}")
            else:
                codes = placed([P, width], U32, f"w1_c{c}", W1_CODES_AT[c])
            plane = sb([P, width], U8, f"w1_s{c}")
            flat = w1_bf[c][:].rearrange("p c j -> p (c j)")
            for c0 in range(0, width, BANK):
                c1 = min(c0 + BANK, width)
                nc.vector.quantize_mx(codes[:, c0:c1].bitcast(FP8X4), plane[:, c0:c1], flat[:, PACK * c0 : PACK * c1])
            for k in range(end - first):
                cols = slice(k * P, (k + 1) * P)
                w1_q[first + k] = (codes[:, cols], plane[:, cols])

        round_w1(0, nc.scalar.copy)
        quantise_w1(0)
        for hh in range(2):
            nc.vector.tensor_copy(v_s[hh][:], tab_s[:].indirect(halves[hh]))
        columns = QUARTER // 16
        for q in range(2):
            nc.vector.tensor_copy(v_w[q][:], tab_w[:].indirect(list1[:, q * columns : (q + 1) * columns]))
        nc.vector.tensor_copy(v_w[2][:], tab_w[:].indirect(halves[1]))
        load_w1(3)
        wgs_neg = placed([P, S], F32, "wgs_neg", WGS_NEG_AT)
        nc.gpsimd.tensor_scalar(wgs_neg[:], wgs_raw[:], -1.0, 0.0, MULT, ADD)
        w2_s.append(placed([P, H - EARLY], U8, "w2_s_late", WGS_AT))
        nc.gpsimd.memset(w2_s[1][:].bitcast(I32), 0)
        load_scale_rows(nc.gpsimd, w2_s[1], w2_scales[0][:, EARLY:])

        def w2_plane(i):
            first = P * i
            return w2_s[0][:, first : first + P] if first < EARLY else w2_s[1][:, first - EARLY : first - EARLY + P]

        refs = {}
        last = ROW_TILES - 1

        def load_ref(i):
            refs[i] = row_tile(i, f"ref{i}")
            nc.sync.dma_start(refs[i][:], ref[i * P : (i + 1) * P, :])

        mags = [sb([P, S], F32, f"mag{k}") for k in range(RING)]
        first_mags = [
            placed([P, len(part) * QUARTER], F32, f"first_mag{k}", FIRST_MAG_AT[k]) for k, part in enumerate(FIRST_PARTS)
        ]
        squares = [sb([P, BANK], F32, f"square{q}") for q in range(4)]

        early_squares = {key: placed([P, BANK], F32, f"early_square{key[0]}_{key[1]}", at) for key, at in SQUARE_AT.items()}
        early_squares[5, 0] = sb([P, BANK], F32, "early_square5")
        early_squares[6, 0] = sb([P, BANK], F32, "early_square6")
        early_squares[last, 3] = sb([P, BANK], F32, "last_square")

        def square_tile(i, q):
            return early_squares.get((i, q), squares[q])

        def respond(i, q):
            acc = next_bank()
            hh = q // 2
            operands = (
                (w2_w[:, 2 * P * i : 2 * P * (i + 1)].bitcast(FP4X4), w2_plane(i)),
                (w1_q[i][0].bitcast(FP8X4), w1_q[i][1]),
            )
            for which, (rhs, rhs_scale) in enumerate(operands):
                for jj in range(2):
                    entries = slice((2 * (q % 2) + jj) * P, (2 * (q % 2) + jj + 1) * P)
                    words = picked_words(q)[:, jj * P : (jj + 1) * P]
                    nc.tensor.matmul_mx(
                        out=acc[:, (2 * which + jj) * P : (2 * which + jj + 1) * P],
                        lhsT=words.bitcast(FP8X4), lhsT_scale=v_s[hh][:, entries],
                        rhs=rhs, rhs_scale=rhs_scale, start=True, stop=True,
                    )
            nc.scalar.activation(square_tile(i, q)[:], acc[:], ACT.Square)

        def add_transposed(acc, blocks, opens=True, closes=True):
            for k, (jj, block) in enumerate(blocks):
                nc.tensor.matmul(
                    acc[:, jj * P : (jj + 1) * P], block, ident[:], is_transpose=True,
                    start=(opens and k == 0), stop=(closes and k == len(blocks) - 1),
                )

        def blocks_of(tile, count=BLOCKS, first=0, to=0):
            return [(to + jj, tile[:, (first + jj) * P : (first + jj + 1) * P]) for jj in range(count)]

        def magnitude(i, target, quarters):
            total = next_bank()
            blocks = []
            for k, q in enumerate(quarters):
                square = square_tile(i, q)
                blocks.extend(blocks_of(square, 2, 0, 2 * k) + blocks_of(square, 2, 2, 2 * k))
            add_transposed(total, blocks)
            nc.scalar.activation(target, total[:, : len(quarters) * QUARTER], ACT.Sqrt)

        def half_magnitude(i, hh):
            magnitude(i, mags[i % RING][:, hh * BANK : (hh + 1) * BANK], (2 * hh, 2 * hh + 1))

        first_sum = placed([P, FIRST_SUM_ROOM], F32, "first_sum", FIRST_SUM_AT)[:, :QUARTER]

        def first_magnitude():
            acc, square = next_bank(), square_tile(0, 0)
            weights = ((w1_q[0][0].bitcast(FP8X4), w1_q[0][1]), (w2_w[:, : 2 * P].bitcast(FP4X4), w2_plane(0)))
            for which, (lhsT, lhsT_scale) in enumerate(weights):
                nc.tensor.matmul_mx(
                    out=acc[:, which * QUARTER : (which + 1) * QUARTER], lhsT=lhsT, lhsT_scale=lhsT_scale,
                    rhs=v_w[0][:].bitcast(FP8X4), rhs_scale=v_s[0][:, :QUARTER], start=True, stop=True,
                )
            nc.scalar.activation(square[:], acc[:], ACT.Square)
            nc.vector.tensor_tensor(first_sum, square[:, :QUARTER], square[:, QUARTER:], ADD)

        def place(i):
            nc.vector.tensor_tensor(pages[i % RING][:].indirect(list2[:]), mags[i % RING][:], wgs_neg[:], MULT)

        def place_first(k):
            first, end = FIRST_PARTS[k][0], FIRST_PARTS[k][-1] + 1
            nc.vector.tensor_tensor(
                pages[0][:].indirect(list2[:, first * columns : end * columns]), first_mags[k][:],
                wgs_neg[:, first * QUARTER : end * QUARTER], MULT,
            )

        z_t = {}

        def deviation(i, g, acc=None):
            b, quarter = divmod(i, TILES_PER_PASS)
            if quarter == 0:
                z_t[b, g] = sb([P, BLOCKS, 2, P, 2], BF16, f"z_t{b}_{g}")
            cols = slice(g * BANK, (g + 1) * BANK)
            if acc is None:
                acc = next_bank()
                add_transposed(acc, blocks_of(refs[i][:, cols]) + blocks_of(pages[i % RING][:, cols]))
            else:
                add_transposed(acc, blocks_of(pages[i % RING][:, cols]), opens=False)
            nc.scalar.copy(
                out=z_t[b, g][:, :, :, 32 * quarter : 32 * quarter + 32, :],
                in_=acc[:].rearrange("s (tb p u e) -> s tb u p e", tb=BLOCKS, u=2, e=2),
            )

        z_q = {}
        z_bf = [sb([P, BANK * PACK], BF16, f"z_bf{g}") for g in range(GROUPS)]

        def turn_back(b, g, second_copy, pair):
            words = z_t[b, g][:].rearrange("s tb u p e -> s (tb u p e)").bitcast(F32)
            grouped_words = z_bf[g][:].bitcast(F32)
            for half, acc in enumerate(pair):
                for k in range(BLOCKS):
                    src = words[:, (BLOCKS * half + k) * P : (BLOCKS * half + k + 1) * P]
                    nc.tensor.transpose(acc[:, k * P : (k + 1) * P], src, ident[:])
                copy = second_copy if half else nc.scalar.copy
                copy(
                    out=grouped_words[:, half * BANK : (half + 1) * BANK].rearrange("p (tb s u) -> p tb s u", tb=2, u=2),
                    in_=acc[:].rearrange("p (tb u s) -> p tb s u", tb=2, u=2),
                )

        def quantise_z(b, g, pieces=1):
            codes = sb([P, BANK], U32, f"z_c{b}_{g}", tag=f"z_t{b}_{g}")
            if b:
                plane = sb([P, BANK], U8, f"z_s{b}_{g}")
            elif g == 0:
                plane = sb([P, BANK], U8, f"z_s{b}_{g}", tag="last_square")
            else:
                plane = placed([P, BANK], U8, f"z_s{b}_{g}", WGS_NEG_AT + g * BANK)
            width = BANK // pieces
            for c0 in range(0, BANK, width):
                cols = slice(c0, c0 + width)
                nc.vector.quantize_mx(
                    codes[:, cols].bitcast(FP8X4), plane[:, cols], z_bf[g][:, PACK * c0 : PACK * (c0 + width)]
                )
            z_q[b, g] = (codes, plane)

        w3_raw = {}
        w3_q = {}

        def load_w3(b, late):
            rows = w3[b * PASS : (b + 1) * PASS, :].rearrange("(p j) n -> p j n", j=PACK)
            if late:
                w3_raw[b, late] = sb([P, PACK, P], F32, f"w3_late{b}", tag=f"v_w{2 * b}")
                nc.sync.dma_start(w3_raw[b, late][:], rows[:, :, 2 * P :])
            else:
                w3_raw[b, late] = placed([P, PACK, 2 * P], F32, f"w3_raw{b}", W3_RAW_AT[b])
                nc.sync.dma_start(w3_raw[b, late][:], rows[:, :, : 2 * P])

        w3_bf = {}

        def round_w3(n, tag, copy):
            late = n == SCORE_TILES - 1
            w3_bf[n] = sb([P, 2 * P, PACK], BF16, f"w3_bf{n}", tag=tag)[:]
            for b in range(2):
                raw = w3_raw[b, late][:] if late else w3_raw[b, late][:, :, n * P : (n + 1) * P]
                round_and_interleave(copy, w3_bf[n][:, b * P : (b + 1) * P, :], raw)

        def quantise_w3(n):
            grouped = w3_bf[n]
            codes = sb([P, 2 * P], U32, f"w3_c{n}")
            plane = placed([P, 2 * P], U8, f"w3_s{n}", WGS_NEG_AT + GROUPS * BANK + n * 2 * P)
            nc.vector.quantize_mx(codes[:].bitcast(FP8X4), plane[:], grouped.rearrange("p c j -> p (c j)"))
            w3_q[n] = (codes, plane)

        def pass_over(count):
            bank_uses.extend([None] * count)

        def both_magnitudes(i):
            half_magnitude(i, 0)
            if i in ROUNDED_IN:
                round_w1(ROUNDED_IN[i], nc.scalar.copy)
                quantise_w1(ROUNDED_IN[i])
            half_magnitude(i, 1)

        load_ref(0)
        load_w1(4)
        first_magnitude()
        respond(0, 1)
        round_w1(1, nc.scalar.copy)
        nc.scalar.activation(first_mags[0][:], first_sum, ACT.Sqrt)
        round_w1(2, nc.vector.tensor_copy)
        place_first(0)
        quantise_w1(1)
        pass_over(1)
        respond(0, 2)
        respond(0, 3)
        pass_over(len(banks) - 2)
        magnitude(0, first_mags[1][:], (1,))
        pass_over(1)
        place_first(1)
        quantise_w1(2)
        pages.append(placed([P, T2], F32, "page1", PAGE1_AT))
        nc.gpsimd.memset(pages[1][:], 0.0)
        magnitude(0, first_mags[2][:], FIRST_PARTS[2])
        place_first(2)
        load_ref(1)
        for q in range(4):
            if q % 3 == 0:
                pass_over(len(banks) - 3)
            respond(1, q)
        pass_over(2)
        both_magnitudes(1)
        pass_over(len(banks) - 4)
        for q in range(4):
            respond(2, q)
        both_magnitudes(2)
        pages.append(placed([P, T2], F32, "page2", PAGE2_AT))
        nc.gpsimd.memset(pages[2][:], 0.0)
        load_w3(0, False)
        load_w3(1, False)
        for i in range(1, ROW_TILES):
            place(i)
            if i + 1 < ROW_TILES:
                load_ref(i + 1)
            ahead = i + AHEAD
            if ahead < ROW_TILES:
                if i <= 2:
                    pass_over(2)
                for q in range(4):
                    respond(ahead, q)
                if i == 1:
                    pass_over(len(banks) - 4)
            for g in range(GROUPS):
                deviation(i - 1, g)
            if ahead < ROW_TILES:
                both_magnitudes(ahead)
            if ahead in (5, 6):
                round_w3(ahead - 5, f"early_square{ahead}", nc.scalar.copy)
            if ahead == last:
                load_w3(0, True)
                load_w3(1, True)
            if ahead == ROW_TILES:
                for g in range(GROUPS // 2):
                    turn_back(0, g, nc.scalar.copy, (next_bank(), next_bank()))
        opened = [next_bank() for g in range(GROUPS)]
        for g in range(GROUPS):
            add_transposed(opened[g], blocks_of(refs[last][:, g * BANK : (g + 1) * BANK]), closes=False)
        for g in range(GROUPS // 2, GROUPS):
            turn_back(0, g, nc.scalar.copy, (next_bank(), next_bank()))
        pass_over(len(opened))
        out_pages = [zeroed(nc.gpsimd, f"out_page{hh}", tag=f"v_s{hh}") for hh in range(2)]
        for g in range(GROUPS):
            quantise_z(0, g)
        for n in range(SCORE_TILES - 1):
            quantise_w3(n)

        sens_t = sb([P, SCORE_TILES, M], F32, "sens_t", tag="w2_w")
        nc.sync.dma_start(sens_t[:], sens.rearrange("(n p) m -> p n m", p=P))
        wgo_t = sb([P, M], F32, "wgo_t", tag=f"w1_c{len(W1_RUNS) - 1}")
        nc.sync.dma_start(wgo_t[:], wgo)

        scores = [row_tile(ROW_TILES + n, f"score{n}") for n in range(SCORE_TILES)]

        def multiply(acc, n, g, b, first=0, width=BANK):
            codes, plane = w3_q[n]
            cols = slice(b * P, (b + 1) * P)
            nc.tensor.matmul_mx(
                out=acc[:, :width], lhsT=codes[:, cols].bitcast(FP8X4), lhsT_scale=plane[:, cols],
                rhs=z_q[b, g][0][:, first : first + width].bitcast(FP8X4),
                rhs_scale=z_q[b, g][1][:, first : first + width], start=(b == 0), stop=(b == 1),
            )

        def empty(acc, n, g, first=0, width=BANK, on_vector=False):
            target = scores[n][:, g * BANK + first : g * BANK + first + width]
            if on_vector:
                nc.vector.tensor_scalar_mul(target, acc[:, :width], -1.0)
            else:
                nc.scalar.activation(target, acc[:, :width], ACT.Copy, scale=-1.0)

        def score(n, g):
            acc = next_bank()
            for b in range(2):
                multiply(acc, n, g, b)
            empty(acc, n, g)

        for g in range(GROUPS):
            deviation(last, g, opened[g])
        for g in range(GROUPS):
            turn_back(1, g, nc.vector.tensor_copy if g < 2 else nc.scalar.copy, (next_bank(), next_bank()))
            if g:
                quantise_z(1, g - 1)
        quantise_z(1, GROUPS - 1, pieces=2)
        parts = [(next_bank(), g, 0, BANK) for g in range(GROUPS - 1)]
        parts.extend((next_bank(), GROUPS - 1, first, BANK // 2) for first in (0, BANK // 2))
        for acc, g, first, width in parts:
            multiply(acc, 0, g, 0, first, width)
        for acc, g, first, width in parts:
            multiply(acc, 0, g, 1, first, width)
            empty(acc, 0, g, first, width, on_vector=(g == GROUPS - 2))
        round_w3(SCORE_TILES - 1, "w3_c0", nc.scalar.copy)
        quantise_w3(SCORE_TILES - 1)
        for n in range(1, SCORE_TILES):
            for g in range(GROUPS):
                score(n, g)

        def pick(n, picked):
            nc.vector.tensor_tensor(picked[:], scores[n][:].indirect(list3[:]), sens_t[:, n, :], MULT)

        def put(n, picked, page):
            nc.vector.tensor_tensor(page[:].indirect(list4[:]), picked[:], wgo_t[:], MULT)
            nc.sync.dma_start(out[n * P : (n + 1) * P, :], page[:])

        pick(0, mags[0])
        put(0, mags[0], out_pages[0])
        pick(2, mags[2])
        picked = placed([P, M], F32, "picked1", ROWS_AT[(ROW_TILES + 2) % RING])
        pick(1, picked)
        put(2, mags[2], out_pages[1])
        put(1, picked, out_pages[0])
